import numpy as np
import ml_dtypes


def mxq(x, axis, fmt="e4m3"):
    dtype, down = {"e4m3": (ml_dtypes.float8_e4m3fn, 7), "e5m2": (ml_dtypes.float8_e5m2, 14)}[fmt]
    v = np.moveaxis(np.asarray(x, np.float32).astype(ml_dtypes.bfloat16).astype(np.float64), axis, -1)
    blocks = v.reshape(v.shape[:-1] + (-1, 32))
    amax = np.abs(blocks).max(-1, keepdims=True)
    byte = np.maximum(np.where(amax > 0, np.frexp(amax)[1] - 1 + 127, 0) - down, 1)
    scale = np.exp2(byte - 127.0)
    codes = (blocks / scale).astype(np.float32).astype(dtype).astype(np.float64)
    return np.moveaxis((codes * scale).reshape(v.shape), -1, axis)


WIDE = False


def mx_kscale(k):
    if not WIDE:
        return np.ones(k)
    levels = np.array([10, -10, 5, -5, 0])
    if k % 512:
        return np.exp2(np.random.permutation(np.resize(levels, k // 32))).repeat(32)
    a = np.empty((k // 512, 16))
    for p in range(k // 512):
        a[p, :8] = np.random.permutation(np.resize(levels, 8))
        for g in range(8):
            far = levels[np.abs(levels - a[p, g]) >= 10]
            a[p, g + 8] = far[np.random.randint(len(far))]
    return np.exp2(a.ravel()).repeat(32)


def f64(x):
    return np.asarray(x).astype(np.float64)


def striped(idx):
    return np.tile(idx.reshape(-1, 16).T, (8, 1)).astype(np.uint16)


def unstriped(offs):
    return offs[:16].T.reshape(-1).astype(np.int64)


E2M1 = np.array([0.0, 0.5, 1.0, 1.5, 2.0, 3.0, 4.0, 6.0, -0.0, -0.5, -1.0, -1.5, -2.0, -3.0, -4.0, -6.0])


def pack_weight(w, fmt):
    k, n = w.shape
    w = f64(np.asarray(w, np.float32).astype(ml_dtypes.bfloat16)).reshape(k // 32, 32, n)
    amax = np.abs(w).max(1)
    if fmt == "e4m3":
        byte = np.frexp(amax)[1] - 1 + 127 - 7
    else:
        mant, ex = np.frexp(amax / 6.0)
        byte = np.where(mant > 0.5, ex, ex - 1) + 127
    byte = np.clip(np.where(amax > 0, byte, 1), 1, 254)
    scaled = (w * np.exp2(127.0 - byte)[:, None, :]).reshape(k, n).astype(np.float32)
    by_word = np.ascontiguousarray(scaled.reshape(k // 512, 128, 4, n).transpose(0, 1, 3, 2))
    if fmt == "e4m3":
        words = by_word.astype(ml_dtypes.float8_e4m3fn).view(np.uint8)
    else:
        c = by_word.astype(ml_dtypes.float4_e2m1fn).view(np.uint8) & 0xF
        words = (c[..., 0::2] | (c[..., 1::2] << 4)).reshape(k // 512, 128, 2 * n)
    return np.ascontiguousarray(words), np.ascontiguousarray(byte.astype(np.uint8).reshape(k // 512, 16, n))


def unpack_weight(words, scales, fmt):
    g, _, n = scales.shape
    words = np.ascontiguousarray(words).reshape(g, 128, n, -1)
    if fmt == "e4m3":
        vals = words.view(ml_dtypes.float8_e4m3fn).astype(np.float64)
    else:
        nib = np.empty((g, 128, n, 4), np.uint8)
        nib[..., 0::2] = words & 0xF
        nib[..., 1::2] = words >> 4
        vals = E2M1[nib]
    vals = vals * np.repeat(np.exp2(scales.astype(np.float64) - 127.0), 8, axis=1)[..., None]
    return vals.transpose(0, 1, 3, 2).reshape(g * 512, n)


K, T, E, C, N = 1024, 640, 10, 128, 384


def by_expert(wq, xq):
    return np.concatenate([wq[e].T @ xq[:, e * C:(e + 1) * C] for e in range(E)], axis=1)


def setup_inputs():
    n = np.random.standard_normal
    s = mx_kscale(K)[:, None]
    first = np.random.permutation(np.repeat(np.arange(E), T // E))
    second = (first + 1 + np.random.permutation(np.repeat(np.arange(E - 1), -(-T // (E - 1)))[:T])) % E
    while np.bincount(second, minlength=E).max() != T // E:
        load = np.bincount(second, minlength=E); hi, lo = int(load.argmax()), int(load.argmin())
        t = np.flatnonzero((second == hi) & (first != lo))[0]; second[t] = lo
    slot_token = np.empty(E * C, np.int64); pos = np.empty((2, T), np.int64); fill = np.zeros(E, np.int64)
    place = np.stack([np.random.permutation(C) for _ in range(E)])
    for r, deal in enumerate((first, second)):
        for t in np.random.permutation(T):
            e = deal[t]; j = e * C + place[e, fill[e]]; fill[e] += 1; slot_token[j] = t; pos[r, t] = j
    g = np.random.uniform(0.2, 0.8, T)
    w = [pack_weight(m, "e2m1") for m in n((E + 1, K, N)) / np.sqrt(K) / s[None]]
    return {
        "xT": (n((K, T)) * s).astype(np.float32),
        "w_words": np.stack([m[0] for m in w]),
        "w_scales": np.stack([m[1] for m in w]),
        "gate": np.stack([np.tile(g, (N, 1)), np.tile(1.0 - g, (N, 1))]).astype(np.float32),
        "offs": striped(slot_token),
        "pos1": striped(pos[0]),
        "pos2": striped(pos[1]),
    }


def reference(xT, w_words, w_scales, gate, offs, pos1, pos2):
    idx = unstriped(offs)
    w = np.stack([unpack_weight(w_words[e], w_scales[e], "e2m1") for e in range(E + 1)])
    wq = w
    xs = mxq(f64(xT), 0, "e4m3")
    ys = wq[E].T @ xs
    xq = mxq(f64(xT)[:, idx], 0, "e4m3")
    y = by_expert(w, xq)
    return ys + f64(gate[0]) * y[:, unstriped(pos1)] + f64(gate[1]) * y[:, unstriped(pos2)]

@@ -1,0 +1,237 @@
+from contextlib import ExitStack
+
+import concourse.mybir as mybir
+
+K, T, E, C, N = 1024, 640, 10, 128, 384
+S = E * C
+FLOPS = 2 * K * N * (S + T)
+
+F32 = mybir.dt.float32
+BF16 = mybir.dt.bfloat16
+U32 = mybir.dt.uint32
+I32 = mybir.dt.int32
+U16 = mybir.dt.uint16
+U8 = mybir.dt.uint8
+FP8X4 = mybir.dt.float8_e4m3fn_x4
+FP4X4 = mybir.dt.float4_e2m1fn_x4
+MULT = mybir.AluOpType.mult
+ADD = mybir.AluOpType.add
+COPY = mybir.ActivationFunctionType.Copy
+
+P = 128
+PASSES = 2
+M = N // P
+
+
+def tile_moe_shr_lin_none_kernel(tc, xT, w_words, w_scales, gate, offs, pos1, pos2, out):
+    nc = tc.nc
+    with ExitStack() as ctx:
+        keep = ctx.enter_context(tc.tile_pool(name="keep", bufs=1))
+        work = ctx.enter_context(tc.tile_pool(name="work", bufs=1))
+        psum = ctx.enter_context(tc.psum_pool(name="psum", bufs=1))
+
+        offs_t = keep.tile([P, S // 16], U16, name="offs_t")
+        pos1_t = keep.tile([P, T // 16], U16, name="pos1_t")
+        pos2_t = keep.tile([P, T // 16], U16, name="pos2_t")
+
+        raw = [work.tile([P, 4, T], F32, name=f"raw{a}") for a in range(PASSES)]
+        x_view = xT.rearrange("(a p j) t -> a p j t", a=PASSES, p=P, j=4)
+
+        def load_x(a, u, t0, t1):
+            nc.sync.dma_start(raw[a][:, 2 * u : 2 * u + 2, t0:t1], x_view[a][:, 2 * u : 2 * u + 2, t0:t1])
+
+        load_x(0, 0, 0, 320)
+        load_x(0, 0, 320, T)
+        nc.sync.dma_start(offs_t[:], offs)
+        load_x(0, 1, 0, T)
+        load_x(1, 0, 0, T)
+        load_x(1, 1, 0, T)
+
+        ws = work.tile([P, (E + 1) * PASSES, N], U8, name="ws", align_bytes=64)
+        nc.vector.memset(ws[:].rearrange("p e n -> p (e n)").bitcast(I32), 0)
+        s_view = w_scales.rearrange("e a q n -> q (e a) n").bitcast(I32)
+        for q in range(4):
+            nc.sync.dma_start(ws[32 * q : 32 * q + 4].bitcast(I32), s_view[4 * q : 4 * q + 4])
+
+        ww = work.tile([P, (E + 1) * PASSES, 2 * N], U8, name="ww", align_bytes=64)
+        w_view = w_words.rearrange("e a p b -> p (e a) b").bitcast(I32)
+        for e0, e1 in ((0, 4), (4, 8), (8, 11)):
+            nc.sync.dma_start(ww[:, PASSES * e0 : PASSES * e1, :].bitcast(I32), w_view[:, PASSES * e0 : PASSES * e1, :])
+        nc.sync.dma_start(pos1_t[:], pos1)
+        nc.sync.dma_start(pos2_t[:], pos2)
+        gates = []
+        for m in range(M):
+            g = work.tile([P, 2, T], F32, name=f"gate{m}")
+            nc.sync.dma_start(g[:], gate[:, m * P : (m + 1) * P, :].rearrange("g p t -> p g t"))
+            gates.append(g)
+
+        pairs = work.tile([P, 2 * PASSES, T, 2], BF16, name="pairs", align_bytes=64)
+        pair_words = pairs[:].rearrange("p b t d -> p (b t d)").bitcast(U32)
+        last_rows = work.tile([P, 2, T], BF16, name="last_rows", align_bytes=64)
+        block = {(1, 0): 0, (1, 1): 1, (0, 0): 2, (0, 1): 3}
+        slots = [work.tile([P, S, 4], BF16, name=f"slots{a}", align_bytes=64) for a in range(PASSES)]
+        slot_codes = [work.tile([P, S], U32, name=f"slot_codes{a}", align_bytes=64) for a in range(PASSES)]
+        slot_scales = [work.tile([P, S], U8, name=f"slot_scales{a}", align_bytes=64) for a in range(PASSES)]
+        toks = work.tile([P, PASSES * T, 4], BF16, name="toks", align_bytes=64)
+        tok_codes = work.tile([P, PASSES * T], U32, name="tok_codes", align_bytes=64)
+        tok_scales = work.tile([P, PASSES * T], U8, name="tok_scales", align_bytes=64)
+
+        def cast(engine_copy, a, u, t0, t1):
+            engine_copy(out=pairs[:, block[a, u], t0:t1, :], in_=raw[a][:, 2 * u : 2 * u + 2, t0:t1].rearrange("p j t -> p t j"))
+
+        def round_on_gpsimd(out, in_):
+            nc.gpsimd.tensor_scalar(out, in_, 1.0, 0.0, MULT, ADD)
+
+        def planes_tile(tag, n):
+            return work.tile([P, 2, n, 2], BF16, name="planes", tag=tag, align_bytes=64)
+
+        def gather(planes, base, a, u, lo, hi):
+            start = block[a, u] * T
+            stop = start + T if a == 0 else start + 2 * T
+            window = pair_words[:, start:stop]
+            dst = planes[:, u, lo - base : hi - base, :].rearrange("p s d -> p (s d)").bitcast(U32)
+            nc.vector.tensor_copy(dst, window.indirect(offs_t[:, lo // 16 : hi // 16]))
+
+        def interleave_slots(copy, dtype, planes, a, lo, hi):
+            src = planes[:].rearrange("p u s d -> p (u s d)").bitcast(dtype).rearrange("p (u s) -> p s u", u=2)
+            dst = slots[a][:].rearrange("p s d -> p (s d)").bitcast(dtype).rearrange("p (s u) -> p s u", u=2)
+            copy(out=dst[:, lo:hi, :], in_=src)
+
+        def quantize_slots(a, lo, hi):
+            nc.vector.quantize_mx(
+                out=slot_codes[a][:, lo:hi].bitcast(FP8X4),
+                scales=slot_scales[a][:, lo:hi],
+                in_=slots[a][:, lo:hi, :].rearrange("p s d -> p (s d)"),
+            )
+
+        def quantize_toks(lo, hi):
+            nc.vector.quantize_mx(
+                out=tok_codes[:, lo:hi].bitcast(FP8X4),
+                scales=tok_scales[:, lo:hi],
+                in_=toks[:, lo:hi, :].rearrange("p s d -> p (s d)"),
+            )
+
+        def round_toks(a):
+            for t0 in (0, 320):
+                dst = toks[:, a * T + t0 : a * T + t0 + 320, :]
+                round_on_gpsimd(dst, raw[a][:, :, t0 : t0 + 320].rearrange("p j t -> p t j"))
+
+        def gather_on_scalar(planes, base, e):
+            for d in range(2):
+                nc.scalar.activation(
+                    planes[:, 1, e * C - base : (e + 1) * C - base, d],
+                    last_rows[:, d, :].indirect(offs_t[:, e * C // 16 : (e + 1) * C // 16]),
+                    COPY,
+                )
+
+        def matmul(dst, e, a, m, codes, scales):
+            nc.tensor.matmul_mx(
+                out=dst,
+                lhsT=ww[:, PASSES * e + a, 2 * m * P : 2 * (m + 1) * P].bitcast(FP4X4),
+                lhsT_scale=ws[:, PASSES * e + a, m * P : (m + 1) * P],
+                rhs=codes.bitcast(FP8X4),
+                rhs_scale=scales,
+                start=(a == 0),
+                stop=(a == PASSES - 1),
+            )
+
+        y = [work.tile([P, S], F32, name=f"y{m}") for m in range(M)]
+
+        def experts(m, e0, e1):
+            bank = psum.tile([P, 512], F32, name="bank", bufs=4)
+            for e in range(e0, e1):
+                for a in range(PASSES):
+                    cols = slice(e * C, (e + 1) * C)
+                    matmul(bank[:, (e - e0) * C : (e - e0 + 1) * C], e, a, m, slot_codes[a][:, cols], slot_scales[a][:, cols])
+            nc.scalar.copy(out=y[m][:, e0 * C : e1 * C], in_=bank[:, : (e1 - e0) * C])
+
+        for half in (0, 320):
+            cast(nc.vector.tensor_copy, 0, 0, half, half + 208)
+            cast(lambda out, in_: nc.scalar.activation(out, in_, COPY), 0, 0, half + 208, half + 320)
+        cast(nc.scalar.copy, 0, 1, 0, T)
+        cast(nc.scalar.copy, 1, 0, 0, T)
+        cast(nc.scalar.copy, 1, 1, 0, T)
+        round_toks(0)
+        for d in range(2):
+            round_on_gpsimd(last_rows[:, d, :], raw[1][:, 2 + d, :])
+        round_toks(1)
+        halves = [planes_tile("planes_a", 640), planes_tile("planes_b", 640)]
+        for lo, hi in ((0, 320), (320, 640)):
+            gather(halves[0], 0, 0, 0, lo, hi)
+        for lo, hi in ((640, 960), (960, S)):
+            gather(halves[1], 640, 0, 0, lo, hi)
+        for lo, hi in ((0, 320), (320, 640)):
+            gather(halves[0], 0, 0, 1, lo, hi)
+        interleave_slots(nc.scalar.copy, U32, halves[0], 0, 0, 640)
+        for lo, hi in ((640, 960), (960, S)):
+            gather(halves[1], 640, 0, 1, lo, hi)
+        interleave_slots(nc.scalar.copy, U32, halves[1], 0, 640, S)
+        part0 = planes_tile("planes_c", 512)
+        for u in range(2):
+            gather(part0, 0, 1, u, 0, 512)
+        interleave_slots(nc.scalar.copy, U32, part0, 1, 0, 512)
+        quantize_slots(0, 0, 1024)
+        quantize_slots(0, 1024, S)
+        part1 = planes_tile("planes_b", 512)
+        gather(part1, 512, 1, 0, 512, 1024)
+        for e in range(4, 8):
+            gather_on_scalar(part1, 512, e)
+        interleave_slots(nc.scalar.copy, U32, part1, 1, 512, 1024)
+        quantize_slots(1, 0, 512)
+        for m in range(M):
+            experts(m, 0, 4)
+        part2 = planes_tile("planes_c", 256)
+        for u in range(2):
+            gather(part2, 1024, 1, u, 1024, S)
+        quantize_slots(1, 512, 1024)
+        interleave_slots(nc.vector.tensor_copy, I32, part2, 1, 1024, S)
+        quantize_slots(1, 1024, S)
+        for m in range(M):
+            experts(m, 4, 8)
+            experts(m, 8, 10)
+        quantize_toks(0, 1024)
+        quantize_toks(1024, PASSES * T)
+
+        ys = [psum.tile([P, 512], F32, name=f"ys{m}") for m in range(M)]
+        shared = [work.tile([P, T], F32, name=f"shared{m}") for m in range(M)]
+        ys_tail = psum.tile([P, M, P], F32, name="ys_tail")
+        for m in range(M):
+            for dst, lo, hi in ((ys[m][:], 0, 512), (ys_tail[:, m, :], 512, T)):
+                for a in range(PASSES):
+                    matmul(dst, E, a, m, tok_codes[:, a * T + lo : a * T + hi], tok_scales[:, a * T + lo : a * T + hi])
+            nc.scalar.copy(out=shared[m][:, :512], in_=ys[m][:])
+            nc.scalar.copy(out=shared[m][:, 512:], in_=ys_tail[:, m, :])
+
+        first = [work.tile([P, T], F32, name=f"first{m}") for m in range(M)]
+        second = [work.tile([P, T], F32, name=f"second{m}") for m in range(M)]
+        both = [work.tile([P, T], F32, name=f"both{m}") for m in range(M)]
+        res = [work.tile([P, T], F32, name=f"res{m}") for m in range(M)]
+
+        def pick1(m):
+            nc.vector.tensor_tensor(first[m][:], y[m][:].indirect(pos1_t[:]), gates[m][:, 0, :], MULT)
+
+        def pick2(m, lo, hi):
+            nc.vector.tensor_tensor(second[m][:, lo:hi], y[m][:].indirect(pos2_t[:, lo // 16 : hi // 16]), gates[m][:, 1, lo:hi], MULT)
+
+        def add(m, lo, hi):
+            nc.vector.tensor_tensor(both[m][:, lo:hi], first[m][:, lo:hi], second[m][:, lo:hi], ADD)
+
+        def finish(m, lo, hi):
+            nc.vector.tensor_tensor(res[m][:, lo:hi], shared[m][:, lo:hi], both[m][:, lo:hi], ADD)
+            nc.sync.dma_start(out[m * P : (m + 1) * P, lo:hi], res[m][:, lo:hi])
+
+        pick1(0)
+        pick2(0, 0, T)
+        pick1(1)
+        add(0, 0, T)
+        pick2(1, 0, T)
+        finish(0, 0, T)
+        pick1(2)
+        add(1, 0, T)
+        pick2(2, 0, 448)
+        finish(1, 0, T)
+        pick2(2, 448, T)
+        add(2, 0, 448)
+        add(2, 448, T)
+        finish(2, 0, 448)
+        finish(2, 448, T)

@@ -1,6 +1,7 @@
 from contextlib import ExitStack
 
 import concourse.mybir as mybir
+from concourse.masks import make_identity
 
 K, T, E, C, N = 1024, 640, 10, 128, 384
 S = E * C
@@ -21,6 +22,8 @@ COPY = mybir.ActivationFunctionType.Copy
 P = 128
 PASSES = 2
 M = N // P
+BANK = 512
+GROUPS = ((0, 4), (4, 8), (8, 10))
 
 
 def tile_moe_shr_lin_none_kernel(tc, xT, w_words, w_scales, gate, offs, pos1, pos2, out):
@@ -34,204 +37,223 @@ def tile_moe_shr_lin_none_kernel(tc, xT, w_words, w_scales, gate, offs, pos1, po
         pos1_t = keep.tile([P, T // 16], U16, name="pos1_t")
         pos2_t = keep.tile([P, T // 16], U16, name="pos2_t")
 
-        raw = [work.tile([P, 4, T], F32, name=f"raw{a}") for a in range(PASSES)]
         x_view = xT.rearrange("(a p j) t -> a p j t", a=PASSES, p=P, j=4)
 
         def load_x(a, u, t0, t1):
-            nc.sync.dma_start(raw[a][:, 2 * u : 2 * u + 2, t0:t1], x_view[a][:, 2 * u : 2 * u + 2, t0:t1])
+            raw = work.tile([P, 2, t1 - t0], F32, name=f"raw{a}{u}_{t0}")
+            nc.sync.dma_start(raw[:], x_view[a][:, 2 * u : 2 * u + 2, t0:t1])
+            return raw
 
-        load_x(0, 0, 0, 320)
-        load_x(0, 0, 320, T)
+        raw_first = [(t0, t1, load_x(0, 0, t0, t1)) for t0, t1 in ((0, 384), (384, T))]
         nc.sync.dma_start(offs_t[:], offs)
-        load_x(0, 1, 0, T)
-        load_x(1, 0, 0, T)
-        load_x(1, 1, 0, T)
+        raw = {au: load_x(au[0], au[1], 0, T) for au in ((0, 1), (1, 0), (1, 1))}
 
         ws = work.tile([P, (E + 1) * PASSES, N], U8, name="ws", align_bytes=64)
-        nc.vector.memset(ws[:].rearrange("p e n -> p (e n)").bitcast(I32), 0)
+        nc.gpsimd.memset(ws[:].rearrange("p e n -> p (e n)").bitcast(I32), 0)
         s_view = w_scales.rearrange("e a q n -> q (e a) n").bitcast(I32)
-        for q in range(4):
-            nc.sync.dma_start(ws[32 * q : 32 * q + 4].bitcast(I32), s_view[4 * q : 4 * q + 4])
+        for r in range(4):
+            nc.sync.dma_start(ws[r:P:32].bitcast(I32), s_view[r:16:4])
 
-        ww = work.tile([P, (E + 1) * PASSES, 2 * N], U8, name="ww", align_bytes=64)
         w_view = w_words.rearrange("e a p b -> p (e a) b").bitcast(I32)
+        ww = {}
         for e0, e1 in ((0, 4), (4, 8), (8, 11)):
-            nc.sync.dma_start(ww[:, PASSES * e0 : PASSES * e1, :].bitcast(I32), w_view[:, PASSES * e0 : PASSES * e1, :])
+            wt = work.tile([P, (e1 - e0) * PASSES, 2 * N], U8, name=f"ww{e0}", align_bytes=64)
+            nc.sync.dma_start(wt[:].bitcast(I32), w_view[:, PASSES * e0 : PASSES * e1, :])
+            for e in range(e0, e1):
+                ww[e] = wt[:, PASSES * (e - e0) : PASSES * (e - e0 + 1), :]
         nc.sync.dma_start(pos1_t[:], pos1)
         nc.sync.dma_start(pos2_t[:], pos2)
-        gates = []
-        for m in range(M):
-            g = work.tile([P, 2, T], F32, name=f"gate{m}")
-            nc.sync.dma_start(g[:], gate[:, m * P : (m + 1) * P, :].rearrange("g p t -> p g t"))
-            gates.append(g)
+        gates = [work.tile([P, T], F32, name=f"gate{g}") for g in range(2)]
+        for g in range(2):
+            nc.sync.dma_start(gates[g][:], gate[g, :P, :])
 
-        pairs = work.tile([P, 2 * PASSES, T, 2], BF16, name="pairs", align_bytes=64)
-        pair_words = pairs[:].rearrange("p b t d -> p (b t d)").bitcast(U32)
-        last_rows = work.tile([P, 2, T], BF16, name="last_rows", align_bytes=64)
-        block = {(1, 0): 0, (1, 1): 1, (0, 0): 2, (0, 1): 3}
-        slots = [work.tile([P, S, 4], BF16, name=f"slots{a}", align_bytes=64) for a in range(PASSES)]
-        slot_codes = [work.tile([P, S], U32, name=f"slot_codes{a}", align_bytes=64) for a in range(PASSES)]
-        slot_scales = [work.tile([P, S], U8, name=f"slot_scales{a}", align_bytes=64) for a in range(PASSES)]
-        toks = work.tile([P, PASSES * T, 4], BF16, name="toks", align_bytes=64)
-        tok_codes = work.tile([P, PASSES * T], U32, name="tok_codes", align_bytes=64)
+        ident = work.tile([P, P], F32, name="ident")
+        make_identity(nc, ident[:])
+
+        pairs = work.tile([P, 2 * PASSES * T * 2], BF16, name="pairs", align_bytes=64)
+        pair_words = pairs[:].bitcast(U32)
+        block = {(1, 1): 0, (1, 0): 1, (0, 1): 2, (0, 0): 3}
+        last_rows = [work.tile([P, T], BF16, name=f"last_row{d}", align_bytes=64) for d in range(2)]
+        toks = work.tile([P, PASSES * T * 4], BF16, name="toks", align_bytes=64)
         tok_scales = work.tile([P, PASSES * T], U8, name="tok_scales", align_bytes=64)
 
-        def cast(engine_copy, a, u, t0, t1):
-            engine_copy(out=pairs[:, block[a, u], t0:t1, :], in_=raw[a][:, 2 * u : 2 * u + 2, t0:t1].rearrange("p j t -> p t j"))
+        width = [(e1 - e0) * C for e0, e1 in GROUPS]
+        cells = [(a, g) for a in range(PASSES) for g in range(len(GROUPS))]
+        planes = {(a, g): work.tile([P, 2, width[g]], U32, name=f"planes{a}{g}", align_bytes=64) for a, g in cells}
+        slots = {(a, g): work.tile([P, width[g] * 4], BF16, name=f"slots{a}{g}", tag=f"slots{a}{g}", align_bytes=64) for a, g in cells}
+        codes = {(a, g): work.tile([P, width[g]], U32, name=f"codes{a}{g}", align_bytes=64) for a, g in cells}
+        scales = {(a, g): work.tile([P, width[g]], U8, name=f"scales{a}{g}", align_bytes=64) for a, g in cells}
 
-        def round_on_gpsimd(out, in_):
+        def cast(copy, a, u, src, t0, t1):
+            base = block[a, u] * 2 * T
+            dst = pairs[:, base + 2 * t0 : base + 2 * t1].rearrange("p (t d) -> p t d", d=2)
+            copy(out=dst, in_=src[:].rearrange("p j t -> p t j"))
+
+        def copy_on_gpsimd(out, in_):
             nc.gpsimd.tensor_scalar(out, in_, 1.0, 0.0, MULT, ADD)
 
-        def planes_tile(tag, n):
-            return work.tile([P, 2, n, 2], BF16, name="planes", tag=tag, align_bytes=64)
-
-        def gather(planes, base, a, u, lo, hi):
+        def gather(a, u, g):
             start = block[a, u] * T
-            stop = start + T if a == 0 else start + 2 * T
-            window = pair_words[:, start:stop]
-            dst = planes[:, u, lo - base : hi - base, :].rearrange("p s d -> p (s d)").bitcast(U32)
-            nc.vector.tensor_copy(dst, window.indirect(offs_t[:, lo // 16 : hi // 16]))
+            lo = GROUPS[g][0] * C
+            if (a, u) == (0, 0):
+                window, piece = pair_words[:, start : start + T], 256
+            else:
+                window, piece = pair_words[:, start : start + 2 * T], width[g]
+            for s in range(0, width[g], piece):
+                nc.vector.tensor_copy(planes[a, g][:, u, s : s + piece], window.indirect(offs_t[:, (lo + s) // 16 : (lo + s + piece) // 16]))
 
-        def interleave_slots(copy, dtype, planes, a, lo, hi):
-            src = planes[:].rearrange("p u s d -> p (u s d)").bitcast(dtype).rearrange("p (u s) -> p s u", u=2)
-            dst = slots[a][:].rearrange("p s d -> p (s d)").bitcast(dtype).rearrange("p (s u) -> p s u", u=2)
-            copy(out=dst[:, lo:hi, :], in_=src)
+        def gather_on_scalar(g):
+            lo = GROUPS[g][0] * C
+            dst = planes[0, g][:, 1, :].bitcast(BF16).rearrange("p (s d) -> p s d", d=2)
+            for s in range(0, width[g], 256):
+                for d in range(2):
+                    nc.scalar.activation(dst[:, s : s + 256, d], last_rows[d][:].indirect(offs_t[:, (lo + s) // 16 : (lo + s + 256) // 16]), COPY)
 
-        def quantize_slots(a, lo, hi):
-            nc.vector.quantize_mx(
-                out=slot_codes[a][:, lo:hi].bitcast(FP8X4),
-                scales=slot_scales[a][:, lo:hi],
-                in_=slots[a][:, lo:hi, :].rearrange("p s d -> p (s d)"),
-            )
+        def weave(copy, dtype, a, g):
+            src = planes[a, g][:].bitcast(dtype).rearrange("p u s -> p s u")
+            dst = slots[a, g][:].bitcast(dtype).rearrange("p (s u) -> p s u", u=2)
+            copy(out=dst, in_=src)
 
-        def quantize_toks(lo, hi):
-            nc.vector.quantize_mx(
-                out=tok_codes[:, lo:hi].bitcast(FP8X4),
-                scales=tok_scales[:, lo:hi],
-                in_=toks[:, lo:hi, :].rearrange("p s d -> p (s d)"),
-            )
+        def quantize_slots(a, g):
+            nc.vector.quantize_mx(out=codes[a, g][:].bitcast(FP8X4), scales=scales[a, g][:], in_=slots[a, g][:])
 
-        def round_toks(a):
+        def quantize_toks(tok_codes, lo, hi):
+            nc.vector.quantize_mx(out=tok_codes[:, lo:hi].bitcast(FP8X4), scales=tok_scales[:, lo:hi], in_=toks[:, 4 * lo : 4 * hi])
+
+        def weave_toks(a):
+            base = block[a, 1] * 2 * T
+            both = pairs[:, base : base + 4 * T].rearrange("p (u t d) -> p t u d", u=2, d=2)
             for t0 in (0, 320):
-                dst = toks[:, a * T + t0 : a * T + t0 + 320, :]
-                round_on_gpsimd(dst, raw[a][:, :, t0 : t0 + 320].rearrange("p j t -> p t j"))
+                dst = toks[:, 4 * (a * T + t0) : 4 * (a * T + t0 + 320)].rearrange("p (t u d) -> p t u d", u=2, d=2)
+                copy_on_gpsimd(dst, both[:, t0 : t0 + 320, ::-1, :])
 
-        def gather_on_scalar(planes, base, e):
-            for d in range(2):
-                nc.scalar.activation(
-                    planes[:, 1, e * C - base : (e + 1) * C - base, d],
-                    last_rows[:, d, :].indirect(offs_t[:, e * C // 16 : (e + 1) * C // 16]),
-                    COPY,
-                )
-
-        def matmul(dst, e, a, m, codes, scales):
+        def matmul(dst, e, a, m, rhs, rhs_scale):
             nc.tensor.matmul_mx(
                 out=dst,
-                lhsT=ww[:, PASSES * e + a, 2 * m * P : 2 * (m + 1) * P].bitcast(FP4X4),
+                lhsT=ww[e][:, a, 2 * m * P : 2 * (m + 1) * P].bitcast(FP4X4),
                 lhsT_scale=ws[:, PASSES * e + a, m * P : (m + 1) * P],
-                rhs=codes.bitcast(FP8X4),
-                rhs_scale=scales,
+                rhs=rhs.bitcast(FP8X4),
+                rhs_scale=rhs_scale,
                 start=(a == 0),
                 stop=(a == PASSES - 1),
             )
 
+        def new_bank():
+            return psum.tile([P, BANK], F32, name="bank", bufs=8)
+
         y = [work.tile([P, S], F32, name=f"y{m}") for m in range(M)]
 
-        def experts(m, e0, e1):
-            bank = psum.tile([P, 512], F32, name="bank", bufs=4)
+        def experts(m, g):
+            bank = new_bank()
+            e0, e1 = GROUPS[g]
             for e in range(e0, e1):
+                cols = slice((e - e0) * C, (e - e0 + 1) * C)
                 for a in range(PASSES):
-                    cols = slice(e * C, (e + 1) * C)
-                    matmul(bank[:, (e - e0) * C : (e - e0 + 1) * C], e, a, m, slot_codes[a][:, cols], slot_scales[a][:, cols])
-            nc.scalar.copy(out=y[m][:, e0 * C : e1 * C], in_=bank[:, : (e1 - e0) * C])
+                    matmul(bank[:, cols], e, a, m, codes[a, g][:, cols], scales[a, g][:, cols])
+            return lambda: nc.scalar.copy(out=y[m][:, e0 * C : e1 * C], in_=bank[:, : width[g]])
 
-        for half in (0, 320):
-            cast(nc.vector.tensor_copy, 0, 0, half, half + 208)
-            cast(lambda out, in_: nc.scalar.activation(out, in_, COPY), 0, 0, half + 208, half + 320)
-        cast(nc.scalar.copy, 0, 1, 0, T)
-        cast(nc.scalar.copy, 1, 0, 0, T)
-        cast(nc.scalar.copy, 1, 1, 0, T)
-        round_toks(0)
+        for t0, t1, src in raw_first:
+            cast(nc.vector.tensor_copy, 0, 0, src, t0, t1)
+        for a, u in ((0, 1), (1, 0)):
+            cast(nc.scalar.copy, a, u, raw[a, u], 0, T)
         for d in range(2):
-            round_on_gpsimd(last_rows[:, d, :], raw[1][:, 2 + d, :])
-        round_toks(1)
-        halves = [planes_tile("planes_a", 640), planes_tile("planes_b", 640)]
-        for lo, hi in ((0, 320), (320, 640)):
-            gather(halves[0], 0, 0, 0, lo, hi)
-        for lo, hi in ((640, 960), (960, S)):
-            gather(halves[1], 640, 0, 0, lo, hi)
-        for lo, hi in ((0, 320), (320, 640)):
-            gather(halves[0], 0, 0, 1, lo, hi)
-        interleave_slots(nc.scalar.copy, U32, halves[0], 0, 0, 640)
-        for lo, hi in ((640, 960), (960, S)):
-            gather(halves[1], 640, 0, 1, lo, hi)
-        interleave_slots(nc.scalar.copy, U32, halves[1], 0, 640, S)
-        part0 = planes_tile("planes_c", 512)
+            copy_on_gpsimd(last_rows[d][:], raw[0, 1][:, d, :])
+        cast(copy_on_gpsimd, 1, 1, raw[1, 1], 0, T)
+        weave_toks(0)
+        weave_toks(1)
+        for g in range(3):
+            gather(0, 0, g)
+        gather(0, 1, 0)
+        gather(0, 1, 2)
+        weave(nc.scalar.copy, U32, 0, 0)
+        weave(nc.scalar.copy, U32, 0, 2)
+        gather_on_scalar(1)
+        weave(nc.scalar.copy, U32, 0, 1)
         for u in range(2):
-            gather(part0, 0, 1, u, 0, 512)
-        interleave_slots(nc.scalar.copy, U32, part0, 1, 0, 512)
-        quantize_slots(0, 0, 1024)
-        quantize_slots(0, 1024, S)
-        part1 = planes_tile("planes_b", 512)
-        gather(part1, 512, 1, 0, 512, 1024)
-        for e in range(4, 8):
-            gather_on_scalar(part1, 512, e)
-        interleave_slots(nc.scalar.copy, U32, part1, 1, 512, 1024)
-        quantize_slots(1, 0, 512)
-        for m in range(M):
-            experts(m, 0, 4)
-        part2 = planes_tile("planes_c", 256)
-        for u in range(2):
-            gather(part2, 1024, 1, u, 1024, S)
-        quantize_slots(1, 512, 1024)
-        interleave_slots(nc.vector.tensor_copy, I32, part2, 1, 1024, S)
-        quantize_slots(1, 1024, S)
-        for m in range(M):
-            experts(m, 4, 8)
-            experts(m, 8, 10)
-        quantize_toks(0, 1024)
-        quantize_toks(1024, PASSES * T)
+            for g in range(3):
+                gather(1, u, g)
+        weave(nc.scalar.copy, U32, 1, 0)
+        weave(nc.scalar.copy, U32, 1, 1)
+        quantize_slots(0, 0)
+        quantize_slots(0, 2)
+        weave(nc.vector.tensor_copy, I32, 1, 2)
+        quantize_slots(0, 1)
+        quantize_slots(1, 0)
+        quantize_slots(1, 2)
+        quantize_slots(1, 1)
+        tok_codes = work.tile([P, PASSES * T], U32, name="tok_codes", tag="slots11", align_bytes=64)
+        quantize_toks(tok_codes, 0, 1024)
+        quantize_toks(tok_codes, 1024, PASSES * T)
 
-        ys = [psum.tile([P, 512], F32, name=f"ys{m}") for m in range(M)]
-        shared = [work.tile([P, T], F32, name=f"shared{m}") for m in range(M)]
-        ys_tail = psum.tile([P, M, P], F32, name="ys_tail")
+        for m, g in ((0, 0), (0, 2), (0, 1), (1, 0), (1, 2), (1, 1)):
+            experts(m, g)()
+        empty_last = [experts(2, g) for g in range(3)]
+
+        shared = work.tile([P, M, T], F32, name="shared")
+
+        def shared_expert(dst, m, lo, hi):
+            for a in range(PASSES):
+                matmul(dst, E, a, m, tok_codes[:, a * T + lo : a * T + hi], tok_scales[:, a * T + lo : a * T + hi])
+
+        def shared_head(m):
+            bank = new_bank()
+            shared_expert(bank[:], m, 0, BANK)
+            nc.scalar.copy(out=shared[:, m, :BANK], in_=bank[:])
+
+        shared_head(0)
+        tail = new_bank()
         for m in range(M):
-            for dst, lo, hi in ((ys[m][:], 0, 512), (ys_tail[:, m, :], 512, T)):
-                for a in range(PASSES):
-                    matmul(dst, E, a, m, tok_codes[:, a * T + lo : a * T + hi], tok_scales[:, a * T + lo : a * T + hi])
-            nc.scalar.copy(out=shared[m][:, :512], in_=ys[m][:])
-            nc.scalar.copy(out=shared[m][:, 512:], in_=ys_tail[:, m, :])
+            shared_expert(tail[:, m * P : (m + 1) * P], m, BANK, T)
+        nc.scalar.copy(out=shared[:, :, BANK:], in_=tail[:, : M * P].rearrange("p (m t) -> p m t", m=M))
+        for empty in empty_last:
+            empty()
+        shared_head(1)
+        shared_head(2)
 
         first = [work.tile([P, T], F32, name=f"first{m}") for m in range(M)]
-        second = [work.tile([P, T], F32, name=f"second{m}") for m in range(M)]
-        both = [work.tile([P, T], F32, name=f"both{m}") for m in range(M)]
-        res = [work.tile([P, T], F32, name=f"res{m}") for m in range(M)]
 
         def pick1(m):
-            nc.vector.tensor_tensor(first[m][:], y[m][:].indirect(pos1_t[:]), gates[m][:, 0, :], MULT)
+            nc.vector.tensor_tensor(first[m][:], y[m][:].indirect(pos1_t[:]), gates[0][:], MULT)
 
         def pick2(m, lo, hi):
-            nc.vector.tensor_tensor(second[m][:, lo:hi], y[m][:].indirect(pos2_t[:, lo // 16 : hi // 16]), gates[m][:, 1, lo:hi], MULT)
+            second = work.tile([P, hi - lo], F32, name=f"second{m}_{lo}")
+            nc.vector.tensor_tensor(second[:], y[m][:].indirect(pos2_t[:, lo // 16 : hi // 16]), gates[1][:, lo:hi], MULT)
+            return second
 
-        def add(m, lo, hi):
-            nc.vector.tensor_tensor(both[m][:, lo:hi], first[m][:, lo:hi], second[m][:, lo:hi], ADD)
+        def sum_turned(m, lo, hi, second):
+            bank = new_bank()
+            for t in range(lo, hi, P):
+                terms = (shared[:, m, t : t + P], first[m][:, t : t + P], second[:, t - lo : t - lo + P])
+                for i, term in enumerate(terms):
+                    nc.tensor.matmul(bank[:, t - lo : t - lo + P], term, ident[:], start=(i == 0), stop=(i == len(terms) - 1), is_transpose=True)
+            turned = work.tile([P, hi - lo], F32, name=f"turned{m}_{lo}")
+            nc.scalar.copy(out=turned[:], in_=bank[:, : hi - lo])
+            return turned
 
-        def finish(m, lo, hi):
-            nc.vector.tensor_tensor(res[m][:, lo:hi], shared[m][:, lo:hi], both[m][:, lo:hi], ADD)
-            nc.sync.dma_start(out[m * P : (m + 1) * P, lo:hi], res[m][:, lo:hi])
+        def turn_back(m, lo, hi, turned):
+            bank = new_bank()
+            for t in range(0, hi - lo, P):
+                nc.tensor.transpose(bank[:, t : t + P], turned[:, t : t + P], ident[:])
+            res = work.tile([P, hi - lo], F32, name=f"res{m}_{lo}")
+            nc.scalar.copy(out=res[:], in_=bank[:, : hi - lo])
+            nc.sync.dma_start(out[m * P : (m + 1) * P, lo:hi], res[:])
 
-        pick1(0)
-        pick2(0, 0, T)
-        pick1(1)
-        add(0, 0, T)
-        pick2(1, 0, T)
-        finish(0, 0, T)
-        pick1(2)
-        add(1, 0, T)
-        pick2(2, 0, 448)
-        finish(1, 0, T)
-        pick2(2, 448, T)
-        add(2, 0, 448)
-        add(2, 448, T)
-        finish(2, 0, 448)
-        finish(2, 448, T)
+        parts = [(0, 0, 384), (0, 384, T), (1, 0, 384), (1, 384, T), (2, 0, 256)]
+        waiting = None
+        for m, lo, hi in parts:
+            if lo == 0:
+                pick1(m)
+            turned = sum_turned(m, lo, hi, pick2(m, lo, hi))
+            if waiting is not None:
+                turn_back(*waiting)
+            waiting = (m, lo, hi, turned)
+        turn_back(*waiting)
+
+        partial = work.tile([P, T - 256], F32, name="partial")
+        nc.vector.tensor_tensor(partial[:], first[2][:, 256:], shared[:, 2, 256:], ADD)
+        ends = ((256, 512), (512, T))
+        seconds = [pick2(2, lo, hi) for lo, hi in ends]
+        for (lo, hi), second in zip(ends, seconds):
+            res = work.tile([P, hi - lo], F32, name=f"res2_{lo}")
+            nc.vector.tensor_tensor(res[:], partial[:, lo - 256 : hi - 256], second[:], ADD)
+            nc.sync.dma_start(out[2 * P :, lo:hi], res[:])

@@ -40,7 +40,7 @@ def tile_moe_shr_lin_none_kernel(tc, xT, w_words, w_scales, gate, offs, pos1, po
         x_view = xT.rearrange("(a p j) t -> a p j t", a=PASSES, p=P, j=4)
 
         def load_x(a, u, t0, t1):
-            raw = work.tile([P, 2, t1 - t0], F32, name=f"raw{a}{u}_{t0}")
+            raw = work.tile([P, 2, t1 - t0], F32, name=f"raw{a}{u}_{t0}", tag=f"raw{a}{u}_{t0}", align_bytes=64)
             nc.sync.dma_start(raw[:], x_view[a][:, 2 * u : 2 * u + 2, t0:t1])
             return raw
 
@@ -73,15 +73,15 @@ def tile_moe_shr_lin_none_kernel(tc, xT, w_words, w_scales, gate, offs, pos1, po
         pairs = work.tile([P, 2 * PASSES * T * 2], BF16, name="pairs", align_bytes=64)
         pair_words = pairs[:].bitcast(U32)
         block = {(1, 1): 0, (1, 0): 1, (0, 1): 2, (0, 0): 3}
-        last_rows = [work.tile([P, T], BF16, name=f"last_row{d}", align_bytes=64) for d in range(2)]
+        last_rows = [work.tile([P, T], BF16, name=f"last_row{d}", tag=("slots02", "slots00")[d], align_bytes=64) for d in range(2)]
         toks = work.tile([P, PASSES * T * 4], BF16, name="toks", align_bytes=64)
         tok_scales = work.tile([P, PASSES * T], U8, name="tok_scales", align_bytes=64)
 
         width = [(e1 - e0) * C for e0, e1 in GROUPS]
         cells = [(a, g) for a in range(PASSES) for g in range(len(GROUPS))]
         planes = {(a, g): work.tile([P, 2, width[g]], U32, name=f"planes{a}{g}", align_bytes=64) for a, g in cells}
-        slots = {(a, g): work.tile([P, width[g] * 4], BF16, name=f"slots{a}{g}", tag=f"slots{a}{g}", align_bytes=64) for a, g in cells}
-        codes = {(a, g): work.tile([P, width[g]], U32, name=f"codes{a}{g}", align_bytes=64) for a, g in cells}
+        slots = {(a, g): work.tile([P, width[g] * 4], BF16, name=f"slots{a}{g}", tag=f"slots{a}{g}", align_bytes=64) for a, g in cells if (a, g) not in ((0, 0), (0, 2))}
+        codes = {(1, g): work.tile([P, width[g]], U32, name=f"codes1{g}", align_bytes=64)[:] for g in range(len(GROUPS))}
         scales = {(a, g): work.tile([P, width[g]], U8, name=f"scales{a}{g}", align_bytes=64) for a, g in cells}
 
         def cast(copy, a, u, src, t0, t1):
@@ -115,17 +115,16 @@ def tile_moe_shr_lin_none_kernel(tc, xT, w_words, w_scales, gate, offs, pos1, po
             copy(out=dst, in_=src)
 
         def quantize_slots(a, g):
-            nc.vector.quantize_mx(out=codes[a, g][:].bitcast(FP8X4), scales=scales[a, g][:], in_=slots[a, g][:])
+            nc.vector.quantize_mx(out=codes[a, g].bitcast(FP8X4), scales=scales[a, g][:], in_=slots[a, g][:])
 
         def quantize_toks(tok_codes, lo, hi):
             nc.vector.quantize_mx(out=tok_codes[:, lo:hi].bitcast(FP8X4), scales=tok_scales[:, lo:hi], in_=toks[:, 4 * lo : 4 * hi])
 
         def weave_toks(a):
-            base = block[a, 1] * 2 * T
-            both = pairs[:, base : base + 4 * T].rearrange("p (u t d) -> p t u d", u=2, d=2)
-            for t0 in (0, 320):
-                dst = toks[:, 4 * (a * T + t0) : 4 * (a * T + t0 + 320)].rearrange("p (t u d) -> p t u d", u=2, d=2)
-                copy_on_gpsimd(dst, both[:, t0 : t0 + 320, ::-1, :])
+            base = block[a, 1] * T
+            src = pair_words[:, base : base + 2 * T].rearrange("p (u t) -> p t u", u=2)
+            dst = toks[:, 4 * a * T : 4 * (a + 1) * T].bitcast(U32).rearrange("p (t u) -> p t u", u=2)
+            nc.scalar.copy(out=dst, in_=src[:, :, ::-1])
 
         def matmul(dst, e, a, m, rhs, rhs_scale):
             nc.tensor.matmul_mx(
@@ -139,7 +138,7 @@ def tile_moe_shr_lin_none_kernel(tc, xT, w_words, w_scales, gate, offs, pos1, po
             )
 
         def new_bank():
-            return psum.tile([P, BANK], F32, name="bank", bufs=8)
+            return psum.tile([P, BANK], F32, name="bank", bufs=6)
 
         y = [work.tile([P, S], F32, name=f"y{m}") for m in range(M)]
 
@@ -154,61 +153,60 @@ def tile_moe_shr_lin_none_kernel(tc, xT, w_words, w_scales, gate, offs, pos1, po
 
         for t0, t1, src in raw_first:
             cast(nc.vector.tensor_copy, 0, 0, src, t0, t1)
-        for a, u in ((0, 1), (1, 0)):
-            cast(nc.scalar.copy, a, u, raw[a, u], 0, T)
+        cast(nc.scalar.copy, 0, 1, raw[0, 1], 0, T)
         for d in range(2):
             copy_on_gpsimd(last_rows[d][:], raw[0, 1][:, d, :])
-        cast(copy_on_gpsimd, 1, 1, raw[1, 1], 0, T)
-        weave_toks(0)
-        weave_toks(1)
+        for u in range(2):
+            cast(copy_on_gpsimd, 1, u, raw[1, u], 0, T)
+        codes0 = work.tile([P, S], U32, name="codes0", tag="raw11_0", align_bytes=64)
+        for g, (e0, e1) in enumerate(GROUPS):
+            codes[0, g] = codes0[:, e0 * C : e1 * C]
         for g in range(3):
             gather(0, 0, g)
         gather(0, 1, 0)
         gather(0, 1, 2)
-        weave(nc.scalar.copy, U32, 0, 0)
-        weave(nc.scalar.copy, U32, 0, 2)
         gather_on_scalar(1)
-        weave(nc.scalar.copy, U32, 0, 1)
+        for g in (0, 2):
+            slots[0, g] = work.tile([P, width[g] * 4], BF16, name=f"slots0{g}", tag=f"slots0{g}", align_bytes=64)
+        for g in (0, 2, 1):
+            weave(nc.scalar.copy, U32, 0, g)
         for u in range(2):
             for g in range(3):
                 gather(1, u, g)
-        weave(nc.scalar.copy, U32, 1, 0)
-        weave(nc.scalar.copy, U32, 1, 1)
-        quantize_slots(0, 0)
-        quantize_slots(0, 2)
-        weave(nc.vector.tensor_copy, I32, 1, 2)
-        quantize_slots(0, 1)
-        quantize_slots(1, 0)
-        quantize_slots(1, 2)
-        quantize_slots(1, 1)
-        tok_codes = work.tile([P, PASSES * T], U32, name="tok_codes", tag="slots11", align_bytes=64)
+        weave_toks(0)
+        for g in range(3):
+            weave(nc.scalar.copy, U32, 1, g)
+        weave_toks(1)
+        for g in range(3):
+            for a in range(PASSES):
+                quantize_slots(a, g)
+        tok_codes = work.tile([P, PASSES * T], U32, name="tok_codes", align_bytes=64)
         quantize_toks(tok_codes, 0, 1024)
         quantize_toks(tok_codes, 1024, PASSES * T)
 
-        for m, g in ((0, 0), (0, 2), (0, 1), (1, 0), (1, 2), (1, 1)):
+        for m, g in ((0, 0), (0, 1), (0, 2), (1, 0), (1, 1), (1, 2)):
             experts(m, g)()
         empty_last = [experts(2, g) for g in range(3)]
 
-        shared = work.tile([P, M, T], F32, name="shared")
+        shared = work.tile([P, M - 1, T], F32, name="shared")
 
         def shared_expert(dst, m, lo, hi):
             for a in range(PASSES):
                 matmul(dst, E, a, m, tok_codes[:, a * T + lo : a * T + hi], tok_scales[:, a * T + lo : a * T + hi])
 
-        def shared_head(m):
-            bank = new_bank()
+        def shared_head(m, bank):
             shared_expert(bank[:], m, 0, BANK)
-            nc.scalar.copy(out=shared[:, m, :BANK], in_=bank[:])
+            return bank
 
-        shared_head(0)
-        tail = new_bank()
+        nc.scalar.copy(out=shared[:, 0, :BANK], in_=shared_head(0, new_bank())[:])
+        tail = psum.tile([P, BANK], F32, name="tail")
         for m in range(M):
             shared_expert(tail[:, m * P : (m + 1) * P], m, BANK, T)
-        nc.scalar.copy(out=shared[:, :, BANK:], in_=tail[:, : M * P].rearrange("p (m t) -> p m t", m=M))
+        nc.scalar.copy(out=shared[:, :, BANK:], in_=tail[:, : (M - 1) * P].rearrange("p (m t) -> p m t", m=M - 1))
         for empty in empty_last:
             empty()
-        shared_head(1)
-        shared_head(2)
+        nc.scalar.copy(out=shared[:, 1, :BANK], in_=shared_head(1, new_bank())[:])
+        head = shared_head(2, psum.tile([P, BANK], F32, name="head"))
 
         first = [work.tile([P, T], F32, name=f"first{m}") for m in range(M)]
 
@@ -238,7 +236,7 @@ def tile_moe_shr_lin_none_kernel(tc, xT, w_words, w_scales, gate, offs, pos1, po
             nc.scalar.copy(out=res[:], in_=bank[:, : hi - lo])
             nc.sync.dma_start(out[m * P : (m + 1) * P, lo:hi], res[:])
 
-        parts = [(0, 0, 384), (0, 384, T), (1, 0, 384), (1, 384, T), (2, 0, 256)]
+        parts = [(0, 0, 384), (0, 384, T), (1, 0, 384), (1, 384, T)]
         waiting = None
         for m, lo, hi in parts:
             if lo == 0:
@@ -249,11 +247,21 @@ def tile_moe_shr_lin_none_kernel(tc, xT, w_words, w_scales, gate, offs, pos1, po
             waiting = (m, lo, hi, turned)
         turn_back(*waiting)
 
-        partial = work.tile([P, T - 256], F32, name="partial")
-        nc.vector.tensor_tensor(partial[:], first[2][:, 256:], shared[:, 2, 256:], ADD)
-        ends = ((256, 512), (512, T))
-        seconds = [pick2(2, lo, hi) for lo, hi in ends]
-        for (lo, hi), second in zip(ends, seconds):
+        pick1(2)
+        ends = ((0, 320), (320, BANK), (BANK, T))
+        seconds = [pick2(2, *ends[0])]
+        partial = work.tile([P, T], F32, name="partial")
+        nc.vector.tensor_tensor(partial[:, :BANK], head[:], first[2][:, :BANK], ADD)
+        nc.vector.tensor_tensor(partial[:, BANK:], tail[:, 2 * P : 3 * P], first[2][:, BANK:], ADD)
+
+        def finish(i):
+            lo, hi = ends[i]
             res = work.tile([P, hi - lo], F32, name=f"res2_{lo}")
-            nc.vector.tensor_tensor(res[:], partial[:, lo - 256 : hi - 256], second[:], ADD)
+            nc.vector.tensor_tensor(res[:], partial[:, lo:hi], seconds[i][:], ADD)
             nc.sync.dma_start(out[2 * P :, lo:hi], res[:])
+
+        seconds.append(pick2(2, *ends[1]))
+        finish(0)
+        seconds.append(pick2(2, *ends[2]))
+        finish(1)
+        finish(2)

@@ -24,6 +24,7 @@ PASSES = 2
 M = N // P
 BANK = 512
 GROUPS = ((0, 4), (4, 8), (8, 10))
+SCALAR_EXTRA = 128
 
 
 def tile_moe_shr_lin_none_kernel(tc, xT, w_words, w_scales, gate, offs, pos1, pos2, out):
@@ -56,16 +57,21 @@ def tile_moe_shr_lin_none_kernel(tc, xT, w_words, w_scales, gate, offs, pos1, po
 
         w_view = w_words.rearrange("e a p b -> p (e a) b").bitcast(I32)
         ww = {}
-        for e0, e1 in ((0, 4), (4, 8), (8, 11)):
+
+        def load_w(e0, e1):
             wt = work.tile([P, (e1 - e0) * PASSES, 2 * N], U8, name=f"ww{e0}", align_bytes=64)
             nc.sync.dma_start(wt[:].bitcast(I32), w_view[:, PASSES * e0 : PASSES * e1, :])
             for e in range(e0, e1):
                 ww[e] = wt[:, PASSES * (e - e0) : PASSES * (e - e0 + 1), :]
-        nc.sync.dma_start(pos1_t[:], pos1)
-        nc.sync.dma_start(pos2_t[:], pos2)
+
         gates = [work.tile([P, T], F32, name=f"gate{g}") for g in range(2)]
-        for g in range(2):
-            nc.sync.dma_start(gates[g][:], gate[g, :P, :])
+        for e0, e1 in GROUPS:
+            load_w(e0, e1)
+        nc.sync.dma_start(pos1_t[:], pos1)
+        nc.sync.dma_start(gates[0][:], gate[0, :P, :])
+        load_w(E, E + 1)
+        nc.sync.dma_start(pos2_t[:], pos2)
+        nc.sync.dma_start(gates[1][:], gate[1, :P, :])
 
         ident = work.tile([P, P], F32, name="ident")
         make_identity(nc, ident[:])
@@ -73,14 +79,14 @@ def tile_moe_shr_lin_none_kernel(tc, xT, w_words, w_scales, gate, offs, pos1, po
         pairs = work.tile([P, 2 * PASSES * T * 2], BF16, name="pairs", align_bytes=64)
         pair_words = pairs[:].bitcast(U32)
         block = {(1, 1): 0, (1, 0): 1, (0, 1): 2, (0, 0): 3}
-        last_rows = [work.tile([P, T], BF16, name=f"last_row{d}", tag=("slots02", "slots00")[d], align_bytes=64) for d in range(2)]
+        last_rows = [work.tile([P, T], BF16, name=f"last_row{d}", tag=("slots01", "slots00")[d], align_bytes=64) for d in range(2)]
         toks = work.tile([P, PASSES * T * 4], BF16, name="toks", align_bytes=64)
         tok_scales = work.tile([P, PASSES * T], U8, name="tok_scales", align_bytes=64)
 
         width = [(e1 - e0) * C for e0, e1 in GROUPS]
         cells = [(a, g) for a in range(PASSES) for g in range(len(GROUPS))]
-        planes = {(a, g): work.tile([P, 2, width[g]], U32, name=f"planes{a}{g}", align_bytes=64) for a, g in cells}
-        slots = {(a, g): work.tile([P, width[g] * 4], BF16, name=f"slots{a}{g}", tag=f"slots{a}{g}", align_bytes=64) for a, g in cells if (a, g) not in ((0, 0), (0, 2))}
+        planes = {(a, g): work.tile([P, 2, width[g]], U32, name=f"planes{a}{g}", tag=f"planes{a}{g}", align_bytes=64) for a, g in cells if (a, g) != (1, 2)}
+        slots = {(a, g): work.tile([P, width[g] * 4], BF16, name=f"slots{a}{g}", tag=f"slots{a}{g}", align_bytes=64) for a, g in cells if (a, g) not in ((0, 0), (0, 1))}
         codes = {(1, g): work.tile([P, width[g]], U32, name=f"codes1{g}", align_bytes=64)[:] for g in range(len(GROUPS))}
         scales = {(a, g): work.tile([P, width[g]], U8, name=f"scales{a}{g}", align_bytes=64) for a, g in cells}
 
@@ -92,22 +98,21 @@ def tile_moe_shr_lin_none_kernel(tc, xT, w_words, w_scales, gate, offs, pos1, po
         def copy_on_gpsimd(out, in_):
             nc.gpsimd.tensor_scalar(out, in_, 1.0, 0.0, MULT, ADD)
 
-        def gather(a, u, g):
+        def gather(a, u, g, count):
             start = block[a, u] * T
             lo = GROUPS[g][0] * C
             if (a, u) == (0, 0):
                 window, piece = pair_words[:, start : start + T], 256
             else:
-                window, piece = pair_words[:, start : start + 2 * T], width[g]
-            for s in range(0, width[g], piece):
+                window, piece = pair_words[:, start : start + 2 * T], count
+            for s in range(0, count, piece):
                 nc.vector.tensor_copy(planes[a, g][:, u, s : s + piece], window.indirect(offs_t[:, (lo + s) // 16 : (lo + s + piece) // 16]))
 
-        def gather_on_scalar(g):
+        def gather_on_scalar(g, s0, s1):
             lo = GROUPS[g][0] * C
             dst = planes[0, g][:, 1, :].bitcast(BF16).rearrange("p (s d) -> p s d", d=2)
-            for s in range(0, width[g], 256):
-                for d in range(2):
-                    nc.scalar.activation(dst[:, s : s + 256, d], last_rows[d][:].indirect(offs_t[:, (lo + s) // 16 : (lo + s + 256) // 16]), COPY)
+            for d in range(2):
+                nc.scalar.activation(dst[:, s0:s1, d], last_rows[d][:].indirect(offs_t[:, (lo + s0) // 16 : (lo + s1) // 16]), COPY)
 
         def weave(copy, dtype, a, g):
             src = planes[a, g][:].bitcast(dtype).rearrange("p u s -> p s u")
@@ -137,13 +142,13 @@ def tile_moe_shr_lin_none_kernel(tc, xT, w_words, w_scales, gate, offs, pos1, po
                 stop=(a == PASSES - 1),
             )
 
-        def new_bank():
-            return psum.tile([P, BANK], F32, name="bank", bufs=6)
+        def new_bank(i):
+            return psum.tile([P, BANK], F32, name=f"bank{i}")
 
         y = [work.tile([P, S], F32, name=f"y{m}") for m in range(M)]
 
         def experts(m, g):
-            bank = new_bank()
+            bank = new_bank(((0, 1, 2), (5, 1, 0), (2, 5, 0))[m][g])
             e0, e1 = GROUPS[g]
             for e in range(e0, e1):
                 cols = slice((e - e0) * C, (e - e0 + 1) * C)
@@ -158,33 +163,43 @@ def tile_moe_shr_lin_none_kernel(tc, xT, w_words, w_scales, gate, offs, pos1, po
             copy_on_gpsimd(last_rows[d][:], raw[0, 1][:, d, :])
         for u in range(2):
             cast(copy_on_gpsimd, 1, u, raw[1, u], 0, T)
-        codes0 = work.tile([P, S], U32, name="codes0", tag="raw11_0", align_bytes=64)
-        for g, (e0, e1) in enumerate(GROUPS):
-            codes[0, g] = codes0[:, e0 * C : e1 * C]
+        codes0 = work.tile([P, 2 * BANK], U32, name="codes0", tag="raw11_0", align_bytes=64)
+        for g in range(2):
+            codes[0, g] = codes0[:, g * BANK : (g + 1) * BANK]
         for g in range(3):
-            gather(0, 0, g)
-        gather(0, 1, 0)
-        gather(0, 1, 2)
-        gather_on_scalar(1)
-        for g in (0, 2):
+            gather(0, 0, g, width[g])
+        gather(0, 1, 0, width[0])
+        gather(0, 1, 1, width[1] - SCALAR_EXTRA)
+        gather_on_scalar(2, 0, width[2])
+        gather_on_scalar(1, width[1] - SCALAR_EXTRA, width[1])
+        for g in (0, 1):
             slots[0, g] = work.tile([P, width[g] * 4], BF16, name=f"slots0{g}", tag=f"slots0{g}", align_bytes=64)
-        for g in (0, 2, 1):
+        weave(nc.scalar.copy, U32, 0, 2)
+        weave_toks(0)
+        for g in range(2):
             weave(nc.scalar.copy, U32, 0, g)
         for u in range(2):
-            for g in range(3):
-                gather(1, u, g)
-        weave_toks(0)
-        for g in range(3):
+            for g in range(2):
+                gather(1, u, g, width[g])
+        for g in range(2):
             weave(nc.scalar.copy, U32, 1, g)
         weave_toks(1)
-        for g in range(3):
-            for a in range(PASSES):
-                quantize_slots(a, g)
-        tok_codes = work.tile([P, PASSES * T], U32, name="tok_codes", align_bytes=64)
+        quantize_slots(0, 0)
+        quantize_slots(1, 0)
+        quantize_slots(0, 1)
+        planes[1, 2] = work.tile([P, 2, width[2]], U32, name="planes12", tag="slots10", align_bytes=64)
+        for u in range(2):
+            gather(1, u, 2, width[2])
+        weave(nc.scalar.copy, U32, 1, 2)
+        quantize_slots(1, 1)
+        codes[0, 2] = work.tile([P, width[2]], U32, name="codes02", tag="planes11", align_bytes=64)[:]
+        quantize_slots(0, 2)
+        quantize_slots(1, 2)
+        tok_codes = work.tile([P, PASSES * T], U32, name="tok_codes", tag="slots12", align_bytes=64)
         quantize_toks(tok_codes, 0, 1024)
         quantize_toks(tok_codes, 1024, PASSES * T)
 
-        for m, g in ((0, 0), (0, 1), (0, 2), (1, 0), (1, 1), (1, 2)):
+        for m, g in ((0, 0), (0, 1), (0, 2), (1, 0), (1, 2), (1, 1)):
             experts(m, g)()
         empty_last = [experts(2, g) for g in range(3)]
 
@@ -198,14 +213,14 @@ def tile_moe_shr_lin_none_kernel(tc, xT, w_words, w_scales, gate, offs, pos1, po
             shared_expert(bank[:], m, 0, BANK)
             return bank
 
-        nc.scalar.copy(out=shared[:, 0, :BANK], in_=shared_head(0, new_bank())[:])
+        nc.scalar.copy(out=shared[:, 0, :BANK], in_=shared_head(0, new_bank(3))[:])
         tail = psum.tile([P, BANK], F32, name="tail")
         for m in range(M):
             shared_expert(tail[:, m * P : (m + 1) * P], m, BANK, T)
         nc.scalar.copy(out=shared[:, :, BANK:], in_=tail[:, : (M - 1) * P].rearrange("p (m t) -> p m t", m=M - 1))
         for empty in empty_last:
             empty()
-        nc.scalar.copy(out=shared[:, 1, :BANK], in_=shared_head(1, new_bank())[:])
+        nc.scalar.copy(out=shared[:, 1, :BANK], in_=shared_head(1, new_bank(4))[:])
         head = shared_head(2, psum.tile([P, BANK], F32, name="head"))
 
         first = [work.tile([P, T], F32, name=f"first{m}") for m in range(M)]
@@ -218,8 +233,10 @@ def tile_moe_shr_lin_none_kernel(tc, xT, w_words, w_scales, gate, offs, pos1, po
             nc.vector.tensor_tensor(second[:], y[m][:].indirect(pos2_t[:, lo // 16 : hi // 16]), gates[1][:, lo:hi], MULT)
             return second
 
+        free = [1, 3, 4, 2, 5, 0, 1, 3]
+
         def sum_turned(m, lo, hi, second):
-            bank = new_bank()
+            bank = new_bank(free.pop(0))
             for t in range(lo, hi, P):
                 terms = (shared[:, m, t : t + P], first[m][:, t : t + P], second[:, t - lo : t - lo + P])
                 for i, term in enumerate(terms):
@@ -229,7 +246,7 @@ def tile_moe_shr_lin_none_kernel(tc, xT, w_words, w_scales, gate, offs, pos1, po
             return turned
 
         def turn_back(m, lo, hi, turned):
-            bank = new_bank()
+            bank = new_bank(free.pop(0))
             for t in range(0, hi - lo, P):
                 nc.tensor.transpose(bank[:, t : t + P], turned[:, t : t + P], ident[:])
             res = work.tile([P, hi - lo], F32, name=f"res{m}_{lo}")

@@ -24,7 +24,8 @@ PASSES = 2
 M = N // P
 BANK = 512
 GROUPS = ((0, 4), (4, 8), (8, 10))
-SCALAR_EXTRA = 128
+HALVES = ((0, 384), (384, T))
+SCALAR_EXTRA = 256
 
 
 def tile_moe_shr_lin_none_kernel(tc, xT, w_words, w_scales, gate, offs, pos1, pos2, out):
@@ -64,14 +65,13 @@ def tile_moe_shr_lin_none_kernel(tc, xT, w_words, w_scales, gate, offs, pos1, po
             for e in range(e0, e1):
                 ww[e] = wt[:, PASSES * (e - e0) : PASSES * (e - e0 + 1), :]
 
-        gates = [work.tile([P, T], F32, name=f"gate{g}") for g in range(2)]
+        gates = work.tile([P, 2, T], F32, name="gates")
         for e0, e1 in GROUPS:
             load_w(e0, e1)
-        nc.sync.dma_start(pos1_t[:], pos1)
-        nc.sync.dma_start(gates[0][:], gate[0, :P, :])
         load_w(E, E + 1)
         nc.sync.dma_start(pos2_t[:], pos2)
-        nc.sync.dma_start(gates[1][:], gate[1, :P, :])
+        nc.sync.dma_start(pos1_t[:], pos1)
+        nc.sync.dma_start(gates[:], gate[:, :P, :].rearrange("g p t -> p g t"))
 
         ident = work.tile([P, P], F32, name="ident")
         make_identity(nc, ident[:])
@@ -80,7 +80,6 @@ def tile_moe_shr_lin_none_kernel(tc, xT, w_words, w_scales, gate, offs, pos1, po
         pair_words = pairs[:].bitcast(U32)
         block = {(1, 1): 0, (1, 0): 1, (0, 1): 2, (0, 0): 3}
         last_rows = [work.tile([P, T], BF16, name=f"last_row{d}", tag=("slots01", "slots00")[d], align_bytes=64) for d in range(2)]
-        toks = work.tile([P, PASSES * T * 4], BF16, name="toks", align_bytes=64)
         tok_scales = work.tile([P, PASSES * T], U8, name="tok_scales", align_bytes=64)
 
         width = [(e1 - e0) * C for e0, e1 in GROUPS]
@@ -104,7 +103,7 @@ def tile_moe_shr_lin_none_kernel(tc, xT, w_words, w_scales, gate, offs, pos1, po
             if (a, u) == (0, 0):
                 window, piece = pair_words[:, start : start + T], 256
             else:
-                window, piece = pair_words[:, start : start + 2 * T], count
+                window, piece = pair_words[:, start : start + (2 * T if count > 480 else T)], count
             for s in range(0, count, piece):
                 nc.vector.tensor_copy(planes[a, g][:, u, s : s + piece], window.indirect(offs_t[:, (lo + s) // 16 : (lo + s + piece) // 16]))
 
@@ -122,10 +121,10 @@ def tile_moe_shr_lin_none_kernel(tc, xT, w_words, w_scales, gate, offs, pos1, po
         def quantize_slots(a, g):
             nc.vector.quantize_mx(out=codes[a, g].bitcast(FP8X4), scales=scales[a, g][:], in_=slots[a, g][:])
 
-        def quantize_toks(tok_codes, lo, hi):
+        def quantize_toks(tok_codes, toks, lo, hi):
             nc.vector.quantize_mx(out=tok_codes[:, lo:hi].bitcast(FP8X4), scales=tok_scales[:, lo:hi], in_=toks[:, 4 * lo : 4 * hi])
 
-        def weave_toks(a):
+        def weave_toks(toks, a):
             base = block[a, 1] * T
             src = pair_words[:, base : base + 2 * T].rearrange("p (u t) -> p t u", u=2)
             dst = toks[:, 4 * a * T : 4 * (a + 1) * T].bitcast(U32).rearrange("p (t u) -> p t u", u=2)
@@ -147,14 +146,13 @@ def tile_moe_shr_lin_none_kernel(tc, xT, w_words, w_scales, gate, offs, pos1, po
 
         y = [work.tile([P, S], F32, name=f"y{m}") for m in range(M)]
 
-        def experts(m, g):
-            bank = new_bank(((0, 1, 2), (5, 1, 0), (2, 5, 0))[m][g])
+        def experts(m, g, bank):
             e0, e1 = GROUPS[g]
             for e in range(e0, e1):
                 cols = slice((e - e0) * C, (e - e0 + 1) * C)
                 for a in range(PASSES):
                     matmul(bank[:, cols], e, a, m, codes[a, g][:, cols], scales[a, g][:, cols])
-            return lambda: nc.scalar.copy(out=y[m][:, e0 * C : e1 * C], in_=bank[:, : width[g]])
+            return bank
 
         for t0, t1, src in raw_first:
             cast(nc.vector.tensor_copy, 0, 0, src, t0, t1)
@@ -163,9 +161,9 @@ def tile_moe_shr_lin_none_kernel(tc, xT, w_words, w_scales, gate, offs, pos1, po
             copy_on_gpsimd(last_rows[d][:], raw[0, 1][:, d, :])
         for u in range(2):
             cast(copy_on_gpsimd, 1, u, raw[1, u], 0, T)
-        codes0 = work.tile([P, 2 * BANK], U32, name="codes0", tag="raw11_0", align_bytes=64)
-        for g in range(2):
-            codes[0, g] = codes0[:, g * BANK : (g + 1) * BANK]
+        codes0 = work.tile([P, S], U32, name="codes0", tag="raw11_0", align_bytes=64)
+        for g, (e0, e1) in enumerate(GROUPS):
+            codes[0, g] = codes0[:, e0 * C : e1 * C]
         for g in range(3):
             gather(0, 0, g, width[g])
         gather(0, 1, 0, width[0])
@@ -175,33 +173,46 @@ def tile_moe_shr_lin_none_kernel(tc, xT, w_words, w_scales, gate, offs, pos1, po
         for g in (0, 1):
             slots[0, g] = work.tile([P, width[g] * 4], BF16, name=f"slots0{g}", tag=f"slots0{g}", align_bytes=64)
         weave(nc.scalar.copy, U32, 0, 2)
-        weave_toks(0)
         for g in range(2):
             weave(nc.scalar.copy, U32, 0, g)
-        for u in range(2):
-            for g in range(2):
-                gather(1, u, g, width[g])
+        toks = work.tile([P, PASSES * T * 4], BF16, name="toks", tag="planes01", align_bytes=64)
+        weave_toks(toks, 0)
+        for g in range(2):
+            gather(1, 0, g, width[g])
+        gather(1, 1, 0, width[0])
+        quantize_slots(0, 0)
+        gather(1, 1, 1, width[1])
         for g in range(2):
             weave(nc.scalar.copy, U32, 1, g)
-        weave_toks(1)
-        quantize_slots(0, 0)
-        quantize_slots(1, 0)
+        weave_toks(toks, 1)
         quantize_slots(0, 1)
-        planes[1, 2] = work.tile([P, 2, width[2]], U32, name="planes12", tag="slots10", align_bytes=64)
+        quantize_slots(0, 2)
+        quantize_slots(1, 0)
+        planes[1, 2] = work.tile([P, 2, width[2]], U32, name="planes12", tag="planes10", align_bytes=64)
         for u in range(2):
             gather(1, u, 2, width[2])
-        weave(nc.scalar.copy, U32, 1, 2)
         quantize_slots(1, 1)
-        codes[0, 2] = work.tile([P, width[2]], U32, name="codes02", tag="planes11", align_bytes=64)[:]
-        quantize_slots(0, 2)
+        weave(nc.vector.tensor_copy, I32, 1, 2)
+        tok_codes = work.tile([P, PASSES * T], U32, name="tok_codes", tag="slots11", align_bytes=64)
+        quantize_toks(tok_codes, toks, 1024, PASSES * T)
         quantize_slots(1, 2)
-        tok_codes = work.tile([P, PASSES * T], U32, name="tok_codes", tag="slots12", align_bytes=64)
-        quantize_toks(tok_codes, 0, 1024)
-        quantize_toks(tok_codes, 1024, PASSES * T)
+        quantize_toks(tok_codes, toks, 0, 1024)
 
-        for m, g in ((0, 0), (0, 1), (0, 2), (1, 0), (1, 2), (1, 1)):
-            experts(m, g)()
-        empty_last = [experts(2, g) for g in range(3)]
+        def empty(m, g, src):
+            e0, e1 = GROUPS[g]
+            nc.scalar.copy(out=y[m][:, e0 * C : e1 * C], in_=src)
+
+        sums = {(m, 0): experts(m, 0, new_bank(m)[:]) for m in range(3)}
+        for g in (1, 2):
+            sums[0, g] = experts(0, g, new_bank(g * M)[:, : width[g]])
+        for g in range(3):
+            empty(0, g, sums[0, g])
+        sums[1, 1] = experts(1, 1, new_bank(M + 1)[:])
+        last = new_bank(7)
+        for m in (1, 2):
+            sums[m, 2] = experts(m, 2, last[:, (m - 1) * width[2] : m * width[2]])
+        for g in range(3):
+            empty(1, g, sums[1, g])
 
         shared = work.tile([P, M - 1, T], F32, name="shared")
 
@@ -213,27 +224,26 @@ def tile_moe_shr_lin_none_kernel(tc, xT, w_words, w_scales, gate, offs, pos1, po
             shared_expert(bank[:], m, 0, BANK)
             return bank
 
-        nc.scalar.copy(out=shared[:, 0, :BANK], in_=shared_head(0, new_bank(3))[:])
-        tail = psum.tile([P, BANK], F32, name="tail")
+        nc.scalar.copy(out=shared[:, 0, :BANK], in_=shared_head(0, new_bank(0))[:])
+        tail = new_bank(3)
         for m in range(M):
             shared_expert(tail[:, m * P : (m + 1) * P], m, BANK, T)
         nc.scalar.copy(out=shared[:, :, BANK:], in_=tail[:, : (M - 1) * P].rearrange("p (m t) -> p m t", m=M - 1))
-        for empty in empty_last:
-            empty()
-        nc.scalar.copy(out=shared[:, 1, :BANK], in_=shared_head(1, new_bank(4))[:])
-        head = shared_head(2, psum.tile([P, BANK], F32, name="head"))
+        sums[2, 1] = experts(2, 1, new_bank(M + 2)[:])
+        for g in range(3):
+            empty(2, g, sums[2, g])
 
         first = [work.tile([P, T], F32, name=f"first{m}") for m in range(M)]
 
         def pick1(m):
-            nc.vector.tensor_tensor(first[m][:], y[m][:].indirect(pos1_t[:]), gates[0][:], MULT)
+            nc.vector.tensor_tensor(first[m][:], y[m][:].indirect(pos1_t[:]), gates[:, 0, :], MULT)
 
         def pick2(m, lo, hi):
             second = work.tile([P, hi - lo], F32, name=f"second{m}_{lo}")
-            nc.vector.tensor_tensor(second[:], y[m][:].indirect(pos2_t[:, lo // 16 : hi // 16]), gates[1][:, lo:hi], MULT)
+            nc.vector.tensor_tensor(second[:], y[m][:].indirect(pos2_t[:, lo // 16 : hi // 16]), gates[:, 1, lo:hi], MULT)
             return second
 
-        free = [1, 3, 4, 2, 5, 0, 1, 3]
+        free = [6, 0, 7, 2, 7, 2, 6, 0]
 
         def sum_turned(m, lo, hi, second):
             bank = new_bank(free.pop(0))
@@ -251,34 +261,33 @@ def tile_moe_shr_lin_none_kernel(tc, xT, w_words, w_scales, gate, offs, pos1, po
                 nc.tensor.transpose(bank[:, t : t + P], turned[:, t : t + P], ident[:])
             res = work.tile([P, hi - lo], F32, name=f"res{m}_{lo}")
             nc.scalar.copy(out=res[:], in_=bank[:, : hi - lo])
-            nc.sync.dma_start(out[m * P : (m + 1) * P, lo:hi], res[:])
+            nc.scalar.dma_start(out[m * P : (m + 1) * P, lo:hi], res[:])
 
-        parts = [(0, 0, 384), (0, 384, T), (1, 0, 384), (1, 384, T)]
-        waiting = None
-        for m, lo, hi in parts:
-            if lo == 0:
-                pick1(m)
-            turned = sum_turned(m, lo, hi, pick2(m, lo, hi))
-            if waiting is not None:
-                turn_back(*waiting)
-            waiting = (m, lo, hi, turned)
-        turn_back(*waiting)
+        pick1(0)
+        turned = [sum_turned(0, lo, hi, pick2(0, lo, hi)) for lo, hi in HALVES]
+        nc.scalar.copy(out=shared[:, 1, :BANK], in_=shared_head(1, new_bank(1))[:])
+        for (lo, hi), part in zip(HALVES, turned):
+            turn_back(0, lo, hi, part)
+        pick1(1)
+        turned = [sum_turned(1, lo, hi, pick2(1, lo, hi)) for lo, hi in HALVES]
+        head = shared_head(2, new_bank(4))
+        for (lo, hi), part in zip(HALVES, turned):
+            turn_back(1, lo, hi, part)
 
         pick1(2)
-        ends = ((0, 320), (320, BANK), (BANK, T))
-        seconds = [pick2(2, *ends[0])]
         partial = work.tile([P, T], F32, name="partial")
-        nc.vector.tensor_tensor(partial[:, :BANK], head[:], first[2][:, :BANK], ADD)
-        nc.vector.tensor_tensor(partial[:, BANK:], tail[:, 2 * P : 3 * P], first[2][:, BANK:], ADD)
 
-        def finish(i):
-            lo, hi = ends[i]
+        def finish(lo, hi, second):
             res = work.tile([P, hi - lo], F32, name=f"res2_{lo}")
-            nc.vector.tensor_tensor(res[:], partial[:, lo:hi], seconds[i][:], ADD)
+            nc.vector.tensor_tensor(res[:], partial[:, lo:hi], second[:], ADD)
             nc.sync.dma_start(out[2 * P :, lo:hi], res[:])
 
+        ends = ((BANK, T), (0, 384), (384, BANK))
+        seconds = [pick2(2, *ends[0])]
+        nc.vector.tensor_tensor(partial[:, BANK:], tail[:, 2 * P : 3 * P], first[2][:, BANK:], ADD)
         seconds.append(pick2(2, *ends[1]))
-        finish(0)
+        finish(*ends[0], seconds[0])
+        nc.vector.tensor_tensor(partial[:, :BANK], head[:], first[2][:, :BANK], ADD)
         seconds.append(pick2(2, *ends[2]))
-        finish(1)
-        finish(2)
+        finish(*ends[1], seconds[1])
+        finish(*ends[2], seconds[2])

@@ -25,6 +25,8 @@ M = N // P
 BANK = 512
 GROUPS = ((0, 4), (4, 8), (8, 10))
 HALVES = ((0, 384), (384, T))
+WIDE = 1024
+THIRDS = ((0, 256), (256, BANK), (BANK, T))
 SCALAR_EXTRA = 256
 
 
@@ -85,8 +87,8 @@ def tile_moe_shr_lin_none_kernel(tc, xT, w_words, w_scales, gate, offs, pos1, po
         width = [(e1 - e0) * C for e0, e1 in GROUPS]
         cells = [(a, g) for a in range(PASSES) for g in range(len(GROUPS))]
         planes = {(a, g): work.tile([P, 2, width[g]], U32, name=f"planes{a}{g}", tag=f"planes{a}{g}", align_bytes=64) for a, g in cells if (a, g) != (1, 2)}
-        slots = {(a, g): work.tile([P, width[g] * 4], BF16, name=f"slots{a}{g}", tag=f"slots{a}{g}", align_bytes=64) for a, g in cells if (a, g) not in ((0, 0), (0, 1))}
-        codes = {(1, g): work.tile([P, width[g]], U32, name=f"codes1{g}", align_bytes=64)[:] for g in range(len(GROUPS))}
+        slots = {(a, g): work.tile([P, width[g] * 4], BF16, name=f"slots{a}{g}", tag=f"slots{a}{g}", align_bytes=64) for a, g in cells if (a, g) not in ((0, 0), (0, 1), (1, 2))}
+        codes = {(1, g): work.tile([P, width[g]], U32, name=f"codes1{g}", tag=f"codes1{g}", align_bytes=64)[:] for g in range(len(GROUPS))}
         scales = {(a, g): work.tile([P, width[g]], U8, name=f"scales{a}{g}", align_bytes=64) for a, g in cells}
 
         def cast(copy, a, u, src, t0, t1):
@@ -122,13 +124,12 @@ def tile_moe_shr_lin_none_kernel(tc, xT, w_words, w_scales, gate, offs, pos1, po
             nc.vector.quantize_mx(out=codes[a, g].bitcast(FP8X4), scales=scales[a, g][:], in_=slots[a, g][:])
 
         def quantize_toks(tok_codes, toks, lo, hi):
-            nc.vector.quantize_mx(out=tok_codes[:, lo:hi].bitcast(FP8X4), scales=tok_scales[:, lo:hi], in_=toks[:, 4 * lo : 4 * hi])
+            nc.vector.quantize_mx(out=tok_codes[:, lo:hi].bitcast(FP8X4), scales=tok_scales[:, lo:hi], in_=toks[:])
 
-        def weave_toks(toks, a):
+        def weave_toks(dst, a, t0, t1):
             base = block[a, 1] * T
             src = pair_words[:, base : base + 2 * T].rearrange("p (u t) -> p t u", u=2)
-            dst = toks[:, 4 * a * T : 4 * (a + 1) * T].bitcast(U32).rearrange("p (t u) -> p t u", u=2)
-            nc.scalar.copy(out=dst, in_=src[:, :, ::-1])
+            nc.scalar.copy(out=dst.bitcast(U32).rearrange("p (t u) -> p t u", u=2), in_=src[:, t0:t1, ::-1])
 
         def matmul(dst, e, a, m, rhs, rhs_scale):
             nc.tensor.matmul_mx(
@@ -144,7 +145,6 @@ def tile_moe_shr_lin_none_kernel(tc, xT, w_words, w_scales, gate, offs, pos1, po
         def new_bank(i):
             return psum.tile([P, BANK], F32, name=f"bank{i}")
 
-        y = [work.tile([P, S], F32, name=f"y{m}") for m in range(M)]
 
         def experts(m, g, bank):
             e0, e1 = GROUPS[g]
@@ -161,9 +161,9 @@ def tile_moe_shr_lin_none_kernel(tc, xT, w_words, w_scales, gate, offs, pos1, po
             copy_on_gpsimd(last_rows[d][:], raw[0, 1][:, d, :])
         for u in range(2):
             cast(copy_on_gpsimd, 1, u, raw[1, u], 0, T)
-        codes0 = work.tile([P, S], U32, name="codes0", tag="raw11_0", align_bytes=64)
-        for g, (e0, e1) in enumerate(GROUPS):
-            codes[0, g] = codes0[:, e0 * C : e1 * C]
+        codes0 = work.tile([P, 2 * BANK], U32, name="codes0", tag="raw11_0", align_bytes=64)
+        for g in range(2):
+            codes[0, g] = codes0[:, g * BANK : (g + 1) * BANK]
         for g in range(3):
             gather(0, 0, g, width[g])
         gather(0, 1, 0, width[0])
@@ -175,39 +175,56 @@ def tile_moe_shr_lin_none_kernel(tc, xT, w_words, w_scales, gate, offs, pos1, po
         weave(nc.scalar.copy, U32, 0, 2)
         for g in range(2):
             weave(nc.scalar.copy, U32, 0, g)
-        toks = work.tile([P, PASSES * T * 4], BF16, name="toks", tag="planes01", align_bytes=64)
-        weave_toks(toks, 0)
         for g in range(2):
             gather(1, 0, g, width[g])
         gather(1, 1, 0, width[0])
         quantize_slots(0, 0)
+        idle = new_bank(7)
+        for i in range(4):
+            nc.tensor.matmul_mx(
+                out=idle[:],
+                lhsT=ww[0][:, 0, : 2 * P].bitcast(FP4X4),
+                lhsT_scale=scales[0, 0][:, :P],
+                rhs=codes[0, 0].bitcast(FP8X4),
+                rhs_scale=scales[0, 0][:],
+                start=True,
+                stop=True,
+            )
         gather(1, 1, 1, width[1])
-        for g in range(2):
-            weave(nc.scalar.copy, U32, 1, g)
-        weave_toks(toks, 1)
+        weave(nc.scalar.copy, U32, 1, 0)
+        toks = work.tile([P, WIDE * 4], BF16, name="toks", tag="slots00", align_bytes=64)
+        weave_toks(toks[:, : 4 * T], 0, 0, T)
+        weave(nc.scalar.copy, U32, 1, 1)
+        weave_toks(toks[:, 4 * T :], 1, 0, WIDE - T)
         quantize_slots(0, 1)
-        quantize_slots(0, 2)
         quantize_slots(1, 0)
+        toks_end = work.tile([P, (PASSES * T - WIDE) * 4], BF16, name="toks_end", tag="slots10", align_bytes=64)
+        weave_toks(toks_end[:], 1, WIDE - T, T)
         planes[1, 2] = work.tile([P, 2, width[2]], U32, name="planes12", tag="planes10", align_bytes=64)
         for u in range(2):
             gather(1, u, 2, width[2])
         quantize_slots(1, 1)
+        slots[1, 2] = work.tile([P, width[2] * 4], BF16, name="slots12", tag="planes11", align_bytes=64)
         weave(nc.vector.tensor_copy, I32, 1, 2)
-        tok_codes = work.tile([P, PASSES * T], U32, name="tok_codes", tag="slots11", align_bytes=64)
-        quantize_toks(tok_codes, toks, 1024, PASSES * T)
+        codes[0, 2] = work.tile([P, width[2]], U32, name="codes02", tag="slots11", align_bytes=64)[:]
+        quantize_slots(0, 2)
         quantize_slots(1, 2)
-        quantize_toks(tok_codes, toks, 0, 1024)
+        tok_codes = work.tile([P, PASSES * T], U32, name="tok_codes", tag="slots02", align_bytes=64)
+        quantize_toks(tok_codes, toks, 0, WIDE)
+        quantize_toks(tok_codes, toks_end, WIDE, PASSES * T)
+        y = [work.tile([P, S], F32, name=f"y{m}", align_bytes=64) for m in range(M - 1)]
 
         def empty(m, g, src):
             e0, e1 = GROUPS[g]
             nc.scalar.copy(out=y[m][:, e0 * C : e1 * C], in_=src)
 
-        sums = {(m, 0): experts(m, 0, new_bank(m)[:]) for m in range(3)}
+        sums = {(m, 0): experts(m, 0, new_bank(m)[:]) for m in range(1)}
         for g in (1, 2):
             sums[0, g] = experts(0, g, new_bank(g * M)[:, : width[g]])
         for g in range(3):
             empty(0, g, sums[0, g])
-        sums[1, 1] = experts(1, 1, new_bank(M + 1)[:])
+        for g in range(2):
+            sums[1, g] = experts(1, g, new_bank(g * M + 1)[:])
         last = new_bank(7)
         for m in (1, 2):
             sums[m, 2] = experts(m, 2, last[:, (m - 1) * width[2] : m * width[2]])
@@ -224,12 +241,15 @@ def tile_moe_shr_lin_none_kernel(tc, xT, w_words, w_scales, gate, offs, pos1, po
             shared_expert(bank[:], m, 0, BANK)
             return bank
 
-        nc.scalar.copy(out=shared[:, 0, :BANK], in_=shared_head(0, new_bank(0))[:])
+        nc.scalar.copy(out=shared[:, 0, :BANK], in_=shared_head(0, new_bank(2))[:])
         tail = new_bank(3)
         for m in range(M):
             shared_expert(tail[:, m * P : (m + 1) * P], m, BANK, T)
         nc.scalar.copy(out=shared[:, :, BANK:], in_=tail[:, : (M - 1) * P].rearrange("p (m t) -> p m t", m=M - 1))
+        sums[2, 0] = experts(2, 0, new_bank(0)[:])
         sums[2, 1] = experts(2, 1, new_bank(M + 2)[:])
+        second_head = shared_head(1, new_bank(1))
+        y.append(work.tile([P, S], F32, name="y2", tag="codes11", align_bytes=64))
         for g in range(3):
             empty(2, g, sums[2, g])
 
@@ -243,7 +263,7 @@ def tile_moe_shr_lin_none_kernel(tc, xT, w_words, w_scales, gate, offs, pos1, po
             nc.vector.tensor_tensor(second[:], y[m][:].indirect(pos2_t[:, lo // 16 : hi // 16]), gates[:, 1, lo:hi], MULT)
             return second
 
-        free = [6, 0, 7, 2, 7, 2, 6, 0]
+        free = [6, 2, 7, 0, 2, 7, 0, 6, 5, 2]
 
         def sum_turned(m, lo, hi, second):
             bank = new_bank(free.pop(0))
@@ -265,13 +285,13 @@ def tile_moe_shr_lin_none_kernel(tc, xT, w_words, w_scales, gate, offs, pos1, po
 
         pick1(0)
         turned = [sum_turned(0, lo, hi, pick2(0, lo, hi)) for lo, hi in HALVES]
-        nc.scalar.copy(out=shared[:, 1, :BANK], in_=shared_head(1, new_bank(1))[:])
+        nc.scalar.copy(out=shared[:, 1, :BANK], in_=second_head[:])
         for (lo, hi), part in zip(HALVES, turned):
             turn_back(0, lo, hi, part)
-        pick1(1)
-        turned = [sum_turned(1, lo, hi, pick2(1, lo, hi)) for lo, hi in HALVES]
         head = shared_head(2, new_bank(4))
-        for (lo, hi), part in zip(HALVES, turned):
+        pick1(1)
+        turned = [sum_turned(1, lo, hi, pick2(1, lo, hi)) for lo, hi in THIRDS]
+        for (lo, hi), part in zip(THIRDS, turned):
             turn_back(1, lo, hi, part)
 
         pick1(2)

@@ -20,14 +20,18 @@ ADD = mybir.AluOpType.add
 COPY = mybir.ActivationFunctionType.Copy
 
 P = 128
-PASSES = 2
+PASSES = K // 512
 M = N // P
 BANK = 512
 GROUPS = ((0, 4), (4, 8), (8, 10))
-HALVES = ((0, 384), (384, T))
+FIRST_LOADS = ((0, 384), (384, T))
+FIRST_PIECE = 256
+NARROW = 3 * T // 4
+SCALAR_EXTRA = 128
 WIDE = 1024
+HALVES = ((0, 256), (256, T))
 THIRDS = ((0, 256), (256, BANK), (BANK, T))
-SCALAR_EXTRA = 256
+WARM_UPS = 4
 
 
 def tile_moe_shr_lin_none_kernel(tc, xT, w_words, w_scales, gate, offs, pos1, pos2, out):
@@ -44,13 +48,13 @@ def tile_moe_shr_lin_none_kernel(tc, xT, w_words, w_scales, gate, offs, pos1, po
         x_view = xT.rearrange("(a p j) t -> a p j t", a=PASSES, p=P, j=4)
 
         def load_x(a, u, t0, t1):
-            raw = work.tile([P, 2, t1 - t0], F32, name=f"raw{a}{u}_{t0}", tag=f"raw{a}{u}_{t0}", align_bytes=64)
-            nc.sync.dma_start(raw[:], x_view[a][:, 2 * u : 2 * u + 2, t0:t1])
-            return raw
+            rows = work.tile([P, 2, t1 - t0], F32, name=f"raw{a}{u}_{t0}", tag=f"raw{a}{u}_{t0}", align_bytes=64)
+            nc.sync.dma_start(rows[:], x_view[a][:, 2 * u : 2 * u + 2, t0:t1])
+            return rows
 
-        raw_first = [(t0, t1, load_x(0, 0, t0, t1)) for t0, t1 in ((0, 384), (384, T))]
+        raw_first = [load_x(0, 0, t0, t1) for t0, t1 in FIRST_LOADS]
         nc.sync.dma_start(offs_t[:], offs)
-        raw = {au: load_x(au[0], au[1], 0, T) for au in ((0, 1), (1, 0), (1, 1))}
+        raw = {(a, u): load_x(a, u, 0, T) for a, u in ((0, 1), (1, 0), (1, 1))}
 
         ws = work.tile([P, (E + 1) * PASSES, N], U8, name="ws", align_bytes=64)
         nc.gpsimd.memset(ws[:].rearrange("p e n -> p (e n)").bitcast(I32), 0)
@@ -62,74 +66,79 @@ def tile_moe_shr_lin_none_kernel(tc, xT, w_words, w_scales, gate, offs, pos1, po
         ww = {}
 
         def load_w(e0, e1):
-            wt = work.tile([P, (e1 - e0) * PASSES, 2 * N], U8, name=f"ww{e0}", align_bytes=64)
-            nc.sync.dma_start(wt[:].bitcast(I32), w_view[:, PASSES * e0 : PASSES * e1, :])
+            words = work.tile([P, (e1 - e0) * PASSES, 2 * N], U8, name=f"ww{e0}", align_bytes=64)
+            nc.sync.dma_start(words[:].bitcast(I32), w_view[:, PASSES * e0 : PASSES * e1, :])
             for e in range(e0, e1):
-                ww[e] = wt[:, PASSES * (e - e0) : PASSES * (e - e0 + 1), :]
+                ww[e] = words[:, PASSES * (e - e0) : PASSES * (e - e0 + 1), :]
 
-        gates = work.tile([P, 2, T], F32, name="gates")
+        gates = {t0: work.tile([P, 2, t1 - t0], F32, name=f"gates{t0}") for t0, t1 in HALVES}
         for e0, e1 in GROUPS:
             load_w(e0, e1)
-        load_w(E, E + 1)
         nc.sync.dma_start(pos2_t[:], pos2)
         nc.sync.dma_start(pos1_t[:], pos1)
-        nc.sync.dma_start(gates[:], gate[:, :P, :].rearrange("g p t -> p g t"))
+        for t0, t1 in HALVES:
+            nc.sync.dma_start(gates[t0][:], gate[:, :P, t0:t1].rearrange("g p t -> p g t"))
+        load_w(E, E + 1)
 
         ident = work.tile([P, P], F32, name="ident")
         make_identity(nc, ident[:])
 
         pairs = work.tile([P, 2 * PASSES * T * 2], BF16, name="pairs", align_bytes=64)
         pair_words = pairs[:].bitcast(U32)
-        block = {(1, 1): 0, (1, 0): 1, (0, 1): 2, (0, 0): 3}
-        last_rows = [work.tile([P, T], BF16, name=f"last_row{d}", tag=("slots01", "slots00")[d], align_bytes=64) for d in range(2)]
+        place = {(1, 1): 0, (1, 0): 1, (0, 1): 2, (0, 0): 3}
+        single_rows = [work.tile([P, T], BF16, name=f"single_row{d}", tag=("slots01", "slots00")[d], align_bytes=64) for d in range(2)]
         tok_scales = work.tile([P, PASSES * T], U8, name="tok_scales", align_bytes=64)
 
         width = [(e1 - e0) * C for e0, e1 in GROUPS]
         cells = [(a, g) for a in range(PASSES) for g in range(len(GROUPS))]
-        planes = {(a, g): work.tile([P, 2, width[g]], U32, name=f"planes{a}{g}", tag=f"planes{a}{g}", align_bytes=64) for a, g in cells if (a, g) != (1, 2)}
-        slots = {(a, g): work.tile([P, width[g] * 4], BF16, name=f"slots{a}{g}", tag=f"slots{a}{g}", align_bytes=64) for a, g in cells if (a, g) not in ((0, 0), (0, 1), (1, 2))}
-        codes = {(1, g): work.tile([P, width[g]], U32, name=f"codes1{g}", tag=f"codes1{g}", align_bytes=64)[:] for g in range(len(GROUPS))}
+        planes = {
+            (a, g): work.tile([P, 2, width[g]], U32, name=f"planes{a}{g}", tag=f"planes{a}{g}", align_bytes=64)
+            for a, g in cells
+            if (a, g) != (1, 2)
+        }
+        slots = {
+            (a, g): work.tile([P, width[g] * 4], BF16, name=f"slots{a}{g}", tag=f"slots{a}{g}", align_bytes=64)
+            for a, g in ((0, 2), (1, 0), (1, 1))
+        }
+        codes = {
+            (1, g): work.tile([P, width[g]], U32, name=f"codes1{g}", tag=f"codes1{g}", align_bytes=64)[:]
+            for g in range(len(GROUPS))
+        }
         scales = {(a, g): work.tile([P, width[g]], U8, name=f"scales{a}{g}", align_bytes=64) for a, g in cells}
 
-        def cast(copy, a, u, src, t0, t1):
-            base = block[a, u] * 2 * T
+        def round_pairs(copy, a, u, rows, t0, t1):
+            base = place[a, u] * 2 * T
             dst = pairs[:, base + 2 * t0 : base + 2 * t1].rearrange("p (t d) -> p t d", d=2)
-            copy(out=dst, in_=src[:].rearrange("p j t -> p t j"))
+            copy(out=dst, in_=rows[:].rearrange("p d t -> p t d"))
 
         def copy_on_gpsimd(out, in_):
             nc.gpsimd.tensor_scalar(out, in_, 1.0, 0.0, MULT, ADD)
 
-        def gather(a, u, g, count):
-            start = block[a, u] * T
+        def gather(a, u, g, s0, s1):
+            start = place[a, u] * T
             lo = GROUPS[g][0] * C
-            if (a, u) == (0, 0):
-                window, piece = pair_words[:, start : start + T], 256
-            else:
-                window, piece = pair_words[:, start : start + (2 * T if count > 480 else T)], count
-            for s in range(0, count, piece):
-                nc.vector.tensor_copy(planes[a, g][:, u, s : s + piece], window.indirect(offs_t[:, (lo + s) // 16 : (lo + s + piece) // 16]))
+            window = pair_words[:, start : start + (T if s1 - s0 <= NARROW else 2 * T)]
+            nc.vector.tensor_copy(planes[a, g][:, u, s0:s1], window.indirect(offs_t[:, (lo + s0) // 16 : (lo + s1) // 16]))
 
         def gather_on_scalar(g, s0, s1):
             lo = GROUPS[g][0] * C
             dst = planes[0, g][:, 1, :].bitcast(BF16).rearrange("p (s d) -> p s d", d=2)
             for d in range(2):
-                nc.scalar.activation(dst[:, s0:s1, d], last_rows[d][:].indirect(offs_t[:, (lo + s0) // 16 : (lo + s1) // 16]), COPY)
+                window = single_rows[d][:].indirect(offs_t[:, (lo + s0) // 16 : (lo + s1) // 16])
+                nc.scalar.activation(dst[:, s0:s1, d], window, COPY)
 
         def weave(copy, dtype, a, g):
             src = planes[a, g][:].bitcast(dtype).rearrange("p u s -> p s u")
             dst = slots[a, g][:].bitcast(dtype).rearrange("p (s u) -> p s u", u=2)
             copy(out=dst, in_=src)
 
-        def quantize_slots(a, g):
-            nc.vector.quantize_mx(out=codes[a, g].bitcast(FP8X4), scales=scales[a, g][:], in_=slots[a, g][:])
-
-        def quantize_toks(tok_codes, toks, lo, hi):
-            nc.vector.quantize_mx(out=tok_codes[:, lo:hi].bitcast(FP8X4), scales=tok_scales[:, lo:hi], in_=toks[:])
-
-        def weave_toks(dst, a, t0, t1):
-            base = block[a, 1] * T
+        def weave_tokens(dst, a, t0, t1):
+            base = place[a, 1] * T
             src = pair_words[:, base : base + 2 * T].rearrange("p (u t) -> p t u", u=2)
             nc.scalar.copy(out=dst.bitcast(U32).rearrange("p (t u) -> p t u", u=2), in_=src[:, t0:t1, ::-1])
+
+        def quantize_slots(a, g):
+            nc.vector.quantize_mx(out=codes[a, g].bitcast(FP8X4), scales=scales[a, g][:], in_=slots[a, g][:])
 
         def matmul(dst, e, a, m, rhs, rhs_scale):
             nc.tensor.matmul_mx(
@@ -142,47 +151,47 @@ def tile_moe_shr_lin_none_kernel(tc, xT, w_words, w_scales, gate, offs, pos1, po
                 stop=(a == PASSES - 1),
             )
 
-        def new_bank(i):
+        def bank(i):
             return psum.tile([P, BANK], F32, name=f"bank{i}")
 
-
-        def experts(m, g, bank):
+        def experts(m, g, dst):
             e0, e1 = GROUPS[g]
             for e in range(e0, e1):
                 cols = slice((e - e0) * C, (e - e0 + 1) * C)
                 for a in range(PASSES):
-                    matmul(bank[:, cols], e, a, m, codes[a, g][:, cols], scales[a, g][:, cols])
-            return bank
+                    matmul(dst[:, cols], e, a, m, codes[a, g][:, cols], scales[a, g][:, cols])
+            return dst
 
-        for t0, t1, src in raw_first:
-            cast(nc.vector.tensor_copy, 0, 0, src, t0, t1)
-        cast(nc.scalar.copy, 0, 1, raw[0, 1], 0, T)
+        for (t0, t1), rows in zip(FIRST_LOADS, raw_first):
+            round_pairs(nc.vector.tensor_copy, 0, 0, rows, t0, t1)
+        round_pairs(nc.scalar.copy, 0, 1, raw[0, 1], 0, T)
         for d in range(2):
-            copy_on_gpsimd(last_rows[d][:], raw[0, 1][:, d, :])
+            copy_on_gpsimd(single_rows[d][:], raw[0, 1][:, d, :])
         for u in range(2):
-            cast(copy_on_gpsimd, 1, u, raw[1, u], 0, T)
-        codes0 = work.tile([P, 2 * BANK], U32, name="codes0", tag="raw11_0", align_bytes=64)
-        for g in range(2):
-            codes[0, g] = codes0[:, g * BANK : (g + 1) * BANK]
-        for g in range(3):
-            gather(0, 0, g, width[g])
-        gather(0, 1, 0, width[0])
-        gather(0, 1, 1, width[1] - SCALAR_EXTRA)
+            round_pairs(copy_on_gpsimd, 1, u, raw[1, u], 0, T)
+        first_codes = work.tile([P, width[0] + width[1]], U32, name="first_codes", tag="raw11_0", align_bytes=64)
+        codes[0, 0], codes[0, 1] = first_codes[:, : width[0]], first_codes[:, width[0] :]
+
+        for g in range(len(GROUPS)):
+            for s0 in range(0, width[g], FIRST_PIECE):
+                gather(0, 0, g, s0, s0 + FIRST_PIECE)
+        gather(0, 1, 0, 0, width[0])
+        gather(0, 1, 1, 0, width[1] - SCALAR_EXTRA)
         gather_on_scalar(2, 0, width[2])
         gather_on_scalar(1, width[1] - SCALAR_EXTRA, width[1])
-        for g in (0, 1):
+        for g in range(2):
             slots[0, g] = work.tile([P, width[g] * 4], BF16, name=f"slots0{g}", tag=f"slots0{g}", align_bytes=64)
-        weave(nc.scalar.copy, U32, 0, 2)
-        for g in range(2):
+        for g in (2, 0, 1):
             weave(nc.scalar.copy, U32, 0, g)
+
         for g in range(2):
-            gather(1, 0, g, width[g])
-        gather(1, 1, 0, width[0])
+            gather(1, 0, g, 0, width[g])
+        gather(1, 1, 0, 0, width[0])
         quantize_slots(0, 0)
-        idle = new_bank(7)
-        for i in range(4):
+        unread = bank(7)
+        for i in range(WARM_UPS):
             nc.tensor.matmul_mx(
-                out=idle[:],
+                out=unread[:],
                 lhsT=ww[0][:, 0, : 2 * P].bitcast(FP4X4),
                 lhsT_scale=scales[0, 0][:, :P],
                 rhs=codes[0, 0].bitcast(FP8X4),
@@ -190,19 +199,20 @@ def tile_moe_shr_lin_none_kernel(tc, xT, w_words, w_scales, gate, offs, pos1, po
                 start=True,
                 stop=True,
             )
-        gather(1, 1, 1, width[1])
+        gather(1, 1, 1, 0, width[1])
         weave(nc.scalar.copy, U32, 1, 0)
-        toks = work.tile([P, WIDE * 4], BF16, name="toks", tag="slots00", align_bytes=64)
-        weave_toks(toks[:, : 4 * T], 0, 0, T)
+        tokens = work.tile([P, WIDE * 4], BF16, name="tokens", tag="slots00", align_bytes=64)
+        weave_tokens(tokens[:, : 4 * T], 0, 0, T)
         weave(nc.scalar.copy, U32, 1, 1)
-        weave_toks(toks[:, 4 * T :], 1, 0, WIDE - T)
+        weave_tokens(tokens[:, 4 * T :], 1, 0, WIDE - T)
         quantize_slots(0, 1)
         quantize_slots(1, 0)
-        toks_end = work.tile([P, (PASSES * T - WIDE) * 4], BF16, name="toks_end", tag="slots10", align_bytes=64)
-        weave_toks(toks_end[:], 1, WIDE - T, T)
+        tokens_end = work.tile([P, (PASSES * T - WIDE) * 4], BF16, name="tokens_end", tag="slots10", align_bytes=64)
+        weave_tokens(tokens_end[:], 1, WIDE - T, T)
+
         planes[1, 2] = work.tile([P, 2, width[2]], U32, name="planes12", tag="planes10", align_bytes=64)
         for u in range(2):
-            gather(1, u, 2, width[2])
+            gather(1, u, 2, 0, width[2])
         quantize_slots(1, 1)
         slots[1, 2] = work.tile([P, width[2] * 4], BF16, name="slots12", tag="planes11", align_bytes=64)
         weave(nc.vector.tensor_copy, I32, 1, 2)
@@ -210,91 +220,92 @@ def tile_moe_shr_lin_none_kernel(tc, xT, w_words, w_scales, gate, offs, pos1, po
         quantize_slots(0, 2)
         quantize_slots(1, 2)
         tok_codes = work.tile([P, PASSES * T], U32, name="tok_codes", tag="slots02", align_bytes=64)
-        quantize_toks(tok_codes, toks, 0, WIDE)
-        quantize_toks(tok_codes, toks_end, WIDE, PASSES * T)
+        for woven, lo, hi in ((tokens, 0, WIDE), (tokens_end, WIDE, PASSES * T)):
+            nc.vector.quantize_mx(out=tok_codes[:, lo:hi].bitcast(FP8X4), scales=tok_scales[:, lo:hi], in_=woven[:])
+
         y = [work.tile([P, S], F32, name=f"y{m}", align_bytes=64) for m in range(M - 1)]
 
-        def empty(m, g, src):
-            e0, e1 = GROUPS[g]
-            nc.scalar.copy(out=y[m][:, e0 * C : e1 * C], in_=src)
+        def empty(m, sums):
+            for (e0, e1), src in zip(GROUPS, sums):
+                nc.scalar.copy(out=y[m][:, e0 * C : e1 * C], in_=src)
 
-        sums = {(m, 0): experts(m, 0, new_bank(m)[:]) for m in range(1)}
-        for g in (1, 2):
-            sums[0, g] = experts(0, g, new_bank(g * M)[:, : width[g]])
-        for g in range(3):
-            empty(0, g, sums[0, g])
-        for g in range(2):
-            sums[1, g] = experts(1, g, new_bank(g * M + 1)[:])
-        last = new_bank(7)
-        for m in (1, 2):
-            sums[m, 2] = experts(m, 2, last[:, (m - 1) * width[2] : m * width[2]])
-        for g in range(3):
-            empty(1, g, sums[1, g])
+        first_group = [experts(m, 0, bank(m)[:]) for m in range(M)]
+        empty(0, first_group[:1] + [experts(0, g, bank(M * g)[:, : width[g]]) for g in (1, 2)])
+        second_group1 = experts(1, 1, bank(M + 1)[:])
+        last_bank = bank(7)
+        last_group = {m: experts(m, 2, last_bank[:, (m - 1) * width[2] : m * width[2]]) for m in (1, 2)}
+        empty(1, [first_group[1], second_group1, last_group[1]])
 
         shared = work.tile([P, M - 1, T], F32, name="shared")
 
         def shared_expert(dst, m, lo, hi):
             for a in range(PASSES):
                 matmul(dst, E, a, m, tok_codes[:, a * T + lo : a * T + hi], tok_scales[:, a * T + lo : a * T + hi])
+            return dst
 
-        def shared_head(m, bank):
-            shared_expert(bank[:], m, 0, BANK)
-            return bank
-
-        nc.scalar.copy(out=shared[:, 0, :BANK], in_=shared_head(0, new_bank(2))[:])
-        tail = new_bank(3)
+        nc.scalar.copy(out=shared[:, 0, :BANK], in_=shared_expert(bank(0)[:], 0, 0, BANK))
+        tails = bank(3)
         for m in range(M):
-            shared_expert(tail[:, m * P : (m + 1) * P], m, BANK, T)
-        nc.scalar.copy(out=shared[:, :, BANK:], in_=tail[:, : (M - 1) * P].rearrange("p (m t) -> p m t", m=M - 1))
-        sums[2, 0] = experts(2, 0, new_bank(0)[:])
-        sums[2, 1] = experts(2, 1, new_bank(M + 2)[:])
-        second_head = shared_head(1, new_bank(1))
+            shared_expert(tails[:, m * P : (m + 1) * P], m, BANK, T)
+        nc.scalar.copy(out=shared[:, :, BANK:], in_=tails[:, : (M - 1) * P].rearrange("p (m t) -> p m t", m=M - 1))
+        second_group2 = experts(2, 1, bank(M + 2)[:])
+        head1 = shared_expert(bank(1)[:], 1, 0, BANK)
         y.append(work.tile([P, S], F32, name="y2", tag="codes11", align_bytes=64))
-        for g in range(3):
-            empty(2, g, sums[2, g])
+        empty(2, [first_group[2], second_group2, last_group[2]])
+        nc.scalar.copy(out=shared[:, 1, :BANK], in_=head1)
 
         first = [work.tile([P, T], F32, name=f"first{m}") for m in range(M)]
 
-        def pick1(m):
-            nc.vector.tensor_tensor(first[m][:], y[m][:].indirect(pos1_t[:]), gates[:, 0, :], MULT)
+        def gate_of(choice, lo, hi):
+            t0 = max(start for start in gates if start <= lo)
+            return gates[t0][:, choice, lo - t0 : hi - t0]
+
+        def pick1(m, lo, hi):
+            window = y[m][:].indirect(pos1_t[:, lo // 16 : hi // 16])
+            nc.vector.tensor_tensor(first[m][:, lo:hi], window, gate_of(0, lo, hi), MULT)
 
         def pick2(m, lo, hi):
             second = work.tile([P, hi - lo], F32, name=f"second{m}_{lo}")
-            nc.vector.tensor_tensor(second[:], y[m][:].indirect(pos2_t[:, lo // 16 : hi // 16]), gates[:, 1, lo:hi], MULT)
+            window = y[m][:].indirect(pos2_t[:, lo // 16 : hi // 16])
+            nc.vector.tensor_tensor(second[:], window, gate_of(1, lo, hi), MULT)
             return second
 
-        free = [6, 2, 7, 0, 2, 7, 0, 6, 5, 2]
-
-        def sum_turned(m, lo, hi, second):
-            bank = new_bank(free.pop(0))
+        def sum_turned(m, lo, hi, second, i):
+            acc = bank(i)
             for t in range(lo, hi, P):
                 terms = (shared[:, m, t : t + P], first[m][:, t : t + P], second[:, t - lo : t - lo + P])
-                for i, term in enumerate(terms):
-                    nc.tensor.matmul(bank[:, t - lo : t - lo + P], term, ident[:], start=(i == 0), stop=(i == len(terms) - 1), is_transpose=True)
+                for n, term in enumerate(terms):
+                    nc.tensor.matmul(
+                        acc[:, t - lo : t - lo + P], term, ident[:], start=(n == 0), stop=(n == len(terms) - 1), is_transpose=True
+                    )
             turned = work.tile([P, hi - lo], F32, name=f"turned{m}_{lo}")
-            nc.scalar.copy(out=turned[:], in_=bank[:, : hi - lo])
+            nc.scalar.copy(out=turned[:], in_=acc[:, : hi - lo])
             return turned
 
-        def turn_back(m, lo, hi, turned):
-            bank = new_bank(free.pop(0))
+        def turn_back(m, lo, hi, turned, i):
+            back = bank(i)
             for t in range(0, hi - lo, P):
-                nc.tensor.transpose(bank[:, t : t + P], turned[:, t : t + P], ident[:])
+                nc.tensor.transpose(back[:, t : t + P], turned[:, t : t + P], ident[:])
             res = work.tile([P, hi - lo], F32, name=f"res{m}_{lo}")
-            nc.scalar.copy(out=res[:], in_=bank[:, : hi - lo])
+            nc.scalar.copy(out=res[:], in_=back[:, : hi - lo])
             nc.scalar.dma_start(out[m * P : (m + 1) * P, lo:hi], res[:])
 
-        pick1(0)
-        turned = [sum_turned(0, lo, hi, pick2(0, lo, hi)) for lo, hi in HALVES]
-        nc.scalar.copy(out=shared[:, 1, :BANK], in_=second_head[:])
-        for (lo, hi), part in zip(HALVES, turned):
-            turn_back(0, lo, hi, part)
-        head = shared_head(2, new_bank(4))
-        pick1(1)
-        turned = [sum_turned(1, lo, hi, pick2(1, lo, hi)) for lo, hi in THIRDS]
-        for (lo, hi), part in zip(THIRDS, turned):
-            turn_back(1, lo, hi, part)
+        turned = []
+        for (lo, hi), i in zip(HALVES, (6, 0)):
+            pick1(0, lo, hi)
+            turned.append(sum_turned(0, lo, hi, pick2(0, lo, hi), i))
+        for (lo, hi), part, i in zip(HALVES, turned, (7, 2)):
+            turn_back(0, lo, hi, part, i)
+        head2 = shared_expert(bank(4)[:], 2, 0, BANK)
 
-        pick1(2)
+        for lo, hi in HALVES:
+            pick1(1, lo, hi)
+        turned = [sum_turned(1, lo, hi, pick2(1, lo, hi), i) for (lo, hi), i in zip(THIRDS, (0, 7, 2))]
+        for (lo, hi), part, i in zip(THIRDS, turned, (6, 5, 0)):
+            turn_back(1, lo, hi, part, i)
+
+        for lo, hi in HALVES:
+            pick1(2, lo, hi)
         partial = work.tile([P, T], F32, name="partial")
 
         def finish(lo, hi, second):
@@ -302,12 +313,12 @@ def tile_moe_shr_lin_none_kernel(tc, xT, w_words, w_scales, gate, offs, pos1, po
             nc.vector.tensor_tensor(res[:], partial[:, lo:hi], second[:], ADD)
             nc.sync.dma_start(out[2 * P :, lo:hi], res[:])
 
-        ends = ((BANK, T), (0, 384), (384, BANK))
-        seconds = [pick2(2, *ends[0])]
-        nc.vector.tensor_tensor(partial[:, BANK:], tail[:, 2 * P : 3 * P], first[2][:, BANK:], ADD)
-        seconds.append(pick2(2, *ends[1]))
-        finish(*ends[0], seconds[0])
-        nc.vector.tensor_tensor(partial[:, :BANK], head[:], first[2][:, :BANK], ADD)
-        seconds.append(pick2(2, *ends[2]))
-        finish(*ends[1], seconds[1])
-        finish(*ends[2], seconds[2])
+        low, middle, high = THIRDS
+        second_high = pick2(2, *high)
+        nc.vector.tensor_tensor(partial[:, BANK:], tails[:, 2 * P : 3 * P], first[2][:, BANK:], ADD)
+        second_middle = pick2(2, *middle)
+        finish(*high, second_high)
+        nc.vector.tensor_tensor(partial[:, :BANK], head2, first[2][:, :BANK], ADD)
+        second_low = pick2(2, *low)
+        finish(*middle, second_middle)
+        finish(*low, second_low)

@@ -25,13 +25,13 @@ M = N // P
 BANK = 512
 GROUPS = ((0, 4), (4, 8), (8, 10))
 FIRST_LOADS = ((0, 384), (384, T))
-FIRST_PIECE = 256
+SPARE = 64
 NARROW = 3 * T // 4
-SCALAR_EXTRA = 128
+SCALAR_EXTRA = 256
 WIDE = 1024
 HALVES = ((0, 256), (256, T))
 THIRDS = ((0, 256), (256, BANK), (BANK, T))
-WARM_UPS = 4
+WARM_UPS = 1
 
 
 def tile_moe_shr_lin_none_kernel(tc, xT, w_words, w_scales, gate, offs, pos1, pos2, out):
@@ -39,6 +39,7 @@ def tile_moe_shr_lin_none_kernel(tc, xT, w_words, w_scales, gate, offs, pos1, po
     with ExitStack() as ctx:
         keep = ctx.enter_context(tc.tile_pool(name="keep", bufs=1))
         work = ctx.enter_context(tc.tile_pool(name="work", bufs=1))
+        placed = ctx.enter_context(tc.tile_pool(name="placed", bufs=1))
         psum = ctx.enter_context(tc.psum_pool(name="psum", bufs=1))
 
         offs_t = keep.tile([P, S // 16], U16, name="offs_t")
@@ -54,7 +55,11 @@ def tile_moe_shr_lin_none_kernel(tc, xT, w_words, w_scales, gate, offs, pos1, po
 
         raw_first = [load_x(0, 0, t0, t1) for t0, t1 in FIRST_LOADS]
         nc.sync.dma_start(offs_t[:], offs)
-        raw = {(a, u): load_x(a, u, 0, T) for a, u in ((0, 1), (1, 0), (1, 1))}
+        raw_second = [load_x(0, 1, t0, t1) for t0, t1 in FIRST_LOADS]
+        raw1 = placed.tile([P, 4 * T], F32, name="raw1", offset=8192, align_bytes=64)
+        raw1_rows = raw1[:].rearrange("p (j t) -> p j t", j=4)
+        for u in range(2):
+            nc.sync.dma_start(raw1_rows[:, 2 * u : 2 * u + 2, :], x_view[1][:, 2 * u : 2 * u + 2, :])
 
         ws = work.tile([P, (E + 1) * PASSES, N], U8, name="ws", align_bytes=64)
         nc.gpsimd.memset(ws[:].rearrange("p e n -> p (e n)").bitcast(I32), 0)
@@ -71,20 +76,19 @@ def tile_moe_shr_lin_none_kernel(tc, xT, w_words, w_scales, gate, offs, pos1, po
             for e in range(e0, e1):
                 ww[e] = words[:, PASSES * (e - e0) : PASSES * (e - e0 + 1), :]
 
-        gates = {t0: work.tile([P, 2, t1 - t0], F32, name=f"gates{t0}") for t0, t1 in HALVES}
-        for e0, e1 in GROUPS:
-            load_w(e0, e1)
+        gates = work.tile([P, 2, T], F32, name="gates")
+        load_w(*GROUPS[0])
+        load_w(GROUPS[1][0], E + 1)
         nc.sync.dma_start(pos2_t[:], pos2)
         nc.sync.dma_start(pos1_t[:], pos1)
-        for t0, t1 in HALVES:
-            nc.sync.dma_start(gates[t0][:], gate[:, :P, t0:t1].rearrange("g p t -> p g t"))
-        load_w(E, E + 1)
+        nc.sync.dma_start(gates[:], gate[:, :P, :].rearrange("g p t -> p g t"))
 
         ident = work.tile([P, P], F32, name="ident")
         make_identity(nc, ident[:])
 
-        pairs = work.tile([P, 2 * PASSES * T * 2], BF16, name="pairs", align_bytes=64)
+        pairs = work.tile([P, (2 * PASSES * T + SPARE) * 2], BF16, name="pairs", align_bytes=64)
         pair_words = pairs[:].bitcast(U32)
+        nc.gpsimd.memset(pair_words[:, 2 * PASSES * T :], 0)
         place = {(1, 1): 0, (1, 0): 1, (0, 1): 2, (0, 0): 3}
         single_rows = [work.tile([P, T], BF16, name=f"single_row{d}", tag=("slots01", "slots00")[d], align_bytes=64) for d in range(2)]
         tok_scales = work.tile([P, PASSES * T], U8, name="tok_scales", align_bytes=64)
@@ -94,8 +98,9 @@ def tile_moe_shr_lin_none_kernel(tc, xT, w_words, w_scales, gate, offs, pos1, po
         planes = {
             (a, g): work.tile([P, 2, width[g]], U32, name=f"planes{a}{g}", tag=f"planes{a}{g}", align_bytes=64)
             for a, g in cells
-            if (a, g) != (1, 2)
+            if (a, g) not in ((1, 0), (1, 2))
         }
+        planes[1, 0] = placed.tile([P, 2, width[0]], U32, name="planes10", offset=0, align_bytes=64)
         slots = {
             (a, g): work.tile([P, width[g] * 4], BF16, name=f"slots{a}{g}", tag=f"slots{a}{g}", align_bytes=64)
             for a, g in ((0, 2), (1, 0), (1, 1))
@@ -109,7 +114,7 @@ def tile_moe_shr_lin_none_kernel(tc, xT, w_words, w_scales, gate, offs, pos1, po
         def round_pairs(copy, a, u, rows, t0, t1):
             base = place[a, u] * 2 * T
             dst = pairs[:, base + 2 * t0 : base + 2 * t1].rearrange("p (t d) -> p t d", d=2)
-            copy(out=dst, in_=rows[:].rearrange("p d t -> p t d"))
+            copy(out=dst, in_=rows.rearrange("p d t -> p t d"))
 
         def copy_on_gpsimd(out, in_):
             nc.gpsimd.tensor_scalar(out, in_, 1.0, 0.0, MULT, ADD)
@@ -117,7 +122,7 @@ def tile_moe_shr_lin_none_kernel(tc, xT, w_words, w_scales, gate, offs, pos1, po
         def gather(a, u, g, s0, s1):
             start = place[a, u] * T
             lo = GROUPS[g][0] * C
-            window = pair_words[:, start : start + (T if s1 - s0 <= NARROW else 2 * T)]
+            window = pair_words[:, start : start + (T if s1 - s0 <= NARROW else T + SPARE if (a, u) == (0, 0) else 2 * T)]
             nc.vector.tensor_copy(planes[a, g][:, u, s0:s1], window.indirect(offs_t[:, (lo + s0) // 16 : (lo + s1) // 16]))
 
         def gather_on_scalar(g, s0, s1):
@@ -154,34 +159,39 @@ def tile_moe_shr_lin_none_kernel(tc, xT, w_words, w_scales, gate, offs, pos1, po
         def bank(i):
             return psum.tile([P, BANK], F32, name=f"bank{i}")
 
-        def experts(m, g, dst):
+        def experts(m, g, dst, part=None):
             e0, e1 = GROUPS[g]
-            for e in range(e0, e1):
+            for e in part or range(e0, e1):
                 cols = slice((e - e0) * C, (e - e0 + 1) * C)
                 for a in range(PASSES):
                     matmul(dst[:, cols], e, a, m, codes[a, g][:, cols], scales[a, g][:, cols])
             return dst
 
         for (t0, t1), rows in zip(FIRST_LOADS, raw_first):
-            round_pairs(nc.vector.tensor_copy, 0, 0, rows, t0, t1)
-        round_pairs(nc.scalar.copy, 0, 1, raw[0, 1], 0, T)
+            round_pairs(nc.vector.tensor_copy, 0, 0, rows[:], t0, t1)
+        for (t0, t1), rows in zip(FIRST_LOADS, raw_second):
+            round_pairs(nc.scalar.copy, 0, 1, rows[:], t0, t1)
         for d in range(2):
-            copy_on_gpsimd(single_rows[d][:], raw[0, 1][:, d, :])
+            for (t0, t1), rows in zip(FIRST_LOADS, raw_second):
+                copy_on_gpsimd(single_rows[d][:, t0:t1], rows[:, d, :])
         for u in range(2):
-            round_pairs(copy_on_gpsimd, 1, u, raw[1, u], 0, T)
-        first_codes = work.tile([P, width[0] + width[1]], U32, name="first_codes", tag="raw11_0", align_bytes=64)
-        codes[0, 0], codes[0, 1] = first_codes[:, : width[0]], first_codes[:, width[0] :]
+            round_pairs(copy_on_gpsimd, 1, u, raw1_rows[:, 2 * u : 2 * u + 2, :], 0, T)
+        tokens = work.tile([P, WIDE * 4], BF16, name="tokens", tag="tokens", align_bytes=64)
+        tokens_end = work.tile([P, (PASSES * T - WIDE) * 4], BF16, name="tokens_end", align_bytes=64)
+        for dst, t0, t1 in ((tokens[:, 4 * T :], 0, WIDE - T), (tokens_end[:, : 4 * (512 - WIDE + T)], WIDE - T, 512)):
+            copy_on_gpsimd(dst.rearrange("p (t j) -> p t j", j=4), raw1_rows[:, :, t0:t1].rearrange("p j t -> p t j"))
+        for a in range(PASSES):
+            codes[a, 0] = placed.tile([P, width[0]], U32, name=f"codes{a}0", offset=8192 + 4 * width[0] * a, align_bytes=64)[:]
 
         for g in range(len(GROUPS)):
-            for s0 in range(0, width[g], FIRST_PIECE):
-                gather(0, 0, g, s0, s0 + FIRST_PIECE)
+            gather(0, 0, g, 0, width[g])
         gather(0, 1, 0, 0, width[0])
         gather(0, 1, 1, 0, width[1] - SCALAR_EXTRA)
         gather_on_scalar(2, 0, width[2])
         gather_on_scalar(1, width[1] - SCALAR_EXTRA, width[1])
         for g in range(2):
             slots[0, g] = work.tile([P, width[g] * 4], BF16, name=f"slots0{g}", tag=f"slots0{g}", align_bytes=64)
-        for g in (2, 0, 1):
+        for g in (0, 1, 2):
             weave(nc.scalar.copy, U32, 0, g)
 
         for g in range(2):
@@ -200,41 +210,44 @@ def tile_moe_shr_lin_none_kernel(tc, xT, w_words, w_scales, gate, offs, pos1, po
                 stop=True,
             )
         gather(1, 1, 1, 0, width[1])
+        weave_tokens(tokens_end[:, 4 * (512 - WIDE + T) :], 1, 512, T)
         weave(nc.scalar.copy, U32, 1, 0)
-        tokens = work.tile([P, WIDE * 4], BF16, name="tokens", tag="slots00", align_bytes=64)
-        weave_tokens(tokens[:, : 4 * T], 0, 0, T)
         weave(nc.scalar.copy, U32, 1, 1)
-        weave_tokens(tokens[:, 4 * T :], 1, 0, WIDE - T)
-        quantize_slots(0, 1)
+        weave_tokens(tokens[:, : 4 * T], 0, 0, T)
         quantize_slots(1, 0)
-        tokens_end = work.tile([P, (PASSES * T - WIDE) * 4], BF16, name="tokens_end", tag="slots10", align_bytes=64)
-        weave_tokens(tokens_end[:], 1, WIDE - T, T)
+        codes[0, 1] = placed.tile([P, width[1]], U32, name="codes01", offset=8192 + 4096, align_bytes=64)[:]
 
-        planes[1, 2] = work.tile([P, 2, width[2]], U32, name="planes12", tag="planes10", align_bytes=64)
+        y = {0: work.tile([P, S], F32, name="y0", align_bytes=64)}
+
+        def empty(m, g, src):
+            nc.scalar.copy(out=y[m][:, GROUPS[g][0] * C : GROUPS[g][1] * C], in_=src)
+
+        first_group = [experts(m, 0, bank(m)[:]) for m in range(2)]
+
+        planes[1, 2] = placed.tile([P, 2, width[2]], U32, name="planes12", offset=8192 + 6144, align_bytes=64)
         for u in range(2):
             gather(1, u, 2, 0, width[2])
-        quantize_slots(1, 1)
-        slots[1, 2] = work.tile([P, width[2] * 4], BF16, name="slots12", tag="planes11", align_bytes=64)
-        weave(nc.vector.tensor_copy, I32, 1, 2)
-        codes[0, 2] = work.tile([P, width[2]], U32, name="codes02", tag="slots11", align_bytes=64)[:]
-        quantize_slots(0, 2)
-        quantize_slots(1, 2)
-        tok_codes = work.tile([P, PASSES * T], U32, name="tok_codes", tag="slots02", align_bytes=64)
+        slots[1, 2] = work.tile([P, width[2] * 4], BF16, name="slots12", align_bytes=64)
+        weave(nc.scalar.copy, U32, 1, 2)
+        codes[0, 2] = work.tile([P, width[2]], U32, name="codes02", tag="planes11", align_bytes=64)[:]
+        for a, g in ((0, 1), (1, 1), (0, 2), (1, 2)):
+            quantize_slots(a, g)
+        tok_codes = placed.tile([P, PASSES * T], U32, name="tok_codes", offset=8192 + 6144, align_bytes=64)
         for woven, lo, hi in ((tokens, 0, WIDE), (tokens_end, WIDE, PASSES * T)):
             nc.vector.quantize_mx(out=tok_codes[:, lo:hi].bitcast(FP8X4), scales=tok_scales[:, lo:hi], in_=woven[:])
 
-        y = [work.tile([P, S], F32, name=f"y{m}", align_bytes=64) for m in range(M - 1)]
-
-        def empty(m, sums):
-            for (e0, e1), src in zip(GROUPS, sums):
-                nc.scalar.copy(out=y[m][:, e0 * C : e1 * C], in_=src)
-
-        first_group = [experts(m, 0, bank(m)[:]) for m in range(M)]
-        empty(0, first_group[:1] + [experts(0, g, bank(M * g)[:, : width[g]]) for g in (1, 2)])
-        second_group1 = experts(1, 1, bank(M + 1)[:])
+        empty(0, 0, first_group[0])
+        for i, lo in ((3, 0), (2, 2)):
+            half = experts(0, 1, bank(i)[:], range(4 + lo, 6 + lo))
+            nc.scalar.copy(out=y[0][:, (4 + lo) * C : (6 + lo) * C], in_=half[:, lo * C : (lo + 2) * C])
+        empty(0, 2, experts(0, 2, bank(6)[:, : width[2]]))
+        y[1] = work.tile([P, S], F32, name="y1", align_bytes=64)
+        third = experts(2, 0, bank(5)[:])
+        empty(1, 0, first_group[1])
+        empty(1, 1, experts(1, 1, bank(2)[:]))
         last_bank = bank(7)
         last_group = {m: experts(m, 2, last_bank[:, (m - 1) * width[2] : m * width[2]]) for m in (1, 2)}
-        empty(1, [first_group[1], second_group1, last_group[1]])
+        empty(1, 2, last_group[1])
 
         shared = work.tile([P, M - 1, T], F32, name="shared")
 
@@ -244,36 +257,33 @@ def tile_moe_shr_lin_none_kernel(tc, xT, w_words, w_scales, gate, offs, pos1, po
             return dst
 
         nc.scalar.copy(out=shared[:, 0, :BANK], in_=shared_expert(bank(0)[:], 0, 0, BANK))
-        tails = bank(3)
+        tails = bank(4)
         for m in range(M):
             shared_expert(tails[:, m * P : (m + 1) * P], m, BANK, T)
         nc.scalar.copy(out=shared[:, :, BANK:], in_=tails[:, : (M - 1) * P].rearrange("p (m t) -> p m t", m=M - 1))
-        second_group2 = experts(2, 1, bank(M + 2)[:])
-        head1 = shared_expert(bank(1)[:], 1, 0, BANK)
-        y.append(work.tile([P, S], F32, name="y2", tag="codes11", align_bytes=64))
-        empty(2, [first_group[2], second_group2, last_group[2]])
-        nc.scalar.copy(out=shared[:, 1, :BANK], in_=head1)
 
         first = [work.tile([P, T], F32, name=f"first{m}") for m in range(M)]
 
         def gate_of(choice, lo, hi):
-            t0 = max(start for start in gates if start <= lo)
-            return gates[t0][:, choice, lo - t0 : hi - t0]
+            return gates[:, choice, lo:hi]
 
         def pick1(m, lo, hi):
             window = y[m][:].indirect(pos1_t[:, lo // 16 : hi // 16])
             nc.vector.tensor_tensor(first[m][:, lo:hi], window, gate_of(0, lo, hi), MULT)
 
-        def pick2(m, lo, hi):
-            second = work.tile([P, hi - lo], F32, name=f"second{m}_{lo}")
+        def pick2(m, lo, hi, second=None):
+            if second is None:
+                second = work.tile([P, hi - lo], F32, name=f"second{m}_{lo}")[:]
             window = y[m][:].indirect(pos2_t[:, lo // 16 : hi // 16])
-            nc.vector.tensor_tensor(second[:], window, gate_of(1, lo, hi), MULT)
+            nc.vector.tensor_tensor(second, window, gate_of(1, lo, hi), MULT)
             return second
 
         def sum_turned(m, lo, hi, second, i):
             acc = bank(i)
             for t in range(lo, hi, P):
-                terms = (shared[:, m, t : t + P], first[m][:, t : t + P], second[:, t - lo : t - lo + P])
+                terms = [shared[:, m, t : t + P], first[m][:, t : t + P]]
+                if second is not None:
+                    terms.append(second[:, t - lo : t - lo + P])
                 for n, term in enumerate(terms):
                     nc.tensor.matmul(
                         acc[:, t - lo : t - lo + P], term, ident[:], start=(n == 0), stop=(n == len(terms) - 1), is_transpose=True
@@ -288,29 +298,34 @@ def tile_moe_shr_lin_none_kernel(tc, xT, w_words, w_scales, gate, offs, pos1, po
                 nc.tensor.transpose(back[:, t : t + P], turned[:, t : t + P], ident[:])
             res = work.tile([P, hi - lo], F32, name=f"res{m}_{lo}")
             nc.scalar.copy(out=res[:], in_=back[:, : hi - lo])
-            nc.scalar.dma_start(out[m * P : (m + 1) * P, lo:hi], res[:])
+            (nc.sync if m == 0 else nc.scalar).dma_start(out[m * P : (m + 1) * P, lo:hi], res[:])
 
+        y[2] = work.tile([P, S], F32, name="y2", tag="codes12", align_bytes=64)
+        empty(2, 2, last_group[2])
+        empty(2, 0, third)
+        fourth = experts(2, 1, bank(6)[:])
+        nc.scalar.copy(out=shared[:, 1, :BANK], in_=shared_expert(bank(1)[:], 1, 0, BANK))
         turned = []
-        for (lo, hi), i in zip(HALVES, (6, 0)):
+        for (lo, hi), i in zip(HALVES, (3, 0)):
             pick1(0, lo, hi)
             turned.append(sum_turned(0, lo, hi, pick2(0, lo, hi), i))
+            if lo == 0:
+                empty(2, 1, fourth)
+        head2 = shared_expert(bank(3)[:], 2, 0, BANK)
         for (lo, hi), part, i in zip(HALVES, turned, (7, 2)):
             turn_back(0, lo, hi, part, i)
-        head2 = shared_expert(bank(4)[:], 2, 0, BANK)
 
-        for lo, hi in HALVES:
-            pick1(1, lo, hi)
+        pick1(1, 0, T)
         turned = [sum_turned(1, lo, hi, pick2(1, lo, hi), i) for (lo, hi), i in zip(THIRDS, (0, 7, 2))]
-        for (lo, hi), part, i in zip(THIRDS, turned, (6, 5, 0)):
+        for (lo, hi), part, i in zip(THIRDS, turned, (5, 6, 1)):
             turn_back(1, lo, hi, part, i)
 
-        for lo, hi in HALVES:
-            pick1(2, lo, hi)
+        pick1(2, 0, T)
         partial = work.tile([P, T], F32, name="partial")
 
         def finish(lo, hi, second):
             res = work.tile([P, hi - lo], F32, name=f"res2_{lo}")
-            nc.vector.tensor_tensor(res[:], partial[:, lo:hi], second[:], ADD)
+            nc.vector.tensor_tensor(res[:], partial[:, lo:hi], second, ADD)
             nc.sync.dma_start(out[2 * P :, lo:hi], res[:])
 
         low, middle, high = THIRDS

@@ -27,8 +27,9 @@ GROUPS = ((0, 4), (4, 8), (8, 10))
 FIRST_LOADS = ((0, 384), (384, T))
 SPARE = 64
 NARROW = 3 * T // 4
-SCALAR_EXTRA = 256
+SCALAR_EXTRA = 128
 WIDE = 1024
+GPSIMD_TOKENS = 384
 HALVES = ((0, 256), (256, T))
 THIRDS = ((0, 256), (256, BANK), (BANK, T))
 WARM_UPS = 1
@@ -61,12 +62,6 @@ def tile_moe_shr_lin_none_kernel(tc, xT, w_words, w_scales, gate, offs, pos1, po
         for u in range(2):
             nc.sync.dma_start(raw1_rows[:, 2 * u : 2 * u + 2, :], x_view[1][:, 2 * u : 2 * u + 2, :])
 
-        ws = work.tile([P, (E + 1) * PASSES, N], U8, name="ws", align_bytes=64)
-        nc.gpsimd.memset(ws[:].rearrange("p e n -> p (e n)").bitcast(I32), 0)
-        s_view = w_scales.rearrange("e a q n -> q (e a) n").bitcast(I32)
-        for r in range(4):
-            nc.sync.dma_start(ws[r:P:32].bitcast(I32), s_view[r:16:4])
-
         w_view = w_words.rearrange("e a p b -> p (e a) b").bitcast(I32)
         ww = {}
 
@@ -78,7 +73,14 @@ def tile_moe_shr_lin_none_kernel(tc, xT, w_words, w_scales, gate, offs, pos1, po
 
         gates = work.tile([P, 2, T], F32, name="gates")
         load_w(*GROUPS[0])
-        load_w(GROUPS[1][0], E + 1)
+        load_w(*GROUPS[1])
+        ws = work.tile([P, (E + 1) * PASSES, N], U8, name="ws", align_bytes=64)
+        nc.gpsimd.memset(ws[:].rearrange("p e n -> p (e n)").bitcast(I32), 0)
+        s_view = w_scales.rearrange("e a q n -> q (e a) n").bitcast(I32)
+        for r in range(4):
+            nc.sync.dma_start(ws[r:P:32].bitcast(I32), s_view[r:16:4])
+
+        load_w(GROUPS[2][0], E + 1)
         nc.sync.dma_start(pos2_t[:], pos2)
         nc.sync.dma_start(pos1_t[:], pos1)
         nc.sync.dma_start(gates[:], gate[:, :P, :].rearrange("g p t -> p g t"))
@@ -176,10 +178,11 @@ def tile_moe_shr_lin_none_kernel(tc, xT, w_words, w_scales, gate, offs, pos1, po
                 copy_on_gpsimd(single_rows[d][:, t0:t1], rows[:, d, :])
         for u in range(2):
             round_pairs(copy_on_gpsimd, 1, u, raw1_rows[:, 2 * u : 2 * u + 2, :], 0, T)
-        tokens = work.tile([P, WIDE * 4], BF16, name="tokens", tag="tokens", align_bytes=64)
-        tokens_end = work.tile([P, (PASSES * T - WIDE) * 4], BF16, name="tokens_end", align_bytes=64)
-        for dst, t0, t1 in ((tokens[:, 4 * T :], 0, WIDE - T), (tokens_end[:, : 4 * (512 - WIDE + T)], WIDE - T, 512)):
-            copy_on_gpsimd(dst.rearrange("p (t j) -> p t j", j=4), raw1_rows[:, :, t0:t1].rearrange("p j t -> p t j"))
+        tokens = work.tile([P, PASSES * T * 4], BF16, name="tokens", align_bytes=64)
+        copy_on_gpsimd(
+            tokens[:, 4 * T : 4 * (T + GPSIMD_TOKENS)].rearrange("p (t j) -> p t j", j=4),
+            raw1_rows[:, :, :GPSIMD_TOKENS].rearrange("p j t -> p t j"),
+        )
         for a in range(PASSES):
             codes[a, 0] = placed.tile([P, width[0]], U32, name=f"codes{a}0", offset=8192 + 4 * width[0] * a, align_bytes=64)[:]
 
@@ -210,7 +213,6 @@ def tile_moe_shr_lin_none_kernel(tc, xT, w_words, w_scales, gate, offs, pos1, po
                 stop=True,
             )
         gather(1, 1, 1, 0, width[1])
-        weave_tokens(tokens_end[:, 4 * (512 - WIDE + T) :], 1, 512, T)
         weave(nc.scalar.copy, U32, 1, 0)
         weave(nc.scalar.copy, U32, 1, 1)
         weave_tokens(tokens[:, : 4 * T], 0, 0, T)
@@ -222,29 +224,33 @@ def tile_moe_shr_lin_none_kernel(tc, xT, w_words, w_scales, gate, offs, pos1, po
         def empty(m, g, src):
             nc.scalar.copy(out=y[m][:, GROUPS[g][0] * C : GROUPS[g][1] * C], in_=src)
 
-        first_group = [experts(m, 0, bank(m)[:]) for m in range(2)]
+        first_group = [experts(0, 0, bank(0)[:])]
+        halves = [bank(i) for i in (3, 2)]
+        experts(1, 0, halves[0][:], range(2, 4))
+        experts(1, 0, halves[1][:], range(0, 2))
 
         planes[1, 2] = placed.tile([P, 2, width[2]], U32, name="planes12", offset=8192 + 6144, align_bytes=64)
         for u in range(2):
             gather(1, u, 2, 0, width[2])
         slots[1, 2] = work.tile([P, width[2] * 4], BF16, name="slots12", align_bytes=64)
         weave(nc.scalar.copy, U32, 1, 2)
+        weave_tokens(tokens[:, 4 * (T + GPSIMD_TOKENS) :], 1, GPSIMD_TOKENS, T)
         codes[0, 2] = work.tile([P, width[2]], U32, name="codes02", tag="planes11", align_bytes=64)[:]
         for a, g in ((0, 1), (1, 1), (0, 2), (1, 2)):
             quantize_slots(a, g)
         tok_codes = placed.tile([P, PASSES * T], U32, name="tok_codes", offset=8192 + 6144, align_bytes=64)
-        for woven, lo, hi in ((tokens, 0, WIDE), (tokens_end, WIDE, PASSES * T)):
-            nc.vector.quantize_mx(out=tok_codes[:, lo:hi].bitcast(FP8X4), scales=tok_scales[:, lo:hi], in_=woven[:])
+        for lo, hi in ((0, WIDE), (WIDE, PASSES * T)):
+            nc.vector.quantize_mx(out=tok_codes[:, lo:hi].bitcast(FP8X4), scales=tok_scales[:, lo:hi], in_=tokens[:, 4 * lo : 4 * hi])
 
         empty(0, 0, first_group[0])
-        for i, lo in ((3, 0), (2, 2)):
-            half = experts(0, 1, bank(i)[:], range(4 + lo, 6 + lo))
+        for half, lo in zip(halves, (0, 2)):
+            experts(0, 1, half[:], range(4 + lo, 6 + lo))
             nc.scalar.copy(out=y[0][:, (4 + lo) * C : (6 + lo) * C], in_=half[:, lo * C : (lo + 2) * C])
         empty(0, 2, experts(0, 2, bank(6)[:, : width[2]]))
         y[1] = work.tile([P, S], F32, name="y1", align_bytes=64)
-        third = experts(2, 0, bank(5)[:])
-        empty(1, 0, first_group[1])
-        empty(1, 1, experts(1, 1, bank(2)[:]))
+        for half, lo in zip(halves, (2, 0)):
+            nc.scalar.copy(out=y[1][:, lo * C : (lo + 2) * C], in_=half[:, lo * C : (lo + 2) * C])
+        empty(1, 1, experts(1, 1, bank(1)[:]))
         last_bank = bank(7)
         last_group = {m: experts(m, 2, last_bank[:, (m - 1) * width[2] : m * width[2]]) for m in (1, 2)}
         empty(1, 2, last_group[1])
@@ -298,8 +304,9 @@ def tile_moe_shr_lin_none_kernel(tc, xT, w_words, w_scales, gate, offs, pos1, po
                 nc.tensor.transpose(back[:, t : t + P], turned[:, t : t + P], ident[:])
             res = work.tile([P, hi - lo], F32, name=f"res{m}_{lo}")
             nc.scalar.copy(out=res[:], in_=back[:, : hi - lo])
-            (nc.sync if m == 0 else nc.scalar).dma_start(out[m * P : (m + 1) * P, lo:hi], res[:])
+            nc.scalar.dma_start(out[m * P : (m + 1) * P, lo:hi], res[:])
 
+        third = experts(2, 0, bank(5)[:])
         y[2] = work.tile([P, S], F32, name="y2", tag="codes12", align_bytes=64)
         empty(2, 2, last_group[2])
         empty(2, 0, third)

@@ -25,14 +25,15 @@ M = N // P
 BANK = 512
 GROUPS = ((0, 4), (4, 8), (8, 10))
 FIRST_LOADS = ((0, 384), (384, T))
-SPARE = 64
+SECOND_LOADS = ((0, 448), (448, T))
+SPARE = 256
 NARROW = 3 * T // 4
-SCALAR_EXTRA = 128
+ON_SCALAR = 384
 WIDE = 1024
-GPSIMD_TOKENS = 384
+EARLY_TOKENS = 256
 HALVES = ((0, 256), (256, T))
 THIRDS = ((0, 256), (256, BANK), (BANK, T))
-WARM_UPS = 1
+WARM_UPS = 3
 
 
 def tile_moe_shr_lin_none_kernel(tc, xT, w_words, w_scales, gate, offs, pos1, pos2, out):
@@ -56,8 +57,8 @@ def tile_moe_shr_lin_none_kernel(tc, xT, w_words, w_scales, gate, offs, pos1, po
 
         raw_first = [load_x(0, 0, t0, t1) for t0, t1 in FIRST_LOADS]
         nc.sync.dma_start(offs_t[:], offs)
-        raw_second = [load_x(0, 1, t0, t1) for t0, t1 in FIRST_LOADS]
-        raw1 = placed.tile([P, 4 * T], F32, name="raw1", offset=8192, align_bytes=64)
+        raw_second = [load_x(0, 1, t0, t1) for t0, t1 in SECOND_LOADS]
+        raw1 = work.tile([P, 4 * T], F32, name="raw1", align_bytes=64)
         raw1_rows = raw1[:].rearrange("p (j t) -> p j t", j=4)
         for u in range(2):
             nc.sync.dma_start(raw1_rows[:, 2 * u : 2 * u + 2, :], x_view[1][:, 2 * u : 2 * u + 2, :])
@@ -71,38 +72,45 @@ def tile_moe_shr_lin_none_kernel(tc, xT, w_words, w_scales, gate, offs, pos1, po
             for e in range(e0, e1):
                 ww[e] = words[:, PASSES * (e - e0) : PASSES * (e - e0 + 1), :]
 
-        gates = work.tile([P, 2, T], F32, name="gates")
+        gates = [work.tile([P, T], F32, name=f"gate{c}") for c in range(2)]
         load_w(*GROUPS[0])
-        load_w(*GROUPS[1])
         ws = work.tile([P, (E + 1) * PASSES, N], U8, name="ws", align_bytes=64)
         nc.gpsimd.memset(ws[:].rearrange("p e n -> p (e n)").bitcast(I32), 0)
         s_view = w_scales.rearrange("e a q n -> q (e a) n").bitcast(I32)
         for r in range(4):
             nc.sync.dma_start(ws[r:P:32].bitcast(I32), s_view[r:16:4])
 
-        load_w(GROUPS[2][0], E + 1)
-        nc.sync.dma_start(pos2_t[:], pos2)
         nc.sync.dma_start(pos1_t[:], pos1)
-        nc.sync.dma_start(gates[:], gate[:, :P, :].rearrange("g p t -> p g t"))
+        nc.sync.dma_start(pos2_t[:], pos2)
+        load_w(*GROUPS[1])
+        load_w(*GROUPS[2])
+        nc.sync.dma_start(gates[0][:], gate[0, :P, :])
+        load_w(E, E + 1)
+        nc.sync.dma_start(gates[1][:], gate[1, :P, :])
 
         ident = work.tile([P, P], F32, name="ident")
         make_identity(nc, ident[:])
 
         pairs = work.tile([P, (2 * PASSES * T + SPARE) * 2], BF16, name="pairs", align_bytes=64)
         pair_words = pairs[:].bitcast(U32)
-        nc.gpsimd.memset(pair_words[:, 2 * PASSES * T :], 0)
+        nc.vector.memset(pair_words[:, 2 * PASSES * T :], 0)
         place = {(1, 1): 0, (1, 0): 1, (0, 1): 2, (0, 0): 3}
-        single_rows = [work.tile([P, T], BF16, name=f"single_row{d}", tag=("slots01", "slots00")[d], align_bytes=64) for d in range(2)]
+        single_rows = [placed.tile([P, T], BF16, name=f"single_row{d}", offset=(8192, 16384 - T)[d], align_bytes=64) for d in range(2)]
         tok_scales = work.tile([P, PASSES * T], U8, name="tok_scales", align_bytes=64)
 
         width = [(e1 - e0) * C for e0, e1 in GROUPS]
         cells = [(a, g) for a in range(PASSES) for g in range(len(GROUPS))]
         planes = {
-            (a, g): work.tile([P, 2, width[g]], U32, name=f"planes{a}{g}", tag=f"planes{a}{g}", align_bytes=64)
+            (a, g): placed.tile([P, 2, width[g]], U32, name=f"planes{a}{g}", offset=0, align_bytes=64)
             for a, g in cells
-            if (a, g) not in ((1, 0), (1, 2))
+            if (a, g) == (1, 0)
         }
-        planes[1, 0] = placed.tile([P, 2, width[0]], U32, name="planes10", offset=0, align_bytes=64)
+        planes = {cell: tile[:] for cell, tile in planes.items()}
+        row = work.tile([P, 3 * S], U32, name="row", tag="row", align_bytes=64)
+        rows3 = row[:].rearrange("p (u s) -> p u s", u=3)
+        for g, (e0, e1) in enumerate(GROUPS):
+            planes[0, g] = rows3[:, :2, e0 * C : e1 * C]
+        planes[1, 1] = rows3[:, :0:-1, : width[1]]
         slots = {
             (a, g): work.tile([P, width[g] * 4], BF16, name=f"slots{a}{g}", tag=f"slots{a}{g}", align_bytes=64)
             for a, g in ((0, 2), (1, 0), (1, 1))
@@ -121,21 +129,16 @@ def tile_moe_shr_lin_none_kernel(tc, xT, w_words, w_scales, gate, offs, pos1, po
         def copy_on_gpsimd(out, in_):
             nc.gpsimd.tensor_scalar(out, in_, 1.0, 0.0, MULT, ADD)
 
-        def gather(a, u, g, s0, s1):
+        def gather(dst, a, u, s0, s1):
             start = place[a, u] * T
-            lo = GROUPS[g][0] * C
             window = pair_words[:, start : start + (T if s1 - s0 <= NARROW else T + SPARE if (a, u) == (0, 0) else 2 * T)]
-            nc.vector.tensor_copy(planes[a, g][:, u, s0:s1], window.indirect(offs_t[:, (lo + s0) // 16 : (lo + s1) // 16]))
+            nc.vector.tensor_copy(dst, window.indirect(offs_t[:, s0 // 16 : s1 // 16]))
 
-        def gather_on_scalar(g, s0, s1):
-            lo = GROUPS[g][0] * C
-            dst = planes[0, g][:, 1, :].bitcast(BF16).rearrange("p (s d) -> p s d", d=2)
-            for d in range(2):
-                window = single_rows[d][:].indirect(offs_t[:, (lo + s0) // 16 : (lo + s1) // 16])
-                nc.scalar.activation(dst[:, s0:s1, d], window, COPY)
+        def gather_group(u, g):
+            gather(planes[1, g][:, u, :], 1, u, GROUPS[g][0] * C, GROUPS[g][1] * C)
 
         def weave(copy, dtype, a, g):
-            src = planes[a, g][:].bitcast(dtype).rearrange("p u s -> p s u")
+            src = planes[a, g].rearrange("p u s -> p s u")
             dst = slots[a, g][:].bitcast(dtype).rearrange("p (s u) -> p s u", u=2)
             copy(out=dst, in_=src)
 
@@ -171,35 +174,35 @@ def tile_moe_shr_lin_none_kernel(tc, xT, w_words, w_scales, gate, offs, pos1, po
 
         for (t0, t1), rows in zip(FIRST_LOADS, raw_first):
             round_pairs(nc.vector.tensor_copy, 0, 0, rows[:], t0, t1)
-        for (t0, t1), rows in zip(FIRST_LOADS, raw_second):
+        for (t0, t1), rows in zip(SECOND_LOADS, raw_second):
             round_pairs(nc.scalar.copy, 0, 1, rows[:], t0, t1)
         for d in range(2):
-            for (t0, t1), rows in zip(FIRST_LOADS, raw_second):
+            for (t0, t1), rows in zip(SECOND_LOADS, raw_second):
                 copy_on_gpsimd(single_rows[d][:, t0:t1], rows[:, d, :])
         for u in range(2):
             round_pairs(copy_on_gpsimd, 1, u, raw1_rows[:, 2 * u : 2 * u + 2, :], 0, T)
-        tokens = work.tile([P, PASSES * T * 4], BF16, name="tokens", align_bytes=64)
-        copy_on_gpsimd(
-            tokens[:, 4 * T : 4 * (T + GPSIMD_TOKENS)].rearrange("p (t j) -> p t j", j=4),
-            raw1_rows[:, :, :GPSIMD_TOKENS].rearrange("p j t -> p t j"),
-        )
-        for a in range(PASSES):
-            codes[a, 0] = placed.tile([P, width[0]], U32, name=f"codes{a}0", offset=8192 + 4 * width[0] * a, align_bytes=64)[:]
 
-        for g in range(len(GROUPS)):
-            gather(0, 0, g, 0, width[g])
-        gather(0, 1, 0, 0, width[0])
-        gather(0, 1, 1, 0, width[1] - SCALAR_EXTRA)
-        gather_on_scalar(2, 0, width[2])
-        gather_on_scalar(1, width[1] - SCALAR_EXTRA, width[1])
+        for s0 in (0, S // 2):
+            gather(row[:, s0 : s0 + S // 2], 0, 0, s0, s0 + S // 2)
+        gather(row[:, S : 2 * S - ON_SCALAR], 0, 1, 0, S - ON_SCALAR)
+        scalar_share = row[:, 2 * S - ON_SCALAR : 2 * S].bitcast(BF16).rearrange("p (s d) -> p s d", d=2)
+        for d in range(2):
+            nc.scalar.activation(scalar_share[:, :, d], single_rows[d][:].indirect(offs_t[:, (S - ON_SCALAR) // 16 :]), COPY)
+        tokens = placed.tile([P, PASSES * T * 4], BF16, name="tokens", offset=16384, align_bytes=64)
+        copy_on_gpsimd(
+            tokens[:, 4 * WIDE :].rearrange("p (t j) -> p t j", j=4),
+            raw1_rows[:, :, WIDE - T :].rearrange("p j t -> p t j"),
+        )
+
         for g in range(2):
-            slots[0, g] = work.tile([P, width[g] * 4], BF16, name=f"slots0{g}", tag=f"slots0{g}", align_bytes=64)
-        for g in (0, 1, 2):
+            slots[0, g] = placed.tile([P, width[g] * 4], BF16, name=f"slots0{g}", offset=(12288, 8192)[g], align_bytes=64)
+        for g in (2, 1, 0):
             weave(nc.scalar.copy, U32, 0, g)
 
         for g in range(2):
-            gather(1, 0, g, 0, width[g])
-        gather(1, 1, 0, 0, width[0])
+            gather_group(0, g)
+        gather_group(1, 0)
+        codes[0, 0] = work.tile([P, width[0]], U32, name="codes00", align_bytes=64)[:]
         quantize_slots(0, 0)
         unread = bank(7)
         for i in range(WARM_UPS):
@@ -212,14 +215,16 @@ def tile_moe_shr_lin_none_kernel(tc, xT, w_words, w_scales, gate, offs, pos1, po
                 start=True,
                 stop=True,
             )
-        gather(1, 1, 1, 0, width[1])
+        gather_group(1, 1)
+        weave_tokens(tokens[:, 4 * T : 4 * (T + EARLY_TOKENS)], 1, 0, EARLY_TOKENS)
         weave(nc.scalar.copy, U32, 1, 0)
+        weave_tokens(tokens[:, : 4 * 256], 0, 0, 256)
         weave(nc.scalar.copy, U32, 1, 1)
-        weave_tokens(tokens[:, : 4 * T], 0, 0, T)
+        weave_tokens(tokens[:, 4 * 256 : 4 * T], 0, 256, T)
         quantize_slots(1, 0)
-        codes[0, 1] = placed.tile([P, width[1]], U32, name="codes01", offset=8192 + 4096, align_bytes=64)[:]
+        codes[0, 1] = placed.tile([P, width[1]], U32, name="codes01", offset=0, align_bytes=64)[:]
 
-        y = {0: work.tile([P, S], F32, name="y0", align_bytes=64)}
+        y = {0: work.tile([P, S], F32, name="y0", tag="y0", align_bytes=64)}
 
         def empty(m, g, src):
             nc.scalar.copy(out=y[m][:, GROUPS[g][0] * C : GROUPS[g][1] * C], in_=src)
@@ -228,18 +233,19 @@ def tile_moe_shr_lin_none_kernel(tc, xT, w_words, w_scales, gate, offs, pos1, po
         halves = [bank(i) for i in (3, 2)]
         experts(1, 0, halves[0][:], range(2, 4))
         experts(1, 0, halves[1][:], range(0, 2))
+        third = experts(2, 0, bank(5)[:])
 
-        planes[1, 2] = placed.tile([P, 2, width[2]], U32, name="planes12", offset=8192 + 6144, align_bytes=64)
+        planes[1, 2] = placed.tile([P, 2, width[2]], U32, name="planes12", offset=2048, align_bytes=64)[:]
         for u in range(2):
-            gather(1, u, 2, 0, width[2])
+            gather_group(u, 2)
         slots[1, 2] = work.tile([P, width[2] * 4], BF16, name="slots12", align_bytes=64)
         weave(nc.scalar.copy, U32, 1, 2)
-        weave_tokens(tokens[:, 4 * (T + GPSIMD_TOKENS) :], 1, GPSIMD_TOKENS, T)
-        codes[0, 2] = work.tile([P, width[2]], U32, name="codes02", tag="planes11", align_bytes=64)[:]
+        weave_tokens(tokens[:, 4 * (T + EARLY_TOKENS) : 4 * WIDE], 1, EARLY_TOKENS, WIDE - T)
+        codes[0, 2] = work.tile([P, width[2]], U32, name="codes02", tag="row", align_bytes=64)[:]
         for a, g in ((0, 1), (1, 1), (0, 2), (1, 2)):
             quantize_slots(a, g)
-        tok_codes = placed.tile([P, PASSES * T], U32, name="tok_codes", offset=8192 + 6144, align_bytes=64)
-        for lo, hi in ((0, WIDE), (WIDE, PASSES * T)):
+        tok_codes = placed.tile([P, PASSES * T], U32, name="tok_codes", offset=2048, align_bytes=64)
+        for lo, hi in ((WIDE, PASSES * T), (0, WIDE)):
             nc.vector.quantize_mx(out=tok_codes[:, lo:hi].bitcast(FP8X4), scales=tok_scales[:, lo:hi], in_=tokens[:, 4 * lo : 4 * hi])
 
         empty(0, 0, first_group[0])
@@ -250,10 +256,10 @@ def tile_moe_shr_lin_none_kernel(tc, xT, w_words, w_scales, gate, offs, pos1, po
         y[1] = work.tile([P, S], F32, name="y1", align_bytes=64)
         for half, lo in zip(halves, (2, 0)):
             nc.scalar.copy(out=y[1][:, lo * C : (lo + 2) * C], in_=half[:, lo * C : (lo + 2) * C])
-        empty(1, 1, experts(1, 1, bank(1)[:]))
         last_bank = bank(7)
         last_group = {m: experts(m, 2, last_bank[:, (m - 1) * width[2] : m * width[2]]) for m in (1, 2)}
         empty(1, 2, last_group[1])
+        empty(1, 1, experts(1, 1, bank(1)[:]))
 
         shared = work.tile([P, M - 1, T], F32, name="shared")
 
@@ -268,10 +274,10 @@ def tile_moe_shr_lin_none_kernel(tc, xT, w_words, w_scales, gate, offs, pos1, po
             shared_expert(tails[:, m * P : (m + 1) * P], m, BANK, T)
         nc.scalar.copy(out=shared[:, :, BANK:], in_=tails[:, : (M - 1) * P].rearrange("p (m t) -> p m t", m=M - 1))
 
-        first = [work.tile([P, T], F32, name=f"first{m}") for m in range(M)]
+        first = {m: work.tile([P, T], F32, name=f"first{m}") for m in (0, 2)}
 
         def gate_of(choice, lo, hi):
-            return gates[:, choice, lo:hi]
+            return gates[choice][:, lo:hi]
 
         def pick1(m, lo, hi):
             window = y[m][:].indirect(pos1_t[:, lo // 16 : hi // 16])
@@ -287,9 +293,9 @@ def tile_moe_shr_lin_none_kernel(tc, xT, w_words, w_scales, gate, offs, pos1, po
         def sum_turned(m, lo, hi, second, i):
             acc = bank(i)
             for t in range(lo, hi, P):
-                terms = [shared[:, m, t : t + P], first[m][:, t : t + P]]
-                if second is not None:
-                    terms.append(second[:, t - lo : t - lo + P])
+                terms = [shared[:, m, t : t + P], first[m][:, t : t + P], second[:, t - lo : t - lo + P]]
+                if m == 1:
+                    terms = [terms[0], terms[2], terms[1]]
                 for n, term in enumerate(terms):
                     nc.tensor.matmul(
                         acc[:, t - lo : t - lo + P], term, ident[:], start=(n == 0), stop=(n == len(terms) - 1), is_transpose=True
@@ -306,25 +312,28 @@ def tile_moe_shr_lin_none_kernel(tc, xT, w_words, w_scales, gate, offs, pos1, po
             nc.scalar.copy(out=res[:], in_=back[:, : hi - lo])
             nc.scalar.dma_start(out[m * P : (m + 1) * P, lo:hi], res[:])
 
-        third = experts(2, 0, bank(5)[:])
         y[2] = work.tile([P, S], F32, name="y2", tag="codes12", align_bytes=64)
         empty(2, 2, last_group[2])
         empty(2, 0, third)
         fourth = experts(2, 1, bank(6)[:])
         nc.scalar.copy(out=shared[:, 1, :BANK], in_=shared_expert(bank(1)[:], 1, 0, BANK))
         turned = []
+        pick1(0, 0, T)
         for (lo, hi), i in zip(HALVES, (3, 0)):
-            pick1(0, lo, hi)
             turned.append(sum_turned(0, lo, hi, pick2(0, lo, hi), i))
             if lo == 0:
                 empty(2, 1, fourth)
         head2 = shared_expert(bank(3)[:], 2, 0, BANK)
-        for (lo, hi), part, i in zip(HALVES, turned, (7, 2)):
+        for (lo, hi), part, i in zip(HALVES, turned, (7, 5)):
             turn_back(0, lo, hi, part, i)
 
-        pick1(1, 0, T)
-        turned = [sum_turned(1, lo, hi, pick2(1, lo, hi), i) for (lo, hi), i in zip(THIRDS, (0, 7, 2))]
-        for (lo, hi), part, i in zip(THIRDS, turned, (5, 6, 1)):
+        second1 = pick2(1, 0, T)
+        first[1] = work.tile([P, T], F32, name="first1", tag="y0", align_bytes=64)
+        turned = []
+        for (lo, hi), i in zip(THIRDS, (0, 7, 5)):
+            pick1(1, lo, hi)
+            turned.append(sum_turned(1, lo, hi, second1[:, lo:hi], i))
+        for (lo, hi), part, i in zip(THIRDS, turned, (2, 6, 1)):
             turn_back(1, lo, hi, part, i)
 
         pick1(2, 0, T)

@@ -26,7 +26,7 @@ BANK = 512
 GROUPS = ((0, 4), (4, 8), (8, 10))
 FIRST_LOADS = ((0, 384), (384, T))
 SECOND_LOADS = ((0, 448), (448, T))
-SPARE = 256
+SPARE = 1152
 NARROW = 3 * T // 4
 ON_SCALAR = 384
 WIDE = 1024
@@ -172,8 +172,10 @@ def tile_moe_shr_lin_none_kernel(tc, xT, w_words, w_scales, gate, offs, pos1, po
                     matmul(dst[:, cols], e, a, m, codes[a, g][:, cols], scales[a, g][:, cols])
             return dst
 
-        for (t0, t1), rows in zip(FIRST_LOADS, raw_first):
-            round_pairs(nc.vector.tensor_copy, 0, 0, rows[:], t0, t1)
+        (t0, t1), (t2, t3) = FIRST_LOADS
+        round_pairs(nc.vector.tensor_copy, 0, 0, raw_first[0][:], t0, t1)
+        round_pairs(nc.vector.tensor_copy, 0, 0, raw_first[1][:, :, :160], t2, t2 + 160)
+        round_pairs(nc.scalar.copy, 0, 0, raw_first[1][:, :, 160:], t2 + 160, t3)
         for (t0, t1), rows in zip(SECOND_LOADS, raw_second):
             round_pairs(nc.scalar.copy, 0, 1, rows[:], t0, t1)
         for d in range(2):
@@ -182,8 +184,7 @@ def tile_moe_shr_lin_none_kernel(tc, xT, w_words, w_scales, gate, offs, pos1, po
         for u in range(2):
             round_pairs(copy_on_gpsimd, 1, u, raw1_rows[:, 2 * u : 2 * u + 2, :], 0, T)
 
-        for s0 in (0, S // 2):
-            gather(row[:, s0 : s0 + S // 2], 0, 0, s0, s0 + S // 2)
+        gather(row[:, :S], 0, 0, 0, S)
         gather(row[:, S : 2 * S - ON_SCALAR], 0, 1, 0, S - ON_SCALAR)
         scalar_share = row[:, 2 * S - ON_SCALAR : 2 * S].bitcast(BF16).rearrange("p (s d) -> p s d", d=2)
         for d in range(2):
@@ -317,23 +318,27 @@ def tile_moe_shr_lin_none_kernel(tc, xT, w_words, w_scales, gate, offs, pos1, po
         empty(2, 0, third)
         fourth = experts(2, 1, bank(6)[:])
         nc.scalar.copy(out=shared[:, 1, :BANK], in_=shared_expert(bank(1)[:], 1, 0, BANK))
-        turned = []
+        head2 = shared_expert(bank(0)[:], 2, 0, BANK)
+        low, middle, high = THIRDS
         pick1(0, 0, T)
-        for (lo, hi), i in zip(HALVES, (3, 0)):
-            turned.append(sum_turned(0, lo, hi, pick2(0, lo, hi), i))
-            if lo == 0:
-                empty(2, 1, fourth)
-        head2 = shared_expert(bank(3)[:], 2, 0, BANK)
-        for (lo, hi), part, i in zip(HALVES, turned, (7, 5)):
-            turn_back(0, lo, hi, part, i)
+        second0 = pick2(0, 0, T)
+        turned0 = [sum_turned(0, *HALVES[0], second0[:, : HALVES[0][1]], 2)]
+        empty(2, 1, fourth)
+        turned0.append(sum_turned(0, *HALVES[1], second0[:, HALVES[1][0] :], 3))
 
         second1 = pick2(1, 0, T)
         first[1] = work.tile([P, T], F32, name="first1", tag="y0", align_bytes=64)
-        turned = []
-        for (lo, hi), i in zip(THIRDS, (0, 7, 5)):
+
+        def block1(lo, hi, i):
             pick1(1, lo, hi)
-            turned.append(sum_turned(1, lo, hi, second1[:, lo:hi], i))
-        for (lo, hi), part, i in zip(THIRDS, turned, (2, 6, 1)):
+            return sum_turned(1, lo, hi, second1[:, lo:hi], i)
+
+        turn_back(0, *HALVES[0], turned0[0], 5)
+        turned1 = [block1(*low, 2)]
+        turn_back(0, *HALVES[1], turned0[1], 7)
+        turned1.append(block1(*middle, 3))
+        turned1.append(block1(*high, 5))
+        for (lo, hi), part, i in zip(THIRDS, turned1, (6, 1, 7)):
             turn_back(1, lo, hi, part, i)
 
         pick1(2, 0, T)
@@ -344,12 +349,11 @@ def tile_moe_shr_lin_none_kernel(tc, xT, w_words, w_scales, gate, offs, pos1, po
             nc.vector.tensor_tensor(res[:], partial[:, lo:hi], second, ADD)
             nc.sync.dma_start(out[2 * P :, lo:hi], res[:])
 
-        low, middle, high = THIRDS
-        second_high = pick2(2, *high)
-        nc.vector.tensor_tensor(partial[:, BANK:], tails[:, 2 * P : 3 * P], first[2][:, BANK:], ADD)
-        second_middle = pick2(2, *middle)
-        finish(*high, second_high)
-        nc.vector.tensor_tensor(partial[:, :BANK], head2, first[2][:, :BANK], ADD)
         second_low = pick2(2, *low)
-        finish(*middle, second_middle)
+        nc.vector.tensor_tensor(partial[:, :BANK], head2, first[2][:, :BANK], ADD)
+        second_middle = pick2(2, *middle)
         finish(*low, second_low)
+        nc.vector.tensor_tensor(partial[:, BANK:], tails[:, 2 * P : 3 * P], first[2][:, BANK:], ADD)
+        second_high = pick2(2, *high)
+        finish(*middle, second_middle)
+        finish(*high, second_high)

@@ -25,8 +25,8 @@ M = N // P
 BANK = 512
 GROUPS = ((0, 4), (4, 8), (8, 10))
 FIRST_LOADS = ((0, 384), (384, T))
-SECOND_LOADS = ((0, 448), (448, T))
-SPARE = 1152
+SECOND_LOADS = ((0, 384), (384, T))
+SPARE = 224
 NARROW = 3 * T // 4
 ON_SCALAR = 384
 WIDE = 1024
@@ -75,7 +75,9 @@ def tile_moe_shr_lin_none_kernel(tc, xT, w_words, w_scales, gate, offs, pos1, po
         gates = [work.tile([P, T], F32, name=f"gate{c}") for c in range(2)]
         load_w(*GROUPS[0])
         ws = work.tile([P, (E + 1) * PASSES, N], U8, name="ws", align_bytes=64)
-        nc.gpsimd.memset(ws[:].rearrange("p e n -> p (e n)").bitcast(I32), 0)
+        ws_words = ws[:].rearrange("p e n -> p (e n)").bitcast(I32)
+        nc.vector.memset(ws_words[:, : (E + 1) * N // 3], 0)
+        nc.gpsimd.memset(ws_words[:, (E + 1) * N // 3 :], 0)
         s_view = w_scales.rearrange("e a q n -> q (e a) n").bitcast(I32)
         for r in range(4):
             nc.sync.dma_start(ws[r:P:32].bitcast(I32), s_view[r:16:4])
@@ -95,7 +97,8 @@ def tile_moe_shr_lin_none_kernel(tc, xT, w_words, w_scales, gate, offs, pos1, po
         pair_words = pairs[:].bitcast(U32)
         nc.vector.memset(pair_words[:, 2 * PASSES * T :], 0)
         place = {(1, 1): 0, (1, 0): 1, (0, 1): 2, (0, 0): 3}
-        single_rows = [placed.tile([P, T], BF16, name=f"single_row{d}", offset=(8192, 16384 - T)[d], align_bytes=64) for d in range(2)]
+        single_rows = placed.tile([P, 2 * T], BF16, name="single_rows", offset=16384 - 2 * T, align_bytes=64)
+        single_view = single_rows[:].rearrange("p (d t) -> p d t", d=2)
         tok_scales = work.tile([P, PASSES * T], U8, name="tok_scales", align_bytes=64)
 
         width = [(e1 - e0) * C for e0, e1 in GROUPS]
@@ -150,15 +153,15 @@ def tile_moe_shr_lin_none_kernel(tc, xT, w_words, w_scales, gate, offs, pos1, po
         def quantize_slots(a, g):
             nc.vector.quantize_mx(out=codes[a, g].bitcast(FP8X4), scales=scales[a, g][:], in_=slots[a, g][:])
 
-        def matmul(dst, e, a, m, rhs, rhs_scale):
+        def matmul(dst, e, a, m, rhs, rhs_scale, start=True, stop=True):
             nc.tensor.matmul_mx(
                 out=dst,
                 lhsT=ww[e][:, a, 2 * m * P : 2 * (m + 1) * P].bitcast(FP4X4),
                 lhsT_scale=ws[:, PASSES * e + a, m * P : (m + 1) * P],
                 rhs=rhs.bitcast(FP8X4),
                 rhs_scale=rhs_scale,
-                start=(a == 0),
-                stop=(a == PASSES - 1),
+                start=start and a == 0,
+                stop=stop and a == PASSES - 1,
             )
 
         def bank(i):
@@ -166,10 +169,11 @@ def tile_moe_shr_lin_none_kernel(tc, xT, w_words, w_scales, gate, offs, pos1, po
 
         def experts(m, g, dst, part=None):
             e0, e1 = GROUPS[g]
-            for e in part or range(e0, e1):
-                cols = slice((e - e0) * C, (e - e0 + 1) * C)
-                for a in range(PASSES):
-                    matmul(dst[:, cols], e, a, m, codes[a, g][:, cols], scales[a, g][:, cols])
+            these = part or range(e0, e1)
+            for a in range(PASSES):
+                for e in these:
+                    cols = slice((e - e0) * C, (e - e0 + 1) * C)
+                    matmul(dst[:, cols], e, a, m, codes[a, g][:, cols], scales[a, g][:, cols], e == these[0], e == these[-1])
             return dst
 
         (t0, t1), (t2, t3) = FIRST_LOADS
@@ -177,18 +181,17 @@ def tile_moe_shr_lin_none_kernel(tc, xT, w_words, w_scales, gate, offs, pos1, po
         round_pairs(nc.vector.tensor_copy, 0, 0, raw_first[1][:, :, :160], t2, t2 + 160)
         round_pairs(nc.scalar.copy, 0, 0, raw_first[1][:, :, 160:], t2 + 160, t3)
         for (t0, t1), rows in zip(SECOND_LOADS, raw_second):
-            round_pairs(nc.scalar.copy, 0, 1, rows[:], t0, t1)
-        for d in range(2):
-            for (t0, t1), rows in zip(SECOND_LOADS, raw_second):
-                copy_on_gpsimd(single_rows[d][:, t0:t1], rows[:, d, :])
+            round_pairs(copy_on_gpsimd, 0, 1, rows[:], t0, t1)
+            nc.scalar.copy(out=single_view[:, :, t0:t1], in_=rows[:])
         for u in range(2):
             round_pairs(copy_on_gpsimd, 1, u, raw1_rows[:, 2 * u : 2 * u + 2, :], 0, T)
 
-        gather(row[:, :S], 0, 0, 0, S)
+        for s0 in (0, T):
+            gather(row[:, s0 : s0 + T], 0, 0, s0, s0 + T)
         gather(row[:, S : 2 * S - ON_SCALAR], 0, 1, 0, S - ON_SCALAR)
         scalar_share = row[:, 2 * S - ON_SCALAR : 2 * S].bitcast(BF16).rearrange("p (s d) -> p s d", d=2)
         for d in range(2):
-            nc.scalar.activation(scalar_share[:, :, d], single_rows[d][:].indirect(offs_t[:, (S - ON_SCALAR) // 16 :]), COPY)
+            nc.scalar.activation(scalar_share[:, :, d], single_view[:, d, :].indirect(offs_t[:, (S - ON_SCALAR) // 16 :]), COPY)
         tokens = placed.tile([P, PASSES * T * 4], BF16, name="tokens", offset=16384, align_bytes=64)
         copy_on_gpsimd(
             tokens[:, 4 * WIDE :].rearrange("p (t j) -> p t j", j=4),
@@ -260,7 +263,7 @@ def tile_moe_shr_lin_none_kernel(tc, xT, w_words, w_scales, gate, offs, pos1, po
         last_bank = bank(7)
         last_group = {m: experts(m, 2, last_bank[:, (m - 1) * width[2] : m * width[2]]) for m in (1, 2)}
         empty(1, 2, last_group[1])
-        empty(1, 1, experts(1, 1, bank(1)[:]))
+        empty(1, 1, experts(1, 1, bank(0)[:]))
 
         shared = work.tile([P, M - 1, T], F32, name="shared")
 
@@ -269,7 +272,7 @@ def tile_moe_shr_lin_none_kernel(tc, xT, w_words, w_scales, gate, offs, pos1, po
                 matmul(dst, E, a, m, tok_codes[:, a * T + lo : a * T + hi], tok_scales[:, a * T + lo : a * T + hi])
             return dst
 
-        nc.scalar.copy(out=shared[:, 0, :BANK], in_=shared_expert(bank(0)[:], 0, 0, BANK))
+        nc.scalar.copy(out=shared[:, 0, :BANK], in_=shared_expert(bank(1)[:], 0, 0, BANK))
         tails = bank(4)
         for m in range(M):
             shared_expert(tails[:, m * P : (m + 1) * P], m, BANK, T)
@@ -293,14 +296,14 @@ def tile_moe_shr_lin_none_kernel(tc, xT, w_words, w_scales, gate, offs, pos1, po
 
         def sum_turned(m, lo, hi, second, i):
             acc = bank(i)
-            for t in range(lo, hi, P):
-                terms = [shared[:, m, t : t + P], first[m][:, t : t + P], second[:, t - lo : t - lo + P]]
-                if m == 1:
-                    terms = [terms[0], terms[2], terms[1]]
-                for n, term in enumerate(terms):
-                    nc.tensor.matmul(
-                        acc[:, t - lo : t - lo + P], term, ident[:], start=(n == 0), stop=(n == len(terms) - 1), is_transpose=True
-                    )
+            terms = [shared[:, m, lo:hi], first[m][:, lo:hi], second]
+            if m == 1:
+                terms = [terms[0], terms[2], terms[1]]
+            steps = [(term, t) for term in terms for t in range(0, hi - lo, P)]
+            for n, (term, t) in enumerate(steps):
+                nc.tensor.matmul(
+                    acc[:, t : t + P], term[:, t : t + P], ident[:], start=(n == 0), stop=(n == len(steps) - 1), is_transpose=True
+                )
             turned = work.tile([P, hi - lo], F32, name=f"turned{m}_{lo}")
             nc.scalar.copy(out=turned[:], in_=acc[:, : hi - lo])
             return turned

@@ -24,15 +24,14 @@ PASSES = K // 512
 M = N // P
 BANK = 512
 GROUPS = ((0, 4), (4, 8), (8, 10))
-FIRST_LOADS = ((0, 384), (384, T))
+FIRST_LOADS = ((0, 512), (512, T))
+ON_VECTOR = 352
 SECOND_LOADS = ((0, 384), (384, T))
 SPARE = 224
 NARROW = 3 * T // 4
 ON_SCALAR = 384
 WIDE = 1024
 EARLY_TOKENS = 256
-HALVES = ((0, 256), (256, T))
-THIRDS = ((0, 256), (256, BANK), (BANK, T))
 WARM_UPS = 3
 
 
@@ -177,9 +176,9 @@ def tile_moe_shr_lin_none_kernel(tc, xT, w_words, w_scales, gate, offs, pos1, po
             return dst
 
         (t0, t1), (t2, t3) = FIRST_LOADS
-        round_pairs(nc.vector.tensor_copy, 0, 0, raw_first[0][:], t0, t1)
-        round_pairs(nc.vector.tensor_copy, 0, 0, raw_first[1][:, :, :160], t2, t2 + 160)
-        round_pairs(nc.scalar.copy, 0, 0, raw_first[1][:, :, 160:], t2 + 160, t3)
+        round_pairs(nc.vector.tensor_copy, 0, 0, raw_first[0][:, :, :ON_VECTOR], t0, ON_VECTOR)
+        round_pairs(nc.scalar.copy, 0, 0, raw_first[0][:, :, ON_VECTOR:], ON_VECTOR, t1)
+        round_pairs(nc.vector.tensor_copy, 0, 0, raw_first[1][:], t2, t3)
         for (t0, t1), rows in zip(SECOND_LOADS, raw_second):
             round_pairs(copy_on_gpsimd, 0, 1, rows[:], t0, t1)
             nc.scalar.copy(out=single_view[:, :, t0:t1], in_=rows[:])
@@ -265,98 +264,102 @@ def tile_moe_shr_lin_none_kernel(tc, xT, w_words, w_scales, gate, offs, pos1, po
         empty(1, 2, last_group[1])
         empty(1, 1, experts(1, 1, bank(0)[:]))
 
-        shared = work.tile([P, M - 1, T], F32, name="shared")
+        shared = work.tile([P, M - 1, BANK], F32, name="shared")
+        shared_ends = work.tile([P, M * P], F32, name="shared_ends")
 
         def shared_expert(dst, m, lo, hi):
             for a in range(PASSES):
                 matmul(dst, E, a, m, tok_codes[:, a * T + lo : a * T + hi], tok_scales[:, a * T + lo : a * T + hi])
             return dst
 
-        nc.scalar.copy(out=shared[:, 0, :BANK], in_=shared_expert(bank(1)[:], 0, 0, BANK))
-        tails = bank(4)
-        for m in range(M):
-            shared_expert(tails[:, m * P : (m + 1) * P], m, BANK, T)
-        nc.scalar.copy(out=shared[:, :, BANK:], in_=tails[:, : (M - 1) * P].rearrange("p (m t) -> p m t", m=M - 1))
+        nc.scalar.copy(out=shared[:, 0, :], in_=shared_expert(bank(1)[:], 0, 0, BANK))
+        ends = bank(4)
+        for m, lo in enumerate((BANK, BANK, 0)):
+            shared_expert(ends[:, m * P : (m + 1) * P], m, lo, lo + P)
+        nc.scalar.copy(out=shared_ends[:], in_=ends[:, : M * P])
 
         first = {m: work.tile([P, T], F32, name=f"first{m}") for m in (0, 2)}
+        second = {m: work.tile([P, T], F32, name=f"second{m}") for m in range(M)}
+        result = work.tile([P, (M - 1) * T + P], F32, name="result")
 
-        def gate_of(choice, lo, hi):
-            return gates[choice][:, lo:hi]
+        def pick(choice, m, lo, hi):
+            dst, pos_t = ((first, pos1_t), (second, pos2_t))[choice]
+            window = y[m][:].indirect(pos_t[:, lo // 16 : hi // 16])
+            nc.vector.tensor_tensor(dst[m][:, lo:hi], window, gates[choice][:, lo:hi], MULT)
 
-        def pick1(m, lo, hi):
-            window = y[m][:].indirect(pos1_t[:, lo // 16 : hi // 16])
-            nc.vector.tensor_tensor(first[m][:, lo:hi], window, gate_of(0, lo, hi), MULT)
+        def shared_of(m, t):
+            return shared[:, m, t : t + P] if m < M - 1 and t < BANK else shared_ends[:, m * P : (m + 1) * P]
 
-        def pick2(m, lo, hi, second=None):
-            if second is None:
-                second = work.tile([P, hi - lo], F32, name=f"second{m}_{lo}")[:]
-            window = y[m][:].indirect(pos2_t[:, lo // 16 : hi // 16])
-            nc.vector.tensor_tensor(second, window, gate_of(1, lo, hi), MULT)
-            return second
-
-        def sum_turned(m, lo, hi, second, i):
+        def sum_turned(lo, hi, i):
             acc = bank(i)
-            terms = [shared[:, m, lo:hi], first[m][:, lo:hi], second]
-            if m == 1:
-                terms = [terms[0], terms[2], terms[1]]
-            steps = [(term, t) for term in terms for t in range(0, hi - lo, P)]
-            for n, (term, t) in enumerate(steps):
+            tiles = [divmod(j, T) for j in range(lo, hi, P)]
+            early, late = (first, second) if lo < T else (second, first)
+            steps = [(n, shared_of(m, t)) for n, (m, t) in enumerate(tiles)]
+            for term in (early, late):
+                steps.extend((n, term[m][:, t : t + P]) for n, (m, t) in enumerate(tiles))
+            for s, (n, term) in enumerate(steps):
                 nc.tensor.matmul(
-                    acc[:, t : t + P], term[:, t : t + P], ident[:], start=(n == 0), stop=(n == len(steps) - 1), is_transpose=True
+                    acc[:, n * P : (n + 1) * P], term, ident[:], start=(s == 0), stop=(s == len(steps) - 1), is_transpose=True
                 )
-            turned = work.tile([P, hi - lo], F32, name=f"turned{m}_{lo}")
+            turned = work.tile([P, hi - lo], F32, name=f"turned{lo}")
             nc.scalar.copy(out=turned[:], in_=acc[:, : hi - lo])
             return turned
 
-        def turn_back(m, lo, hi, turned, i):
+        def turn_back(lo, hi, turned, i):
             back = bank(i)
             for t in range(0, hi - lo, P):
                 nc.tensor.transpose(back[:, t : t + P], turned[:, t : t + P], ident[:])
-            res = work.tile([P, hi - lo], F32, name=f"res{m}_{lo}")
-            nc.scalar.copy(out=res[:], in_=back[:, : hi - lo])
-            nc.scalar.dma_start(out[m * P : (m + 1) * P, lo:hi], res[:])
+            nc.scalar.copy(out=result[:, lo:hi], in_=back[:, : hi - lo])
+
+        def store(m, lo, hi):
+            nc.scalar.dma_start(out[m * P : (m + 1) * P, lo:hi], result[:, m * T + lo : m * T + hi])
 
         y[2] = work.tile([P, S], F32, name="y2", tag="codes12", align_bytes=64)
         empty(2, 2, last_group[2])
         empty(2, 0, third)
         fourth = experts(2, 1, bank(6)[:])
-        nc.scalar.copy(out=shared[:, 1, :BANK], in_=shared_expert(bank(1)[:], 1, 0, BANK))
-        head2 = shared_expert(bank(0)[:], 2, 0, BANK)
-        low, middle, high = THIRDS
-        pick1(0, 0, T)
-        second0 = pick2(0, 0, T)
-        turned0 = [sum_turned(0, *HALVES[0], second0[:, : HALVES[0][1]], 2)]
+        nc.scalar.copy(out=shared[:, 1, :], in_=shared_expert(bank(1)[:], 1, 0, BANK))
+        rest2 = shared_expert(bank(0)[:], 2, P, T)
+        pieces = ((0, 256), (256, T), (T, T + 256), (T + 256, T + BANK), (T + BANK, 2 * T + P))
+        pick(0, 0, 0, T)
+        pick(1, 0, 0, T)
+        turned = [sum_turned(*pieces[0], 2)]
         empty(2, 1, fourth)
-        turned0.append(sum_turned(0, *HALVES[1], second0[:, HALVES[1][0] :], 3))
+        turned.append(sum_turned(*pieces[1], 3))
 
-        second1 = pick2(1, 0, T)
+        pick(1, 1, 0, T)
         first[1] = work.tile([P, T], F32, name="first1", tag="y0", align_bytes=64)
+        turn_back(*pieces[0], turned[0], 5)
+        pick(0, 1, 0, 256)
+        turned.append(sum_turned(*pieces[2], 2))
+        turn_back(*pieces[1], turned[1], 7)
+        store(0, 0, T)
+        pick(0, 1, 256, T)
+        turned.append(sum_turned(*pieces[3], 3))
+        pick(1, 2, 0, P)
+        pick(0, 2, 0, P)
+        turn_back(*pieces[2], turned[2], 6)
+        store(1, 0, 256)
+        turned.append(sum_turned(*pieces[4], 5))
+        turn_back(*pieces[3], turned[3], 1)
+        store(1, 256, BANK)
+        turn_back(*pieces[4], turned[4], 7)
+        store(1, BANK, T)
+        store(2, 0, P)
 
-        def block1(lo, hi, i):
-            pick1(1, lo, hi)
-            return sum_turned(1, lo, hi, second1[:, lo:hi], i)
-
-        turn_back(0, *HALVES[0], turned0[0], 5)
-        turned1 = [block1(*low, 2)]
-        turn_back(0, *HALVES[1], turned0[1], 7)
-        turned1.append(block1(*middle, 3))
-        turned1.append(block1(*high, 5))
-        for (lo, hi), part, i in zip(THIRDS, turned1, (6, 1, 7)):
-            turn_back(1, lo, hi, part, i)
-
-        pick1(2, 0, T)
         partial = work.tile([P, T], F32, name="partial")
 
-        def finish(lo, hi, second):
+        def finish(lo, hi):
             res = work.tile([P, hi - lo], F32, name=f"res2_{lo}")
-            nc.vector.tensor_tensor(res[:], partial[:, lo:hi], second, ADD)
+            nc.vector.tensor_tensor(res[:], partial[:, lo:hi], second[2][:, lo:hi], ADD)
             nc.sync.dma_start(out[2 * P :, lo:hi], res[:])
 
-        second_low = pick2(2, *low)
-        nc.vector.tensor_tensor(partial[:, :BANK], head2, first[2][:, :BANK], ADD)
-        second_middle = pick2(2, *middle)
-        finish(*low, second_low)
-        nc.vector.tensor_tensor(partial[:, BANK:], tails[:, 2 * P : 3 * P], first[2][:, BANK:], ADD)
-        second_high = pick2(2, *high)
-        finish(*middle, second_middle)
-        finish(*high, second_high)
+        low, middle, high = (P, 384), (384, BANK), (BANK, T)
+        pick(0, 2, P, T)
+        pick(1, 2, *low)
+        nc.vector.tensor_tensor(partial[:, P:], rest2, first[2][:, P:], ADD)
+        pick(1, 2, *middle)
+        finish(*low)
+        pick(1, 2, *high)
+        finish(*middle)
+        finish(*high)

@@ -265,7 +265,7 @@ def tile_moe_shr_lin_none_kernel(tc, xT, w_words, w_scales, gate, offs, pos1, po
         empty(1, 1, experts(1, 1, bank(0)[:]))
 
         shared = work.tile([P, M - 1, BANK], F32, name="shared")
-        shared_ends = work.tile([P, M * P], F32, name="shared_ends")
+        shared_ends = work.tile([P, (M + 1) * P], F32, name="shared_ends")
 
         def shared_expert(dst, m, lo, hi):
             for a in range(PASSES):
@@ -276,11 +276,11 @@ def tile_moe_shr_lin_none_kernel(tc, xT, w_words, w_scales, gate, offs, pos1, po
         ends = bank(4)
         for m, lo in enumerate((BANK, BANK, 0)):
             shared_expert(ends[:, m * P : (m + 1) * P], m, lo, lo + P)
-        nc.scalar.copy(out=shared_ends[:], in_=ends[:, : M * P])
+        nc.scalar.copy(out=shared_ends[:, : M * P], in_=ends[:, : M * P])
 
-        first = {m: work.tile([P, T], F32, name=f"first{m}") for m in (0, 2)}
-        second = {m: work.tile([P, T], F32, name=f"second{m}") for m in range(M)}
-        result = work.tile([P, (M - 1) * T + P], F32, name="result")
+        first = {0: work.tile([P, T], F32, name="first0")}
+        second = {m: work.tile([P, T], F32, name=f"second{m}") for m in range(M - 1)}
+        result = work.tile([P, (M - 1) * T + 2 * P], F32, name="result")
 
         def pick(choice, m, lo, hi):
             dst, pos_t = ((first, pos1_t), (second, pos2_t))[choice]
@@ -288,7 +288,7 @@ def tile_moe_shr_lin_none_kernel(tc, xT, w_words, w_scales, gate, offs, pos1, po
             nc.vector.tensor_tensor(dst[m][:, lo:hi], window, gates[choice][:, lo:hi], MULT)
 
         def shared_of(m, t):
-            return shared[:, m, t : t + P] if m < M - 1 and t < BANK else shared_ends[:, m * P : (m + 1) * P]
+            return shared[:, m, t : t + P] if m < M - 1 and t < BANK else shared_ends[:, m * P + (t if m == M - 1 else 0) :][:, :P]
 
         def sum_turned(lo, hi, i):
             acc = bank(i)
@@ -319,33 +319,35 @@ def tile_moe_shr_lin_none_kernel(tc, xT, w_words, w_scales, gate, offs, pos1, po
         empty(2, 0, third)
         fourth = experts(2, 1, bank(6)[:])
         nc.scalar.copy(out=shared[:, 1, :], in_=shared_expert(bank(1)[:], 1, 0, BANK))
-        rest2 = shared_expert(bank(0)[:], 2, P, T)
-        pieces = ((0, 256), (256, T), (T, T + 256), (T + 256, T + BANK), (T + BANK, 2 * T + P))
+        pieces = ((0, 256), (256, T), (T, T + 256), (T + 256, 2 * T), (2 * T, 2 * T + 2 * P))
         pick(0, 0, 0, T)
         pick(1, 0, 0, T)
         turned = [sum_turned(*pieces[0], 2)]
         empty(2, 1, fourth)
         turned.append(sum_turned(*pieces[1], 3))
+        rest2 = shared_expert(bank(1)[:], 2, P, T)
 
         pick(1, 1, 0, T)
         first[1] = work.tile([P, T], F32, name="first1", tag="y0", align_bytes=64)
         turn_back(*pieces[0], turned[0], 5)
+        nc.scalar.copy(out=shared_ends[:, M * P :], in_=rest2[:, :P])
         pick(0, 1, 0, 256)
         turned.append(sum_turned(*pieces[2], 2))
         turn_back(*pieces[1], turned[1], 7)
         store(0, 0, T)
         pick(0, 1, 256, T)
         turned.append(sum_turned(*pieces[3], 3))
-        pick(1, 2, 0, P)
-        pick(0, 2, 0, P)
+        first[2] = placed.tile([P, T], F32, name="first2", offset=2048, align_bytes=64)
+        second[2] = placed.tile([P, T], F32, name="second2", offset=2048 + 4 * T, align_bytes=64)
+        pick(1, 2, 0, 2 * P)
+        pick(0, 2, 0, 2 * P)
         turn_back(*pieces[2], turned[2], 6)
         store(1, 0, 256)
         turned.append(sum_turned(*pieces[4], 5))
-        turn_back(*pieces[3], turned[3], 1)
-        store(1, 256, BANK)
+        turn_back(*pieces[3], turned[3], 0)
+        store(1, 256, T)
         turn_back(*pieces[4], turned[4], 7)
-        store(1, BANK, T)
-        store(2, 0, P)
+        store(2, 0, 2 * P)
 
         partial = work.tile([P, T], F32, name="partial")
 
@@ -354,10 +356,10 @@ def tile_moe_shr_lin_none_kernel(tc, xT, w_words, w_scales, gate, offs, pos1, po
             nc.vector.tensor_tensor(res[:], partial[:, lo:hi], second[2][:, lo:hi], ADD)
             nc.sync.dma_start(out[2 * P :, lo:hi], res[:])
 
-        low, middle, high = (P, 384), (384, BANK), (BANK, T)
-        pick(0, 2, P, T)
+        low, middle, high = (2 * P, 384), (384, BANK), (BANK, T)
+        pick(0, 2, 2 * P, T)
         pick(1, 2, *low)
-        nc.vector.tensor_tensor(partial[:, P:], rest2, first[2][:, P:], ADD)
+        nc.vector.tensor_tensor(partial[:, 2 * P :], rest2[:, P:], first[2][:, 2 * P :], ADD)
         pick(1, 2, *middle)
         finish(*low)
         pick(1, 2, *high)

@@ -28,11 +28,10 @@ FIRST_LOADS = ((0, 512), (512, T))
 ON_VECTOR = 352
 SECOND_LOADS = ((0, 384), (384, T))
 SPARE = 224
-NARROW = 3 * T // 4
-ON_SCALAR = 384
+ON_SCALAR = 640
 WIDE = 1024
-EARLY_TOKENS = 256
 WARM_UPS = 3
+CUT = 256
 
 
 def tile_moe_shr_lin_none_kernel(tc, xT, w_words, w_scales, gate, offs, pos1, pos2, out):
@@ -40,27 +39,32 @@ def tile_moe_shr_lin_none_kernel(tc, xT, w_words, w_scales, gate, offs, pos1, po
     with ExitStack() as ctx:
         keep = ctx.enter_context(tc.tile_pool(name="keep", bufs=1))
         work = ctx.enter_context(tc.tile_pool(name="work", bufs=1))
-        placed = ctx.enter_context(tc.tile_pool(name="placed", bufs=1))
         psum = ctx.enter_context(tc.psum_pool(name="psum", bufs=1))
+
+        def tile(name, width, dtype, tag=None):
+            return work.tile([P, width], dtype, name=name, tag=tag or name, align_bytes=64)
 
         offs_t = keep.tile([P, S // 16], U16, name="offs_t")
         pos1_t = keep.tile([P, T // 16], U16, name="pos1_t")
         pos2_t = keep.tile([P, T // 16], U16, name="pos2_t")
 
+        arena = tile("arena", 4 * S, U32)
+        planes = {0: tile("planes0", 2 * S, U32)[:], 1: arena[:, : 2 * S]}
+        tokens = arena[:, 2 * S :]
+        raw_last = tokens[:, 2 * T :].bitcast(F32)
+
         x_view = xT.rearrange("(a p j) t -> a p j t", a=PASSES, p=P, j=4)
 
-        def load_x(a, u, t0, t1):
-            rows = work.tile([P, 2, t1 - t0], F32, name=f"raw{a}{u}_{t0}", tag=f"raw{a}{u}_{t0}", align_bytes=64)
-            nc.sync.dma_start(rows[:], x_view[a][:, 2 * u : 2 * u + 2, t0:t1])
+        def load_x(a, u, t0, t1, dst=None):
+            dst = tile(f"raw{a}{u}_{t0}", 2 * (t1 - t0), F32)[:] if dst is None else dst
+            rows = dst.rearrange("p (d t) -> p d t", d=2)
+            nc.sync.dma_start(rows, x_view[a][:, 2 * u : 2 * u + 2, t0:t1])
             return rows
 
         raw_first = [load_x(0, 0, t0, t1) for t0, t1 in FIRST_LOADS]
         nc.sync.dma_start(offs_t[:], offs)
         raw_second = [load_x(0, 1, t0, t1) for t0, t1 in SECOND_LOADS]
-        raw1 = work.tile([P, 4 * T], F32, name="raw1", align_bytes=64)
-        raw1_rows = raw1[:].rearrange("p (j t) -> p j t", j=4)
-        for u in range(2):
-            nc.sync.dma_start(raw1_rows[:, 2 * u : 2 * u + 2, :], x_view[1][:, 2 * u : 2 * u + 2, :])
+        raw_pass1 = [load_x(1, 0, 0, T), load_x(1, 1, 0, T, raw_last)]
 
         w_view = w_words.rearrange("e a p b -> p (e a) b").bitcast(I32)
         ww = {}
@@ -71,7 +75,7 @@ def tile_moe_shr_lin_none_kernel(tc, xT, w_words, w_scales, gate, offs, pos1, po
             for e in range(e0, e1):
                 ww[e] = words[:, PASSES * (e - e0) : PASSES * (e - e0 + 1), :]
 
-        gates = [work.tile([P, T], F32, name=f"gate{c}") for c in range(2)]
+        gates = [tile(f"gate{c}", T, F32) for c in range(2)]
         load_w(*GROUPS[0])
         ws = work.tile([P, (E + 1) * PASSES, N], U8, name="ws", align_bytes=64)
         ws_words = ws[:].rearrange("p e n -> p (e n)").bitcast(I32)
@@ -80,133 +84,108 @@ def tile_moe_shr_lin_none_kernel(tc, xT, w_words, w_scales, gate, offs, pos1, po
         s_view = w_scales.rearrange("e a q n -> q (e a) n").bitcast(I32)
         for r in range(4):
             nc.sync.dma_start(ws[r:P:32].bitcast(I32), s_view[r:16:4])
-
         nc.sync.dma_start(pos1_t[:], pos1)
         nc.sync.dma_start(pos2_t[:], pos2)
-        load_w(*GROUPS[1])
-        load_w(*GROUPS[2])
+        load_w(GROUPS[1][0], E)
         nc.sync.dma_start(gates[0][:], gate[0, :P, :])
         load_w(E, E + 1)
         nc.sync.dma_start(gates[1][:], gate[1, :P, :])
 
-        ident = work.tile([P, P], F32, name="ident")
+        ident = tile("ident", P, F32)
         make_identity(nc, ident[:])
 
-        pairs = work.tile([P, (2 * PASSES * T + SPARE) * 2], BF16, name="pairs", align_bytes=64)
-        pair_words = pairs[:].bitcast(U32)
-        nc.vector.memset(pair_words[:, 2 * PASSES * T :], 0)
-        place = {(1, 1): 0, (1, 0): 1, (0, 1): 2, (0, 0): 3}
-        single_rows = placed.tile([P, 2 * T], BF16, name="single_rows", offset=16384 - 2 * T, align_bytes=64)
-        single_view = single_rows[:].rearrange("p (d t) -> p d t", d=2)
-        tok_scales = work.tile([P, PASSES * T], U8, name="tok_scales", align_bytes=64)
+        pairs = [tile(f"pairs{a}", 2 * T + SPARE, U32) for a in range(PASSES)]
+        singles = tile("singles", 2 * T + SPARE, BF16)
+        for a in range(PASSES):
+            nc.vector.memset(pairs[a][:, 2 * T :], 0)
+        nc.vector.memset(singles[:, 2 * T :].bitcast(U32), 0)
 
-        width = [(e1 - e0) * C for e0, e1 in GROUPS]
-        cells = [(a, g) for a in range(PASSES) for g in range(len(GROUPS))]
-        planes = {
-            (a, g): placed.tile([P, 2, width[g]], U32, name=f"planes{a}{g}", offset=0, align_bytes=64)
-            for a, g in cells
-            if (a, g) == (1, 0)
-        }
-        planes = {cell: tile[:] for cell, tile in planes.items()}
-        row = work.tile([P, 3 * S], U32, name="row", tag="row", align_bytes=64)
-        rows3 = row[:].rearrange("p (u s) -> p u s", u=3)
-        for g, (e0, e1) in enumerate(GROUPS):
-            planes[0, g] = rows3[:, :2, e0 * C : e1 * C]
-        planes[1, 1] = rows3[:, :0:-1, : width[1]]
-        slots = {
-            (a, g): work.tile([P, width[g] * 4], BF16, name=f"slots{a}{g}", tag=f"slots{a}{g}", align_bytes=64)
-            for a, g in ((0, 2), (1, 0), (1, 1))
-        }
-        codes = {
-            (1, g): work.tile([P, width[g]], U32, name=f"codes1{g}", tag=f"codes1{g}", align_bytes=64)[:]
-            for g in range(len(GROUPS))
-        }
-        scales = {(a, g): work.tile([P, width[g]], U8, name=f"scales{a}{g}", align_bytes=64) for a, g in cells}
-
-        def round_pairs(copy, a, u, rows, t0, t1):
-            base = place[a, u] * 2 * T
-            dst = pairs[:, base + 2 * t0 : base + 2 * t1].rearrange("p (t d) -> p t d", d=2)
-            copy(out=dst, in_=rows.rearrange("p d t -> p t d"))
-
-        def copy_on_gpsimd(out, in_):
+        def on_gpsimd(out, in_):
             nc.gpsimd.tensor_scalar(out, in_, 1.0, 0.0, MULT, ADD)
 
-        def gather(dst, a, u, s0, s1):
-            start = place[a, u] * T
-            window = pair_words[:, start : start + (T if s1 - s0 <= NARROW else T + SPARE if (a, u) == (0, 0) else 2 * T)]
-            nc.vector.tensor_copy(dst, window.indirect(offs_t[:, s0 // 16 : s1 // 16]))
+        def round_pairs(copy, a, u, rows, t0, t1):
+            base = (1 - u) * T
+            dst = pairs[a][:, base + t0 : base + t1].bitcast(BF16).rearrange("p (t d) -> p t d", d=2)
+            copy(out=dst, in_=rows.rearrange("p d t -> p t d"))
 
-        def gather_group(u, g):
-            gather(planes[1, g][:, u, :], 1, u, GROUPS[g][0] * C, GROUPS[g][1] * C)
+        def gather(a, u, s0, s1):
+            window = pairs[a][:, : 2 * T] if u else pairs[a][:, T:]
+            nc.vector.tensor_copy(planes[a][:, u * S + s0 : u * S + s1], window.indirect(offs_t[:, s0 // 16 : s1 // 16]))
 
-        def weave(copy, dtype, a, g):
-            src = planes[a, g].rearrange("p u s -> p s u")
-            dst = slots[a, g][:].bitcast(dtype).rearrange("p (s u) -> p s u", u=2)
-            copy(out=dst, in_=src)
+        span = [(e0 * C, e1 * C) for e0, e1 in GROUPS]
+        width = [s1 - s0 for s0, s1 in span]
+        late = tile("late", 2 * (width[1] + width[2]), U32)
+        slots = {
+            (0, 0): arena[:, S + width[0] : S + 3 * width[0]],
+            (0, 1): tile("slots01", 2 * width[1], U32)[:],
+            (0, 2): tile("slots02", 2 * width[2], U32)[:],
+            (1, 0): tile("slots10", 2 * width[0], U32)[:],
+            (1, 1): late[:, : 2 * width[1]],
+            (1, 2): late[:, 2 * width[1] :],
+        }
+        scales = {cell: tile(f"scales{cell[0]}{cell[1]}", width[cell[1]], U8) for cell in slots}
+        codes = {}
 
-        def weave_tokens(dst, a, t0, t1):
-            base = place[a, 1] * T
-            src = pair_words[:, base : base + 2 * T].rearrange("p (u t) -> p t u", u=2)
-            nc.scalar.copy(out=dst.bitcast(U32).rearrange("p (t u) -> p t u", u=2), in_=src[:, t0:t1, ::-1])
+        def weave(a, g):
+            src = planes[a].rearrange("p (u s) -> p s u", u=2)[:, span[g][0] : span[g][1], :]
+            nc.scalar.copy(out=slots[a, g].rearrange("p (s u) -> p s u", u=2), in_=src)
 
-        def quantize_slots(a, g):
-            nc.vector.quantize_mx(out=codes[a, g].bitcast(FP8X4), scales=scales[a, g][:], in_=slots[a, g][:])
+        def weave_tokens(a):
+            src = pairs[a][:, : 2 * T].rearrange("p (u t) -> p t u", u=2)
+            dst = tokens[:, (1 - a) * 2 * T : (2 - a) * 2 * T].rearrange("p (t u) -> p t u", u=2)
+            nc.gpsimd.tensor_copy(out=dst, in_=src[:, :, ::-1])
 
-        def matmul(dst, e, a, m, rhs, rhs_scale, start=True, stop=True):
+        def quantize(a, g):
+            nc.vector.quantize_mx(out=codes[a, g].bitcast(FP8X4), scales=scales[a, g][:], in_=slots[a, g].bitcast(BF16))
+
+        def matmul(dst, e, a, m, rhs, rhs_scale, start, stop):
             nc.tensor.matmul_mx(
                 out=dst,
                 lhsT=ww[e][:, a, 2 * m * P : 2 * (m + 1) * P].bitcast(FP4X4),
                 lhsT_scale=ws[:, PASSES * e + a, m * P : (m + 1) * P],
                 rhs=rhs.bitcast(FP8X4),
                 rhs_scale=rhs_scale,
-                start=start and a == 0,
-                stop=stop and a == PASSES - 1,
+                start=start,
+                stop=stop,
             )
 
         def bank(i):
             return psum.tile([P, BANK], F32, name=f"bank{i}")
 
-        def experts(m, g, dst, part=None):
+        def experts(dst, m, g, a):
             e0, e1 = GROUPS[g]
-            these = part or range(e0, e1)
-            for a in range(PASSES):
-                for e in these:
-                    cols = slice((e - e0) * C, (e - e0 + 1) * C)
-                    matmul(dst[:, cols], e, a, m, codes[a, g][:, cols], scales[a, g][:, cols], e == these[0], e == these[-1])
-            return dst
+            for e in range(e0, e1):
+                cols = slice((e - e0) * C, (e - e0 + 1) * C)
+                matmul(dst[:, cols], e, a, m, codes[a, g][:, cols], scales[a, g][:, cols], (a, e) == (0, e0), (a, e) == (1, e1 - 1))
 
         (t0, t1), (t2, t3) = FIRST_LOADS
         round_pairs(nc.vector.tensor_copy, 0, 0, raw_first[0][:, :, :ON_VECTOR], t0, ON_VECTOR)
         round_pairs(nc.scalar.copy, 0, 0, raw_first[0][:, :, ON_VECTOR:], ON_VECTOR, t1)
-        round_pairs(nc.vector.tensor_copy, 0, 0, raw_first[1][:], t2, t3)
+        round_pairs(nc.vector.tensor_copy, 0, 0, raw_first[1], t2, t3)
+        single_view = singles[:, : 2 * T].rearrange("p (d t) -> p d t", d=2)
         for (t0, t1), rows in zip(SECOND_LOADS, raw_second):
-            round_pairs(copy_on_gpsimd, 0, 1, rows[:], t0, t1)
-            nc.scalar.copy(out=single_view[:, :, t0:t1], in_=rows[:])
+            round_pairs(on_gpsimd, 0, 1, rows, t0, t1)
+            nc.scalar.copy(out=single_view[:, :, t0:t1], in_=rows[:, ::-1, :])
         for u in range(2):
-            round_pairs(copy_on_gpsimd, 1, u, raw1_rows[:, 2 * u : 2 * u + 2, :], 0, T)
+            round_pairs(on_gpsimd, 1, u, raw_pass1[u], 0, T)
 
         for s0 in (0, T):
-            gather(row[:, s0 : s0 + T], 0, 0, s0, s0 + T)
-        gather(row[:, S : 2 * S - ON_SCALAR], 0, 1, 0, S - ON_SCALAR)
-        scalar_share = row[:, 2 * S - ON_SCALAR : 2 * S].bitcast(BF16).rearrange("p (s d) -> p s d", d=2)
+            gather(0, 0, s0, s0 + T)
+        gather(0, 1, 0, S - ON_SCALAR)
+        share = planes[0][:, 2 * S - ON_SCALAR :].bitcast(BF16).rearrange("p (s d) -> p s d", d=2)
         for d in range(2):
-            nc.scalar.activation(scalar_share[:, :, d], single_view[:, d, :].indirect(offs_t[:, (S - ON_SCALAR) // 16 :]), COPY)
-        tokens = placed.tile([P, PASSES * T * 4], BF16, name="tokens", offset=16384, align_bytes=64)
-        copy_on_gpsimd(
-            tokens[:, 4 * WIDE :].rearrange("p (t j) -> p t j", j=4),
-            raw1_rows[:, :, WIDE - T :].rearrange("p j t -> p t j"),
-        )
+            window = singles[:, : 2 * T] if d else singles[:, T:]
+            nc.scalar.activation(share[:, :, d], window.indirect(offs_t[:, (S - ON_SCALAR) // 16 :]), COPY)
+        weave_tokens(0)
+        for g in range(3):
+            weave(0, g)
+        for s0 in (0, T):
+            gather(1, 0, s0, s0 + T)
+        gather(1, 1, *span[0])
+        weave(1, 0)
 
-        for g in range(2):
-            slots[0, g] = placed.tile([P, width[g] * 4], BF16, name=f"slots0{g}", offset=(12288, 8192)[g], align_bytes=64)
-        for g in (2, 1, 0):
-            weave(nc.scalar.copy, U32, 0, g)
-
-        for g in range(2):
-            gather_group(0, g)
-        gather_group(1, 0)
-        codes[0, 0] = work.tile([P, width[0]], U32, name="codes00", align_bytes=64)[:]
-        quantize_slots(0, 0)
+        codes[0, 0] = tile("codes00", width[0], U32, "pairs0")[:]
+        quantize(0, 0)
         unread = bank(7)
         for i in range(WARM_UPS):
             nc.tensor.matmul_mx(
@@ -218,69 +197,64 @@ def tile_moe_shr_lin_none_kernel(tc, xT, w_words, w_scales, gate, offs, pos1, po
                 start=True,
                 stop=True,
             )
-        gather_group(1, 1)
-        weave_tokens(tokens[:, 4 * T : 4 * (T + EARLY_TOKENS)], 1, 0, EARLY_TOKENS)
-        weave(nc.scalar.copy, U32, 1, 0)
-        weave_tokens(tokens[:, : 4 * 256], 0, 0, 256)
-        weave(nc.scalar.copy, U32, 1, 1)
-        weave_tokens(tokens[:, 4 * 256 : 4 * T], 0, 256, T)
-        quantize_slots(1, 0)
-        codes[0, 1] = placed.tile([P, width[1]], U32, name="codes01", offset=0, align_bytes=64)[:]
+        first_group = [bank(m)[:] for m in range(2)]
+        for m in range(2):
+            experts(first_group[m], m, 0, 0)
+        weave_tokens(1)
+        for g in (1, 2):
+            gather(1, 1, *span[g])
+            weave(1, g)
+        held = tile("codes_held", S, U32, "pairs1")
+        codes[1, 0], codes[0, 1], codes[0, 2] = held[:, :512], held[:, 512:1024], held[:, 1024:]
+        for g in (1, 2):
+            codes[1, g] = tile(f"codes1{g}", width[g], U32)[:]
+        for a, g in ((1, 0), (0, 1), (1, 1), (0, 2), (1, 2)):
+            quantize(a, g)
+        tok_codes = tile("tok_codes", PASSES * T, U32, "late")
+        tok_scales = tile("tok_scales", PASSES * T, U8)
+        for lo, hi in ((WIDE, PASSES * T), (0, WIDE)):
+            nc.vector.quantize_mx(out=tok_codes[:, lo:hi].bitcast(FP8X4), scales=tok_scales[:, lo:hi], in_=tokens[:, 2 * lo : 2 * hi].bitcast(BF16))
 
-        y = {0: work.tile([P, S], F32, name="y0", tag="y0", align_bytes=64)}
+        y = [tile(f"y{m}", S, F32) for m in range(M)]
 
         def empty(m, g, src):
-            nc.scalar.copy(out=y[m][:, GROUPS[g][0] * C : GROUPS[g][1] * C], in_=src)
+            nc.scalar.copy(out=y[m][:, span[g][0] : span[g][1]], in_=src)
 
-        first_group = [experts(0, 0, bank(0)[:])]
-        halves = [bank(i) for i in (3, 2)]
-        experts(1, 0, halves[0][:], range(2, 4))
-        experts(1, 0, halves[1][:], range(0, 2))
-        third = experts(2, 0, bank(5)[:])
+        def both_passes(dst, m, g):
+            for a in range(PASSES):
+                experts(dst, m, g, a)
+            return dst
 
-        planes[1, 2] = placed.tile([P, 2, width[2]], U32, name="planes12", offset=2048, align_bytes=64)[:]
-        for u in range(2):
-            gather_group(u, 2)
-        slots[1, 2] = work.tile([P, width[2] * 4], BF16, name="slots12", align_bytes=64)
-        weave(nc.scalar.copy, U32, 1, 2)
-        weave_tokens(tokens[:, 4 * (T + EARLY_TOKENS) : 4 * WIDE], 1, EARLY_TOKENS, WIDE - T)
-        codes[0, 2] = work.tile([P, width[2]], U32, name="codes02", tag="row", align_bytes=64)[:]
-        for a, g in ((0, 1), (1, 1), (0, 2), (1, 2)):
-            quantize_slots(a, g)
-        tok_codes = placed.tile([P, PASSES * T], U32, name="tok_codes", offset=2048, align_bytes=64)
-        for lo, hi in ((WIDE, PASSES * T), (0, WIDE)):
-            nc.vector.quantize_mx(out=tok_codes[:, lo:hi].bitcast(FP8X4), scales=tok_scales[:, lo:hi], in_=tokens[:, 4 * lo : 4 * hi])
-
+        experts(first_group[0], 0, 0, 1)
         empty(0, 0, first_group[0])
-        for half, lo in zip(halves, (0, 2)):
-            experts(0, 1, half[:], range(4 + lo, 6 + lo))
-            nc.scalar.copy(out=y[0][:, (4 + lo) * C : (6 + lo) * C], in_=half[:, lo * C : (lo + 2) * C])
-        empty(0, 2, experts(0, 2, bank(6)[:, : width[2]]))
-        y[1] = work.tile([P, S], F32, name="y1", align_bytes=64)
-        for half, lo in zip(halves, (2, 0)):
-            nc.scalar.copy(out=y[1][:, lo * C : (lo + 2) * C], in_=half[:, lo * C : (lo + 2) * C])
-        last_bank = bank(7)
-        last_group = {m: experts(m, 2, last_bank[:, (m - 1) * width[2] : m * width[2]]) for m in (1, 2)}
+        empty(0, 1, both_passes(bank(3)[:], 0, 1))
+        empty(0, 2, both_passes(bank(4)[:, : width[2]], 0, 2))
+        experts(first_group[1], 1, 0, 1)
+        empty(1, 0, first_group[1])
+        empty(1, 1, both_passes(bank(3)[:], 1, 1))
+        last_bank = bank(6)
+        last_group = {m: both_passes(last_bank[:, (m - 1) * width[2] : m * width[2]], m, 2) for m in (1, 2)}
         empty(1, 2, last_group[1])
-        empty(1, 1, experts(1, 1, bank(0)[:]))
+        empty(2, 0, both_passes(bank(4)[:], 2, 0))
 
         shared = work.tile([P, M - 1, BANK], F32, name="shared")
-        shared_ends = work.tile([P, (M + 1) * P], F32, name="shared_ends")
+        shared_ends = tile("shared_ends", (M + 1) * P, F32)
 
         def shared_expert(dst, m, lo, hi):
             for a in range(PASSES):
-                matmul(dst, E, a, m, tok_codes[:, a * T + lo : a * T + hi], tok_scales[:, a * T + lo : a * T + hi])
+                cols = slice((1 - a) * T + lo, (1 - a) * T + hi)
+                matmul(dst, E, a, m, tok_codes[:, cols], tok_scales[:, cols], a == 0, a == 1)
             return dst
 
         nc.scalar.copy(out=shared[:, 0, :], in_=shared_expert(bank(1)[:], 0, 0, BANK))
-        ends = bank(4)
+        ends = bank(2)
         for m, lo in enumerate((BANK, BANK, 0)):
             shared_expert(ends[:, m * P : (m + 1) * P], m, lo, lo + P)
         nc.scalar.copy(out=shared_ends[:, : M * P], in_=ends[:, : M * P])
 
-        first = {0: work.tile([P, T], F32, name="first0")}
-        second = {m: work.tile([P, T], F32, name=f"second{m}") for m in range(M - 1)}
-        result = work.tile([P, (M - 1) * T + 2 * P], F32, name="result")
+        first = {0: tile("first0", T, F32)}
+        second = {m: tile(f"second{m}", T, F32) for m in range(M - 1)}
+        result = tile("result", (M - 1) * T + CUT, F32)
 
         def pick(choice, m, lo, hi):
             dst, pos_t = ((first, pos1_t), (second, pos2_t))[choice]
@@ -293,15 +267,15 @@ def tile_moe_shr_lin_none_kernel(tc, xT, w_words, w_scales, gate, offs, pos1, po
         def sum_turned(lo, hi, i):
             acc = bank(i)
             tiles = [divmod(j, T) for j in range(lo, hi, P)]
-            early, late = (first, second) if lo < T else (second, first)
+            early, later = (first, second) if lo < T else (second, first)
             steps = [(n, shared_of(m, t)) for n, (m, t) in enumerate(tiles)]
-            for term in (early, late):
+            for term in (early, later):
                 steps.extend((n, term[m][:, t : t + P]) for n, (m, t) in enumerate(tiles))
             for s, (n, term) in enumerate(steps):
                 nc.tensor.matmul(
                     acc[:, n * P : (n + 1) * P], term, ident[:], start=(s == 0), stop=(s == len(steps) - 1), is_transpose=True
                 )
-            turned = work.tile([P, hi - lo], F32, name=f"turned{lo}")
+            turned = tile(f"turned{lo}", hi - lo, F32)
             nc.scalar.copy(out=turned[:], in_=acc[:, : hi - lo])
             return turned
 
@@ -314,52 +288,48 @@ def tile_moe_shr_lin_none_kernel(tc, xT, w_words, w_scales, gate, offs, pos1, po
         def store(m, lo, hi):
             nc.scalar.dma_start(out[m * P : (m + 1) * P, lo:hi], result[:, m * T + lo : m * T + hi])
 
-        y[2] = work.tile([P, S], F32, name="y2", tag="codes12", align_bytes=64)
         empty(2, 2, last_group[2])
-        empty(2, 0, third)
-        fourth = experts(2, 1, bank(6)[:])
+        empty(2, 1, both_passes(bank(3)[:], 2, 1))
         nc.scalar.copy(out=shared[:, 1, :], in_=shared_expert(bank(1)[:], 1, 0, BANK))
-        pieces = ((0, 256), (256, T), (T, T + 256), (T + 256, 2 * T), (2 * T, 2 * T + 2 * P))
+        pieces = ((0, 256), (256, T), (T, T + 256), (T + 256, 2 * T), (2 * T, 2 * T + CUT))
         pick(0, 0, 0, T)
         pick(1, 0, 0, T)
-        turned = [sum_turned(*pieces[0], 2)]
-        empty(2, 1, fourth)
-        turned.append(sum_turned(*pieces[1], 3))
-        rest2 = shared_expert(bank(1)[:], 2, P, T)
+        turned = [sum_turned(*pieces[0], 0), sum_turned(*pieces[1], 5)]
+        rest = shared_expert(bank(1)[:], 2, P, T)
 
         pick(1, 1, 0, T)
-        first[1] = work.tile([P, T], F32, name="first1", tag="y0", align_bytes=64)
-        turn_back(*pieces[0], turned[0], 5)
-        nc.scalar.copy(out=shared_ends[:, M * P :], in_=rest2[:, :P])
+        first[1] = tile("first1", T, F32, "y0")
+        turn_back(*pieces[0], turned[0], 2)
+        nc.scalar.copy(out=shared_ends[:, M * P :], in_=rest[:, :P])
         pick(0, 1, 0, 256)
-        turned.append(sum_turned(*pieces[2], 2))
+        turned.append(sum_turned(*pieces[2], 0))
         turn_back(*pieces[1], turned[1], 7)
         store(0, 0, T)
         pick(0, 1, 256, T)
-        turned.append(sum_turned(*pieces[3], 3))
-        first[2] = placed.tile([P, T], F32, name="first2", offset=2048, align_bytes=64)
-        second[2] = placed.tile([P, T], F32, name="second2", offset=2048 + 4 * T, align_bytes=64)
-        pick(1, 2, 0, 2 * P)
-        pick(0, 2, 0, 2 * P)
+        turned.append(sum_turned(*pieces[3], 5))
+        terms = tile("terms2", 2 * T, F32, "late")
+        first[2], second[2] = terms[:, :T], terms[:, T:]
+        pick(1, 2, 0, CUT)
+        pick(0, 2, 0, CUT)
         turn_back(*pieces[2], turned[2], 6)
         store(1, 0, 256)
-        turned.append(sum_turned(*pieces[4], 5))
-        turn_back(*pieces[3], turned[3], 0)
+        turned.append(sum_turned(*pieces[4], 2))
+        turn_back(*pieces[3], turned[3], 4)
         store(1, 256, T)
         turn_back(*pieces[4], turned[4], 7)
-        store(2, 0, 2 * P)
+        store(2, 0, CUT)
 
-        partial = work.tile([P, T], F32, name="partial")
+        partial = tile("partial", T, F32)
 
         def finish(lo, hi):
-            res = work.tile([P, hi - lo], F32, name=f"res2_{lo}")
+            res = tile(f"res2_{lo}", hi - lo, F32)
             nc.vector.tensor_tensor(res[:], partial[:, lo:hi], second[2][:, lo:hi], ADD)
             nc.sync.dma_start(out[2 * P :, lo:hi], res[:])
 
-        low, middle, high = (2 * P, 384), (384, BANK), (BANK, T)
-        pick(0, 2, 2 * P, T)
+        low, middle, high = (CUT, 384), (384, BANK), (BANK, T)
+        pick(0, 2, CUT, T)
         pick(1, 2, *low)
-        nc.vector.tensor_tensor(partial[:, 2 * P :], rest2[:, P:], first[2][:, 2 * P :], ADD)
+        nc.vector.tensor_tensor(partial[:, CUT:], rest[:, CUT - P :], first[2][:, CUT:], ADD)
         pick(1, 2, *middle)
         finish(*low)
         pick(1, 2, *high)

@@ -29,8 +29,9 @@ ON_VECTOR = 352
 SECOND_LOADS = ((0, 384), (384, T))
 SPARE = 224
 ON_SCALAR = 640
-WIDE = 1024
-WARM_UPS = 3
+LONG_SPARE = 384
+ON_GPSIMD = 320
+WARM_UPS = 2
 CUT = 256
 
 
@@ -39,6 +40,7 @@ def tile_moe_shr_lin_none_kernel(tc, xT, w_words, w_scales, gate, offs, pos1, po
     with ExitStack() as ctx:
         keep = ctx.enter_context(tc.tile_pool(name="keep", bufs=1))
         work = ctx.enter_context(tc.tile_pool(name="work", bufs=1))
+        placed = ctx.enter_context(tc.tile_pool(name="placed", bufs=1))
         psum = ctx.enter_context(tc.psum_pool(name="psum", bufs=1))
 
         def tile(name, width, dtype, tag=None):
@@ -48,10 +50,11 @@ def tile_moe_shr_lin_none_kernel(tc, xT, w_words, w_scales, gate, offs, pos1, po
         pos1_t = keep.tile([P, T // 16], U16, name="pos1_t")
         pos2_t = keep.tile([P, T // 16], U16, name="pos2_t")
 
-        arena = tile("arena", 4 * S, U32)
-        planes = {0: tile("planes0", 2 * S, U32)[:], 1: arena[:, : 2 * S]}
-        tokens = arena[:, 2 * S :]
-        raw_last = tokens[:, 2 * T :].bitcast(F32)
+        def placed_tile(name, width, dtype, offset):
+            return placed.tile([P, width], dtype, name=name, offset=offset, align_bytes=64)
+
+        planes0 = tile("planes0", 2 * S, U32)[:]
+        raw_last = placed_tile("raw_last", 2 * T, F32, 0)[:]
 
         x_view = xT.rearrange("(a p j) t -> a p j t", a=PASSES, p=P, j=4)
 
@@ -86,7 +89,8 @@ def tile_moe_shr_lin_none_kernel(tc, xT, w_words, w_scales, gate, offs, pos1, po
             nc.sync.dma_start(ws[r:P:32].bitcast(I32), s_view[r:16:4])
         nc.sync.dma_start(pos1_t[:], pos1)
         nc.sync.dma_start(pos2_t[:], pos2)
-        load_w(GROUPS[1][0], E)
+        load_w(*GROUPS[1])
+        load_w(*GROUPS[2])
         nc.sync.dma_start(gates[0][:], gate[0, :P, :])
         load_w(E, E + 1)
         nc.sync.dma_start(gates[1][:], gate[1, :P, :])
@@ -94,7 +98,7 @@ def tile_moe_shr_lin_none_kernel(tc, xT, w_words, w_scales, gate, offs, pos1, po
         ident = tile("ident", P, F32)
         make_identity(nc, ident[:])
 
-        pairs = [tile(f"pairs{a}", 2 * T + SPARE, U32) for a in range(PASSES)]
+        pairs = [tile(f"pairs{a}", 2 * T + spare, U32) for a, spare in enumerate((SPARE, LONG_SPARE))]
         singles = tile("singles", 2 * T + SPARE, BF16)
         for a in range(PASSES):
             nc.vector.memset(pairs[a][:, 2 * T :], 0)
@@ -108,35 +112,38 @@ def tile_moe_shr_lin_none_kernel(tc, xT, w_words, w_scales, gate, offs, pos1, po
             dst = pairs[a][:, base + t0 : base + t1].bitcast(BF16).rearrange("p (t d) -> p t d", d=2)
             copy(out=dst, in_=rows.rearrange("p d t -> p t d"))
 
-        def gather(a, u, s0, s1):
+        def gather(dst, a, u, s0, s1):
             window = pairs[a][:, : 2 * T] if u else pairs[a][:, T:]
-            nc.vector.tensor_copy(planes[a][:, u * S + s0 : u * S + s1], window.indirect(offs_t[:, s0 // 16 : s1 // 16]))
+            nc.vector.tensor_copy(dst, window.indirect(offs_t[:, s0 // 16 : s1 // 16]))
 
         span = [(e0 * C, e1 * C) for e0, e1 in GROUPS]
         width = [s1 - s0 for s0, s1 in span]
-        late = tile("late", 2 * (width[1] + width[2]), U32)
-        slots = {
-            (0, 0): arena[:, S + width[0] : S + 3 * width[0]],
-            (0, 1): tile("slots01", 2 * width[1], U32)[:],
-            (0, 2): tile("slots02", 2 * width[2], U32)[:],
-            (1, 0): tile("slots10", 2 * width[0], U32)[:],
-            (1, 1): late[:, : 2 * width[1]],
-            (1, 2): late[:, 2 * width[1] :],
-        }
-        scales = {cell: tile(f"scales{cell[0]}{cell[1]}", width[cell[1]], U8) for cell in slots}
+        last = tile("slots2", 4 * width[2], U32)
+        slots = {(a, g): tile(f"slots{a}{g}", 2 * width[g], U32)[:] for a in range(PASSES) for g in range(2)}
+        scales = {(a, g): tile(f"scales{a}{g}", width[g], U8)[:] for a in range(PASSES) for g in range(2)}
+        last_scales = tile("scales2", 2 * width[2], U8)
+        last_codes = tile("codes2", 2 * width[2], U32)
         codes = {}
+        for a in range(PASSES):
+            slots[a, 2] = last[:, 2 * a * width[2] : 2 * (a + 1) * width[2]]
+            scales[a, 2] = last_scales[:, a * width[2] : (a + 1) * width[2]]
+            codes[a, 2] = last_codes[:, a * width[2] : (a + 1) * width[2]]
+        planes = {(0, g): planes0.rearrange("p (u s) -> p u s", u=2)[:, :, span[g][0] : span[g][1]] for g in range(3)}
+        planes[1, 0] = tile("planes10", 2 * width[0], U32)[:].rearrange("p (u s) -> p u s", u=2)
+        later = tile("planes1", 2 * (S - width[0]), U32)[:].rearrange("p (u s) -> p u s", u=2)
+        planes[1, 1], planes[1, 2] = later[:, :, : width[1]], later[:, :, width[1] :]
+        tokens = {}
 
         def weave(a, g):
-            src = planes[a].rearrange("p (u s) -> p s u", u=2)[:, span[g][0] : span[g][1], :]
-            nc.scalar.copy(out=slots[a, g].rearrange("p (s u) -> p s u", u=2), in_=src)
+            nc.scalar.copy(out=slots[a, g].rearrange("p (s u) -> p s u", u=2), in_=planes[a, g].rearrange("p u s -> p s u"))
 
-        def weave_tokens(a):
+        def weave_tokens(copy, a, t0, t1):
             src = pairs[a][:, : 2 * T].rearrange("p (u t) -> p t u", u=2)
-            dst = tokens[:, (1 - a) * 2 * T : (2 - a) * 2 * T].rearrange("p (t u) -> p t u", u=2)
-            nc.gpsimd.tensor_copy(out=dst, in_=src[:, :, ::-1])
+            dst = tokens[a].rearrange("p (t u) -> p t u", u=2)
+            copy(out=dst[:, t0:t1, :], in_=src[:, t0:t1, ::-1])
 
         def quantize(a, g):
-            nc.vector.quantize_mx(out=codes[a, g].bitcast(FP8X4), scales=scales[a, g][:], in_=slots[a, g].bitcast(BF16))
+            nc.vector.quantize_mx(out=codes[a, g].bitcast(FP8X4), scales=scales[a, g], in_=slots[a, g].bitcast(BF16))
 
         def matmul(dst, e, a, m, rhs, rhs_scale, start, stop):
             nc.tensor.matmul_mx(
@@ -170,21 +177,22 @@ def tile_moe_shr_lin_none_kernel(tc, xT, w_words, w_scales, gate, offs, pos1, po
             round_pairs(on_gpsimd, 1, u, raw_pass1[u], 0, T)
 
         for s0 in (0, T):
-            gather(0, 0, s0, s0 + T)
-        gather(0, 1, 0, S - ON_SCALAR)
-        share = planes[0][:, 2 * S - ON_SCALAR :].bitcast(BF16).rearrange("p (s d) -> p s d", d=2)
+            gather(planes0[:, s0 : s0 + T], 0, 0, s0, s0 + T)
+        gather(planes0[:, S : 2 * S - ON_SCALAR], 0, 1, 0, S - ON_SCALAR)
+        share = planes0[:, 2 * S - ON_SCALAR :].bitcast(BF16).rearrange("p (s d) -> p s d", d=2)
         for d in range(2):
             window = singles[:, : 2 * T] if d else singles[:, T:]
             nc.scalar.activation(share[:, :, d], window.indirect(offs_t[:, (S - ON_SCALAR) // 16 :]), COPY)
-        weave_tokens(0)
         for g in range(3):
             weave(0, g)
-        for s0 in (0, T):
-            gather(1, 0, s0, s0 + T)
-        gather(1, 1, *span[0])
+        tokens[0] = placed_tile("tokens0", 2 * T, U32, 2048)[:]
+        weave_tokens(nc.gpsimd.tensor_copy, 0, 0, T)
+        gather(planes[1, 0][:, 0, :], 1, 0, *span[0])
+        gather(later[:, 0, :], 1, 0, span[1][0], S)
+        gather(planes[1, 0][:, 1, :], 1, 1, *span[0])
         weave(1, 0)
 
-        codes[0, 0] = tile("codes00", width[0], U32, "pairs0")[:]
+        codes[0, 0] = placed_tile("codes00", width[0], U32, 0)[:]
         quantize(0, 0)
         unread = bank(7)
         for i in range(WARM_UPS):
@@ -193,27 +201,31 @@ def tile_moe_shr_lin_none_kernel(tc, xT, w_words, w_scales, gate, offs, pos1, po
                 lhsT=ww[0][:, 0, : 2 * P].bitcast(FP4X4),
                 lhsT_scale=scales[0, 0][:, :P],
                 rhs=codes[0, 0].bitcast(FP8X4),
-                rhs_scale=scales[0, 0][:],
+                rhs_scale=scales[0, 0],
                 start=True,
                 stop=True,
             )
         first_group = [bank(m)[:] for m in range(2)]
         for m in range(2):
             experts(first_group[m], m, 0, 0)
-        weave_tokens(1)
+        tokens[1] = tile("tokens1", 2 * T, U32, "slots00")[:]
+        weave_tokens(nc.gpsimd.tensor_copy, 1, 0, ON_GPSIMD)
+        weave_tokens(nc.scalar.copy, 1, ON_GPSIMD, T)
         for g in (1, 2):
-            gather(1, 1, *span[g])
+            gather(planes[1, g][:, 1, :], 1, 1, *span[g])
             weave(1, g)
-        held = tile("codes_held", S, U32, "pairs1")
-        codes[1, 0], codes[0, 1], codes[0, 2] = held[:, :512], held[:, 512:1024], held[:, 1024:]
-        for g in (1, 2):
-            codes[1, g] = tile(f"codes1{g}", width[g], U32)[:]
-        for a, g in ((1, 0), (0, 1), (1, 1), (0, 2), (1, 2)):
+        codes[1, 0] = tile("codes10", width[0], U32)[:]
+        codes[0, 1] = tile("codes01", width[1], U32, "planes10")[:]
+        codes[1, 1] = tile("codes11", width[1], U32)[:]
+        for a, g in ((1, 0), (0, 1), (1, 1)):
             quantize(a, g)
-        tok_codes = tile("tok_codes", PASSES * T, U32, "late")
+        nc.vector.quantize_mx(out=last_codes[:].bitcast(FP8X4), scales=last_scales[:], in_=last[:].bitcast(BF16))
+        tok_codes = tile("tok_codes", PASSES * T, U32, "slots11")
         tok_scales = tile("tok_scales", PASSES * T, U8)
-        for lo, hi in ((WIDE, PASSES * T), (0, WIDE)):
-            nc.vector.quantize_mx(out=tok_codes[:, lo:hi].bitcast(FP8X4), scales=tok_scales[:, lo:hi], in_=tokens[:, 2 * lo : 2 * hi].bitcast(BF16))
+        for a in range(PASSES):
+            for lo, hi in ((BANK, T), (0, BANK)):
+                cols = slice(a * T + lo, a * T + hi)
+                nc.vector.quantize_mx(out=tok_codes[:, cols].bitcast(FP8X4), scales=tok_scales[:, cols], in_=tokens[a][:, 2 * lo : 2 * hi].bitcast(BF16))
 
         y = [tile(f"y{m}", S, F32) for m in range(M)]
 
@@ -242,7 +254,7 @@ def tile_moe_shr_lin_none_kernel(tc, xT, w_words, w_scales, gate, offs, pos1, po
 
         def shared_expert(dst, m, lo, hi):
             for a in range(PASSES):
-                cols = slice((1 - a) * T + lo, (1 - a) * T + hi)
+                cols = slice(a * T + lo, a * T + hi)
                 matmul(dst, E, a, m, tok_codes[:, cols], tok_scales[:, cols], a == 0, a == 1)
             return dst
 
@@ -307,7 +319,7 @@ def tile_moe_shr_lin_none_kernel(tc, xT, w_words, w_scales, gate, offs, pos1, po
         store(0, 0, T)
         pick(0, 1, 256, T)
         turned.append(sum_turned(*pieces[3], 5))
-        terms = tile("terms2", 2 * T, F32, "late")
+        terms = tile("terms2", 2 * T, F32, "slots11")
         first[2], second[2] = terms[:, :T], terms[:, T:]
         pick(1, 2, 0, CUT)
         pick(0, 2, 0, CUT)

@@ -28,9 +28,9 @@ FIRST_LOADS = ((0, 512), (512, T))
 ON_VECTOR = 352
 SECOND_LOADS = ((0, 384), (384, T))
 SPARE = 224
-ON_SCALAR = 640
+ON_SCALAR = 512
 LONG_SPARE = 384
-ON_GPSIMD = 320
+ON_GPSIMD = 384
 WARM_UPS = 2
 CUT = 256
 
@@ -185,14 +185,11 @@ def tile_moe_shr_lin_none_kernel(tc, xT, w_words, w_scales, gate, offs, pos1, po
             nc.scalar.activation(share[:, :, d], window.indirect(offs_t[:, (S - ON_SCALAR) // 16 :]), COPY)
         for g in range(3):
             weave(0, g)
-        tokens[0] = placed_tile("tokens0", 2 * T, U32, 2048)[:]
-        weave_tokens(nc.gpsimd.tensor_copy, 0, 0, T)
+        tokens[0] = placed_tile("tokens0", 2 * T, U32, 0)[:]
+        weave_tokens(nc.gpsimd.tensor_copy, 0, 0, ON_GPSIMD)
         gather(planes[1, 0][:, 0, :], 1, 0, *span[0])
         gather(later[:, 0, :], 1, 0, span[1][0], S)
-        gather(planes[1, 0][:, 1, :], 1, 1, *span[0])
-        weave(1, 0)
-
-        codes[0, 0] = placed_tile("codes00", width[0], U32, 0)[:]
+        codes[0, 0] = tile("codes00", width[0], U32, "raw10_0")[:]
         quantize(0, 0)
         unread = bank(7)
         for i in range(WARM_UPS):
@@ -205,13 +202,13 @@ def tile_moe_shr_lin_none_kernel(tc, xT, w_words, w_scales, gate, offs, pos1, po
                 start=True,
                 stop=True,
             )
-        first_group = [bank(m)[:] for m in range(2)]
-        for m in range(2):
+        first_group = [bank(m)[:] for m in range(M)]
+        for m in range(M):
             experts(first_group[m], m, 0, 0)
         tokens[1] = tile("tokens1", 2 * T, U32, "slots00")[:]
-        weave_tokens(nc.gpsimd.tensor_copy, 1, 0, ON_GPSIMD)
-        weave_tokens(nc.scalar.copy, 1, ON_GPSIMD, T)
-        for g in (1, 2):
+        weave_tokens(nc.gpsimd.tensor_copy, 1, 0, T)
+        weave_tokens(nc.scalar.copy, 0, ON_GPSIMD, T)
+        for g in range(3):
             gather(planes[1, g][:, 1, :], 1, 1, *span[g])
             weave(1, g)
         codes[1, 0] = tile("codes10", width[0], U32)[:]
@@ -227,7 +224,7 @@ def tile_moe_shr_lin_none_kernel(tc, xT, w_words, w_scales, gate, offs, pos1, po
                 cols = slice(a * T + lo, a * T + hi)
                 nc.vector.quantize_mx(out=tok_codes[:, cols].bitcast(FP8X4), scales=tok_scales[:, cols], in_=tokens[a][:, 2 * lo : 2 * hi].bitcast(BF16))
 
-        y = [tile(f"y{m}", S, F32) for m in range(M)]
+        y = {m: tile(f"y{m}", S, F32) for m in range(2)}
 
         def empty(m, g, src):
             nc.scalar.copy(out=y[m][:, span[g][0] : span[g][1]], in_=src)
@@ -243,11 +240,11 @@ def tile_moe_shr_lin_none_kernel(tc, xT, w_words, w_scales, gate, offs, pos1, po
         empty(0, 2, both_passes(bank(4)[:, : width[2]], 0, 2))
         experts(first_group[1], 1, 0, 1)
         empty(1, 0, first_group[1])
+        experts(first_group[2], 2, 0, 1)
         empty(1, 1, both_passes(bank(3)[:], 1, 1))
         last_bank = bank(6)
         last_group = {m: both_passes(last_bank[:, (m - 1) * width[2] : m * width[2]], m, 2) for m in (1, 2)}
         empty(1, 2, last_group[1])
-        empty(2, 0, both_passes(bank(4)[:], 2, 0))
 
         shared = work.tile([P, M - 1, BANK], F32, name="shared")
         shared_ends = tile("shared_ends", (M + 1) * P, F32)
@@ -259,7 +256,7 @@ def tile_moe_shr_lin_none_kernel(tc, xT, w_words, w_scales, gate, offs, pos1, po
             return dst
 
         nc.scalar.copy(out=shared[:, 0, :], in_=shared_expert(bank(1)[:], 0, 0, BANK))
-        ends = bank(2)
+        ends = bank(0)
         for m, lo in enumerate((BANK, BANK, 0)):
             shared_expert(ends[:, m * P : (m + 1) * P], m, lo, lo + P)
         nc.scalar.copy(out=shared_ends[:, : M * P], in_=ends[:, : M * P])
@@ -300,35 +297,37 @@ def tile_moe_shr_lin_none_kernel(tc, xT, w_words, w_scales, gate, offs, pos1, po
         def store(m, lo, hi):
             nc.scalar.dma_start(out[m * P : (m + 1) * P, lo:hi], result[:, m * T + lo : m * T + hi])
 
+        y[2] = tile("y2", S, F32, "codes2")
         empty(2, 2, last_group[2])
-        empty(2, 1, both_passes(bank(3)[:], 2, 1))
+        empty(2, 0, first_group[2])
+        empty(2, 1, both_passes(bank(4)[:], 2, 1))
         nc.scalar.copy(out=shared[:, 1, :], in_=shared_expert(bank(1)[:], 1, 0, BANK))
         pieces = ((0, 256), (256, T), (T, T + 256), (T + 256, 2 * T), (2 * T, 2 * T + CUT))
         pick(0, 0, 0, T)
         pick(1, 0, 0, T)
-        turned = [sum_turned(*pieces[0], 0), sum_turned(*pieces[1], 5)]
+        turned = [sum_turned(*pieces[0], 5), sum_turned(*pieces[1], 7)]
         rest = shared_expert(bank(1)[:], 2, P, T)
 
         pick(1, 1, 0, T)
         first[1] = tile("first1", T, F32, "y0")
-        turn_back(*pieces[0], turned[0], 2)
+        turn_back(*pieces[0], turned[0], 0)
         nc.scalar.copy(out=shared_ends[:, M * P :], in_=rest[:, :P])
         pick(0, 1, 0, 256)
-        turned.append(sum_turned(*pieces[2], 0))
-        turn_back(*pieces[1], turned[1], 7)
+        turned.append(sum_turned(*pieces[2], 5))
+        turn_back(*pieces[1], turned[1], 3)
         store(0, 0, T)
         pick(0, 1, 256, T)
-        turned.append(sum_turned(*pieces[3], 5))
+        turned.append(sum_turned(*pieces[3], 7))
         terms = tile("terms2", 2 * T, F32, "slots11")
         first[2], second[2] = terms[:, :T], terms[:, T:]
         pick(1, 2, 0, CUT)
         pick(0, 2, 0, CUT)
         turn_back(*pieces[2], turned[2], 6)
         store(1, 0, 256)
-        turned.append(sum_turned(*pieces[4], 2))
-        turn_back(*pieces[3], turned[3], 4)
+        turned.append(sum_turned(*pieces[4], 0))
+        turn_back(*pieces[3], turned[3], 2)
         store(1, 256, T)
-        turn_back(*pieces[4], turned[4], 7)
+        turn_back(*pieces[4], turned[4], 3)
         store(2, 0, CUT)
 
         partial = tile("partial", T, F32)

@@ -32,7 +32,7 @@ ON_SCALAR = 512
 LONG_SPARE = 384
 ON_GPSIMD = 384
 WARM_UPS = 2
-CUT = 256
+CUT = 128
 
 
 def tile_moe_shr_lin_none_kernel(tc, xT, w_words, w_scales, gate, offs, pos1, pos2, out):
@@ -247,7 +247,7 @@ def tile_moe_shr_lin_none_kernel(tc, xT, w_words, w_scales, gate, offs, pos1, po
         empty(1, 2, last_group[1])
 
         shared = work.tile([P, M - 1, BANK], F32, name="shared")
-        shared_ends = tile("shared_ends", (M + 1) * P, F32)
+        shared_ends = tile("shared_ends", M * P, F32)
 
         def shared_expert(dst, m, lo, hi):
             for a in range(PASSES):
@@ -311,7 +311,6 @@ def tile_moe_shr_lin_none_kernel(tc, xT, w_words, w_scales, gate, offs, pos1, po
         pick(1, 1, 0, T)
         first[1] = tile("first1", T, F32, "y0")
         turn_back(*pieces[0], turned[0], 0)
-        nc.scalar.copy(out=shared_ends[:, M * P :], in_=rest[:, :P])
         pick(0, 1, 0, 256)
         turned.append(sum_turned(*pieces[2], 5))
         turn_back(*pieces[1], turned[1], 3)

@@ -28,9 +28,10 @@ FIRST_LOADS = ((0, 512), (512, T))
 ON_VECTOR = 352
 SECOND_LOADS = ((0, 384), (384, T))
 SPARE = 224
-ON_SCALAR = 512
+ON_SCALAR = 640
 LONG_SPARE = 384
-ON_GPSIMD = 384
+WIDE = 1024
+ON_GPSIMD = 320
 WARM_UPS = 2
 CUT = 128
 
@@ -40,7 +41,6 @@ def tile_moe_shr_lin_none_kernel(tc, xT, w_words, w_scales, gate, offs, pos1, po
     with ExitStack() as ctx:
         keep = ctx.enter_context(tc.tile_pool(name="keep", bufs=1))
         work = ctx.enter_context(tc.tile_pool(name="work", bufs=1))
-        placed = ctx.enter_context(tc.tile_pool(name="placed", bufs=1))
         psum = ctx.enter_context(tc.psum_pool(name="psum", bufs=1))
 
         def tile(name, width, dtype, tag=None):
@@ -50,11 +50,9 @@ def tile_moe_shr_lin_none_kernel(tc, xT, w_words, w_scales, gate, offs, pos1, po
         pos1_t = keep.tile([P, T // 16], U16, name="pos1_t")
         pos2_t = keep.tile([P, T // 16], U16, name="pos2_t")
 
-        def placed_tile(name, width, dtype, offset):
-            return placed.tile([P, width], dtype, name=name, offset=offset, align_bytes=64)
-
         planes0 = tile("planes0", 2 * S, U32)[:]
-        raw_last = placed_tile("raw_last", 2 * T, F32, 0)[:]
+        tokens = tile("tokens", 4 * T, U32)
+        raw_last = tokens[:, : 2 * T].bitcast(F32)
 
         x_view = xT.rearrange("(a p j) t -> a p j t", a=PASSES, p=P, j=4)
 
@@ -119,7 +117,8 @@ def tile_moe_shr_lin_none_kernel(tc, xT, w_words, w_scales, gate, offs, pos1, po
         span = [(e0 * C, e1 * C) for e0, e1 in GROUPS]
         width = [s1 - s0 for s0, s1 in span]
         last = tile("slots2", 4 * width[2], U32)
-        slots = {(a, g): tile(f"slots{a}{g}", 2 * width[g], U32)[:] for a in range(PASSES) for g in range(2)}
+        slots = {(a, g): tile(f"slots{a}{g}", 2 * width[g], U32)[:] for a, g in ((0, 1), (1, 0), (1, 1))}
+        slots[0, 0] = tokens[:, 2 * T : 2 * T + 2 * width[0]]
         scales = {(a, g): tile(f"scales{a}{g}", width[g], U8)[:] for a in range(PASSES) for g in range(2)}
         last_scales = tile("scales2", 2 * width[2], U8)
         last_codes = tile("codes2", 2 * width[2], U32)
@@ -132,14 +131,13 @@ def tile_moe_shr_lin_none_kernel(tc, xT, w_words, w_scales, gate, offs, pos1, po
         planes[1, 0] = tile("planes10", 2 * width[0], U32)[:].rearrange("p (u s) -> p u s", u=2)
         later = tile("planes1", 2 * (S - width[0]), U32)[:].rearrange("p (u s) -> p u s", u=2)
         planes[1, 1], planes[1, 2] = later[:, :, : width[1]], later[:, :, width[1] :]
-        tokens = {}
 
         def weave(a, g):
             nc.scalar.copy(out=slots[a, g].rearrange("p (s u) -> p s u", u=2), in_=planes[a, g].rearrange("p u s -> p s u"))
 
         def weave_tokens(copy, a, t0, t1):
             src = pairs[a][:, : 2 * T].rearrange("p (u t) -> p t u", u=2)
-            dst = tokens[a].rearrange("p (t u) -> p t u", u=2)
+            dst = tokens[:, 2 * a * T : 2 * (a + 1) * T].rearrange("p (t u) -> p t u", u=2)
             copy(out=dst[:, t0:t1, :], in_=src[:, t0:t1, ::-1])
 
         def quantize(a, g):
@@ -185,7 +183,6 @@ def tile_moe_shr_lin_none_kernel(tc, xT, w_words, w_scales, gate, offs, pos1, po
             nc.scalar.activation(share[:, :, d], window.indirect(offs_t[:, (S - ON_SCALAR) // 16 :]), COPY)
         for g in range(3):
             weave(0, g)
-        tokens[0] = placed_tile("tokens0", 2 * T, U32, 0)[:]
         weave_tokens(nc.gpsimd.tensor_copy, 0, 0, ON_GPSIMD)
         gather(planes[1, 0][:, 0, :], 1, 0, *span[0])
         gather(later[:, 0, :], 1, 0, span[1][0], S)
@@ -205,7 +202,6 @@ def tile_moe_shr_lin_none_kernel(tc, xT, w_words, w_scales, gate, offs, pos1, po
         first_group = [bank(m)[:] for m in range(M)]
         for m in range(M):
             experts(first_group[m], m, 0, 0)
-        tokens[1] = tile("tokens1", 2 * T, U32, "slots00")[:]
         weave_tokens(nc.gpsimd.tensor_copy, 1, 0, T)
         weave_tokens(nc.scalar.copy, 0, ON_GPSIMD, T)
         for g in range(3):
@@ -219,10 +215,8 @@ def tile_moe_shr_lin_none_kernel(tc, xT, w_words, w_scales, gate, offs, pos1, po
         nc.vector.quantize_mx(out=last_codes[:].bitcast(FP8X4), scales=last_scales[:], in_=last[:].bitcast(BF16))
         tok_codes = tile("tok_codes", PASSES * T, U32, "slots11")
         tok_scales = tile("tok_scales", PASSES * T, U8)
-        for a in range(PASSES):
-            for lo, hi in ((BANK, T), (0, BANK)):
-                cols = slice(a * T + lo, a * T + hi)
-                nc.vector.quantize_mx(out=tok_codes[:, cols].bitcast(FP8X4), scales=tok_scales[:, cols], in_=tokens[a][:, 2 * lo : 2 * hi].bitcast(BF16))
+        for lo, hi in ((WIDE, PASSES * T), (0, WIDE)):
+            nc.vector.quantize_mx(out=tok_codes[:, lo:hi].bitcast(FP8X4), scales=tok_scales[:, lo:hi], in_=tokens[:, 2 * lo : 2 * hi].bitcast(BF16))
 
         y = {m: tile(f"y{m}", S, F32) for m in range(2)}
 

@@ -70,25 +70,32 @@ def tile_moe_shr_lin_none_kernel(tc, xT, w_words, w_scales, gate, offs, pos1, po
         w_view = w_words.rearrange("e a p b -> p (e a) b").bitcast(I32)
         ww = {}
 
-        def load_w(e0, e1):
-            words = work.tile([P, (e1 - e0) * PASSES, 2 * N], U8, name=f"ww{e0}", align_bytes=64)
-            nc.sync.dma_start(words[:].bitcast(I32), w_view[:, PASSES * e0 : PASSES * e1, :])
+        def load_w(e0, e1, m0=0, m1=M):
+            words = work.tile([P, (e1 - e0) * PASSES, 2 * P * (m1 - m0)], U8, name=f"ww{e0}_{m0}", align_bytes=64)
+            nc.sync.dma_start(words[:].bitcast(I32), w_view[:, PASSES * e0 : PASSES * e1, m0 * P // 2 : m1 * P // 2])
             for e in range(e0, e1):
-                ww[e] = words[:, PASSES * (e - e0) : PASSES * (e - e0 + 1), :]
+                for m in range(m0, m1):
+                    ww[e, m] = words[:, PASSES * (e - e0) : PASSES * (e - e0 + 1), 2 * P * (m - m0) : 2 * P * (m - m0 + 1)]
+
+        s_view = w_scales.rearrange("e a q n -> q (e a) n").bitcast(I32)
+        ws = {}
+
+        def load_scales(e0, e1, memset):
+            plane = work.tile([P, (e1 - e0) * PASSES, N], U8, name=f"ws{e0}", align_bytes=64)
+            memset(plane[:].rearrange("p e n -> p (e n)").bitcast(I32), 0)
+            for r in range(4):
+                nc.sync.dma_start(plane[r:P:32].bitcast(I32), s_view[r:16:4, PASSES * e0 : PASSES * e1, :])
+            for e in range(e0, e1):
+                ws[e] = plane[:, PASSES * (e - e0) : PASSES * (e - e0 + 1), :]
 
         gates = [tile(f"gate{c}", T, F32) for c in range(2)]
         load_w(*GROUPS[0])
-        ws = work.tile([P, (E + 1) * PASSES, N], U8, name="ws", align_bytes=64)
-        ws_words = ws[:].rearrange("p e n -> p (e n)").bitcast(I32)
-        nc.vector.memset(ws_words[:, : (E + 1) * N // 3], 0)
-        nc.gpsimd.memset(ws_words[:, (E + 1) * N // 3 :], 0)
-        s_view = w_scales.rearrange("e a q n -> q (e a) n").bitcast(I32)
-        for r in range(4):
-            nc.sync.dma_start(ws[r:P:32].bitcast(I32), s_view[r:16:4])
+        load_scales(*GROUPS[0], nc.vector.memset)
+        load_w(GROUPS[1][0], E, 0, 1)
+        load_scales(GROUPS[1][0], E + 1, nc.gpsimd.memset)
         nc.sync.dma_start(pos1_t[:], pos1)
         nc.sync.dma_start(pos2_t[:], pos2)
-        load_w(*GROUPS[1])
-        load_w(*GROUPS[2])
+        load_w(GROUPS[1][0], E, 1, M)
         nc.sync.dma_start(gates[0][:], gate[0, :P, :])
         load_w(E, E + 1)
         nc.sync.dma_start(gates[1][:], gate[1, :P, :])
@@ -146,8 +153,8 @@ def tile_moe_shr_lin_none_kernel(tc, xT, w_words, w_scales, gate, offs, pos1, po
         def matmul(dst, e, a, m, rhs, rhs_scale, start, stop):
             nc.tensor.matmul_mx(
                 out=dst,
-                lhsT=ww[e][:, a, 2 * m * P : 2 * (m + 1) * P].bitcast(FP4X4),
-                lhsT_scale=ws[:, PASSES * e + a, m * P : (m + 1) * P],
+                lhsT=ww[e, m][:, a, :].bitcast(FP4X4),
+                lhsT_scale=ws[e][:, a, m * P : (m + 1) * P],
                 rhs=rhs.bitcast(FP8X4),
                 rhs_scale=rhs_scale,
                 start=start,
@@ -192,7 +199,7 @@ def tile_moe_shr_lin_none_kernel(tc, xT, w_words, w_scales, gate, offs, pos1, po
         for i in range(WARM_UPS):
             nc.tensor.matmul_mx(
                 out=unread[:],
-                lhsT=ww[0][:, 0, : 2 * P].bitcast(FP4X4),
+                lhsT=ww[0, 0][:, 0, :].bitcast(FP4X4),
                 lhsT_scale=scales[0, 0][:, :P],
                 rhs=codes[0, 0].bitcast(FP8X4),
                 rhs_scale=scales[0, 0],
@@ -235,10 +242,10 @@ def tile_moe_shr_lin_none_kernel(tc, xT, w_words, w_scales, gate, offs, pos1, po
         experts(first_group[1], 1, 0, 1)
         empty(1, 0, first_group[1])
         experts(first_group[2], 2, 0, 1)
-        empty(1, 1, both_passes(bank(3)[:], 1, 1))
         last_bank = bank(6)
         last_group = {m: both_passes(last_bank[:, (m - 1) * width[2] : m * width[2]], m, 2) for m in (1, 2)}
         empty(1, 2, last_group[1])
+        empty(1, 1, both_passes(bank(3)[:], 1, 1))
 
         shared = work.tile([P, M - 1, BANK], F32, name="shared")
         shared_ends = tile("shared_ends", M * P, F32)

from contextlib import ExitStack

import concourse.mybir as mybir
from concourse.masks import make_identity

K, T, E, C, N = 1024, 640, 10, 128, 384
S = E * C
FLOPS = 2 * K * N * (S + T)

F32 = mybir.dt.float32
BF16 = mybir.dt.bfloat16
U32 = mybir.dt.uint32
I32 = mybir.dt.int32
U16 = mybir.dt.uint16
U8 = mybir.dt.uint8
FP8X4 = mybir.dt.float8_e4m3fn_x4
FP4X4 = mybir.dt.float4_e2m1fn_x4
MULT = mybir.AluOpType.mult
ADD = mybir.AluOpType.add
COPY = mybir.ActivationFunctionType.Copy

P = 128
PASSES = K // 512
M = N // P
BANK = 512
GROUPS = ((0, 4), (4, 8), (8, 10))
FIRST_LOADS = ((0, 512), (512, T))
ON_VECTOR = 352
SECOND_LOADS = ((0, 384), (384, T))
SPARE = 224
ON_SCALAR = 640
LONG_SPARE = 384
WIDE = 1024
ON_GPSIMD = 320
WARM_UPS = 2
CUT = 128


def tile_moe_shr_lin_none_kernel(tc, xT, w_words, w_scales, gate, offs, pos1, pos2, out):
    nc = tc.nc
    with ExitStack() as ctx:
        keep = ctx.enter_context(tc.tile_pool(name="keep", bufs=1))
        work = ctx.enter_context(tc.tile_pool(name="work", bufs=1))
        psum = ctx.enter_context(tc.psum_pool(name="psum", bufs=1))

        def tile(name, width, dtype, tag=None):
            return work.tile([P, width], dtype, name=name, tag=tag or name, align_bytes=64)

        offs_t = keep.tile([P, S // 16], U16, name="offs_t")
        pos1_t = keep.tile([P, T // 16], U16, name="pos1_t")
        pos2_t = keep.tile([P, T // 16], U16, name="pos2_t")

        planes0 = tile("planes0", 2 * S, U32)[:]
        tokens = tile("tokens", 4 * T, U32)
        raw_last = tokens[:, : 2 * T].bitcast(F32)

        x_view = xT.rearrange("(a p j) t -> a p j t", a=PASSES, p=P, j=4)

        def load_x(a, u, t0, t1, dst=None):
            dst = tile(f"raw{a}{u}_{t0}", 2 * (t1 - t0), F32)[:] if dst is None else dst
            rows = dst.rearrange("p (d t) -> p d t", d=2)
            nc.sync.dma_start(rows, x_view[a][:, 2 * u : 2 * u + 2, t0:t1])
            return rows

        raw_first = [load_x(0, 0, t0, t1) for t0, t1 in FIRST_LOADS]
        nc.sync.dma_start(offs_t[:], offs)
        raw_second = [load_x(0, 1, t0, t1) for t0, t1 in SECOND_LOADS]
        raw_pass1 = [load_x(1, 0, 0, T), load_x(1, 1, 0, T, raw_last)]

        w_view = w_words.rearrange("e a p b -> p (e a) b").bitcast(I32)
        ww = {}

        def load_w(e0, e1, m0=0, m1=M):
            words = work.tile([P, (e1 - e0) * PASSES, 2 * P * (m1 - m0)], U8, name=f"ww{e0}_{m0}", align_bytes=64)
            nc.sync.dma_start(words[:].bitcast(I32), w_view[:, PASSES * e0 : PASSES * e1, m0 * P // 2 : m1 * P // 2])
            for e in range(e0, e1):
                for m in range(m0, m1):
                    ww[e, m] = words[:, PASSES * (e - e0) : PASSES * (e - e0 + 1), 2 * P * (m - m0) : 2 * P * (m - m0 + 1)]

        s_view = w_scales.rearrange("e a q n -> q (e a) n").bitcast(I32)
        ws = {}

        def load_scales(e0, e1, memset):
            plane = work.tile([P, (e1 - e0) * PASSES, N], U8, name=f"ws{e0}", align_bytes=64)
            memset(plane[:].rearrange("p e n -> p (e n)").bitcast(I32), 0)
            for r in range(4):
                nc.sync.dma_start(plane[r:P:32].bitcast(I32), s_view[r:16:4, PASSES * e0 : PASSES * e1, :])
            for e in range(e0, e1):
                ws[e] = plane[:, PASSES * (e - e0) : PASSES * (e - e0 + 1), :]

        gates = [tile(f"gate{c}", T, F32) for c in range(2)]
        load_w(*GROUPS[0])
        load_scales(*GROUPS[0], nc.vector.memset)
        load_w(GROUPS[1][0], E, 0, 1)
        load_scales(GROUPS[1][0], E + 1, nc.gpsimd.memset)
        nc.sync.dma_start(pos1_t[:], pos1)
        nc.sync.dma_start(pos2_t[:], pos2)
        load_w(GROUPS[1][0], E, 1, M)
        nc.sync.dma_start(gates[0][:], gate[0, :P, :])
        load_w(E, E + 1)
        nc.sync.dma_start(gates[1][:], gate[1, :P, :])

        ident = tile("ident", P, F32)
        make_identity(nc, ident[:])

        pairs = [tile(f"pairs{a}", 2 * T + spare, U32) for a, spare in enumerate((SPARE, LONG_SPARE))]
        singles = tile("singles", 2 * T + SPARE, BF16)
        for a in range(PASSES):
            nc.vector.memset(pairs[a][:, 2 * T :], 0)
        nc.vector.memset(singles[:, 2 * T :].bitcast(U32), 0)

        def on_gpsimd(out, in_):
            nc.gpsimd.tensor_scalar(out, in_, 1.0, 0.0, MULT, ADD)

        def round_pairs(copy, a, u, rows, t0, t1):
            base = (1 - u) * T
            dst = pairs[a][:, base + t0 : base + t1].bitcast(BF16).rearrange("p (t d) -> p t d", d=2)
            copy(out=dst, in_=rows.rearrange("p d t -> p t d"))

        def gather(dst, a, u, s0, s1):
            window = pairs[a][:, : 2 * T] if u else pairs[a][:, T:]
            nc.vector.tensor_copy(dst, window.indirect(offs_t[:, s0 // 16 : s1 // 16]))

        span = [(e0 * C, e1 * C) for e0, e1 in GROUPS]
        width = [s1 - s0 for s0, s1 in span]
        last = tile("slots2", 4 * width[2], U32)
        slots = {(a, g): tile(f"slots{a}{g}", 2 * width[g], U32)[:] for a, g in ((0, 1), (1, 0), (1, 1))}
        slots[0, 0] = tokens[:, 2 * T : 2 * T + 2 * width[0]]
        scales = {(a, g): tile(f"scales{a}{g}", width[g], U8)[:] for a in range(PASSES) for g in range(2)}
        last_scales = tile("scales2", 2 * width[2], U8)
        last_codes = tile("codes2", 2 * width[2], U32)
        codes = {}
        for a in range(PASSES):
            slots[a, 2] = last[:, 2 * a * width[2] : 2 * (a + 1) * width[2]]
            scales[a, 2] = last_scales[:, a * width[2] : (a + 1) * width[2]]
            codes[a, 2] = last_codes[:, a * width[2] : (a + 1) * width[2]]
        planes = {(0, g): planes0.rearrange("p (u s) -> p u s", u=2)[:, :, span[g][0] : span[g][1]] for g in range(3)}
        planes[1, 0] = tile("planes10", 2 * width[0], U32)[:].rearrange("p (u s) -> p u s", u=2)
        later = tile("planes1", 2 * (S - width[0]), U32)[:].rearrange("p (u s) -> p u s", u=2)
        planes[1, 1], planes[1, 2] = later[:, :, : width[1]], later[:, :, width[1] :]

        def weave(a, g):
            nc.scalar.copy(out=slots[a, g].rearrange("p (s u) -> p s u", u=2), in_=planes[a, g].rearrange("p u s -> p s u"))

        def weave_tokens(copy, a, t0, t1):
            src = pairs[a][:, : 2 * T].rearrange("p (u t) -> p t u", u=2)
            dst = tokens[:, 2 * a * T : 2 * (a + 1) * T].rearrange("p (t u) -> p t u", u=2)
            copy(out=dst[:, t0:t1, :], in_=src[:, t0:t1, ::-1])

        def quantize(a, g):
            nc.vector.quantize_mx(out=codes[a, g].bitcast(FP8X4), scales=scales[a, g], in_=slots[a, g].bitcast(BF16))

        def matmul(dst, e, a, m, rhs, rhs_scale, start, stop):
            nc.tensor.matmul_mx(
                out=dst,
                lhsT=ww[e, m][:, a, :].bitcast(FP4X4),
                lhsT_scale=ws[e][:, a, m * P : (m + 1) * P],
                rhs=rhs.bitcast(FP8X4),
                rhs_scale=rhs_scale,
                start=start,
                stop=stop,
            )

        def bank(i):
            return psum.tile([P, BANK], F32, name=f"bank{i}")

        def experts(dst, m, g, a):
            e0, e1 = GROUPS[g]
            for e in range(e0, e1):
                cols = slice((e - e0) * C, (e - e0 + 1) * C)
                matmul(dst[:, cols], e, a, m, codes[a, g][:, cols], scales[a, g][:, cols], (a, e) == (0, e0), (a, e) == (1, e1 - 1))

        (t0, t1), (t2, t3) = FIRST_LOADS
        round_pairs(nc.vector.tensor_copy, 0, 0, raw_first[0][:, :, :ON_VECTOR], t0, ON_VECTOR)
        round_pairs(nc.scalar.copy, 0, 0, raw_first[0][:, :, ON_VECTOR:], ON_VECTOR, t1)
        round_pairs(nc.vector.tensor_copy, 0, 0, raw_first[1], t2, t3)
        single_view = singles[:, : 2 * T].rearrange("p (d t) -> p d t", d=2)
        for (t0, t1), rows in zip(SECOND_LOADS, raw_second):
            round_pairs(on_gpsimd, 0, 1, rows, t0, t1)
            nc.scalar.copy(out=single_view[:, :, t0:t1], in_=rows[:, ::-1, :])
        for u in range(2):
            round_pairs(on_gpsimd, 1, u, raw_pass1[u], 0, T)

        for s0 in (0, T):
            gather(planes0[:, s0 : s0 + T], 0, 0, s0, s0 + T)
        gather(planes0[:, S : 2 * S - ON_SCALAR], 0, 1, 0, S - ON_SCALAR)
        share = planes0[:, 2 * S - ON_SCALAR :].bitcast(BF16).rearrange("p (s d) -> p s d", d=2)
        for d in range(2):
            window = singles[:, : 2 * T] if d else singles[:, T:]
            nc.scalar.activation(share[:, :, d], window.indirect(offs_t[:, (S - ON_SCALAR) // 16 :]), COPY)
        for g in range(3):
            weave(0, g)
        weave_tokens(nc.gpsimd.tensor_copy, 0, 0, ON_GPSIMD)
        gather(planes[1, 0][:, 0, :], 1, 0, *span[0])
        gather(later[:, 0, :], 1, 0, span[1][0], S)
        codes[0, 0] = tile("codes00", width[0], U32, "raw10_0")[:]
        quantize(0, 0)
        unread = bank(7)
        for i in range(WARM_UPS):
            nc.tensor.matmul_mx(
                out=unread[:],
                lhsT=ww[0, 0][:, 0, :].bitcast(FP4X4),
                lhsT_scale=scales[0, 0][:, :P],
                rhs=codes[0, 0].bitcast(FP8X4),
                rhs_scale=scales[0, 0],
                start=True,
                stop=True,
            )
        first_group = [bank(m)[:] for m in range(M)]
        for m in range(M):
            experts(first_group[m], m, 0, 0)
        weave_tokens(nc.gpsimd.tensor_copy, 1, 0, T)
        weave_tokens(nc.scalar.copy, 0, ON_GPSIMD, T)
        for g in range(3):
            gather(planes[1, g][:, 1, :], 1, 1, *span[g])
            weave(1, g)
        codes[1, 0] = tile("codes10", width[0], U32)[:]
        codes[0, 1] = tile("codes01", width[1], U32, "planes10")[:]
        codes[1, 1] = tile("codes11", width[1], U32)[:]
        for a, g in ((1, 0), (0, 1), (1, 1)):
            quantize(a, g)
        nc.vector.quantize_mx(out=last_codes[:].bitcast(FP8X4), scales=last_scales[:], in_=last[:].bitcast(BF16))
        tok_codes = tile("tok_codes", PASSES * T, U32, "slots11")
        tok_scales = tile("tok_scales", PASSES * T, U8)
        for lo, hi in ((WIDE, PASSES * T), (0, WIDE)):
            nc.vector.quantize_mx(out=tok_codes[:, lo:hi].bitcast(FP8X4), scales=tok_scales[:, lo:hi], in_=tokens[:, 2 * lo : 2 * hi].bitcast(BF16))

        y = {m: tile(f"y{m}", S, F32) for m in range(2)}

        def empty(m, g, src):
            nc.scalar.copy(out=y[m][:, span[g][0] : span[g][1]], in_=src)

        def both_passes(dst, m, g):
            for a in range(PASSES):
                experts(dst, m, g, a)
            return dst

        experts(first_group[0], 0, 0, 1)
        empty(0, 0, first_group[0])
        empty(0, 1, both_passes(bank(3)[:], 0, 1))
        empty(0, 2, both_passes(bank(4)[:, : width[2]], 0, 2))
        experts(first_group[1], 1, 0, 1)
        empty(1, 0, first_group[1])
        experts(first_group[2], 2, 0, 1)
        last_bank = bank(6)
        last_group = {m: both_passes(last_bank[:, (m - 1) * width[2] : m * width[2]], m, 2) for m in (1, 2)}
        empty(1, 2, last_group[1])
        empty(1, 1, both_passes(bank(3)[:], 1, 1))

        shared = work.tile([P, M - 1, BANK], F32, name="shared")
        shared_ends = tile("shared_ends", M * P, F32)

        def shared_expert(dst, m, lo, hi):
            for a in range(PASSES):
                cols = slice(a * T + lo, a * T + hi)
                matmul(dst, E, a, m, tok_codes[:, cols], tok_scales[:, cols], a == 0, a == 1)
            return dst

        nc.scalar.copy(out=shared[:, 0, :], in_=shared_expert(bank(1)[:], 0, 0, BANK))
        ends = bank(0)
        for m, lo in enumerate((BANK, BANK, 0)):
            shared_expert(ends[:, m * P : (m + 1) * P], m, lo, lo + P)
        nc.scalar.copy(out=shared_ends[:, : M * P], in_=ends[:, : M * P])

        first = {0: tile("first0", T, F32)}
        second = {m: tile(f"second{m}", T, F32) for m in range(M - 1)}
        result = tile("result", (M - 1) * T + CUT, F32)

        def pick(choice, m, lo, hi):
            dst, pos_t = ((first, pos1_t), (second, pos2_t))[choice]
            window = y[m][:].indirect(pos_t[:, lo // 16 : hi // 16])
            nc.vector.tensor_tensor(dst[m][:, lo:hi], window, gates[choice][:, lo:hi], MULT)

        def shared_of(m, t):
            return shared[:, m, t : t + P] if m < M - 1 and t < BANK else shared_ends[:, m * P + (t if m == M - 1 else 0) :][:, :P]

        def sum_turned(lo, hi, i):
            acc = bank(i)
            tiles = [divmod(j, T) for j in range(lo, hi, P)]
            early, later = (first, second) if lo < T else (second, first)
            steps = [(n, shared_of(m, t)) for n, (m, t) in enumerate(tiles)]
            for term in (early, later):
                steps.extend((n, term[m][:, t : t + P]) for n, (m, t) in enumerate(tiles))
            for s, (n, term) in enumerate(steps):
                nc.tensor.matmul(
                    acc[:, n * P : (n + 1) * P], term, ident[:], start=(s == 0), stop=(s == len(steps) - 1), is_transpose=True
                )
            turned = tile(f"turned{lo}", hi - lo, F32)
            nc.scalar.copy(out=turned[:], in_=acc[:, : hi - lo])
            return turned

        def turn_back(lo, hi, turned, i):
            back = bank(i)
            for t in range(0, hi - lo, P):
                nc.tensor.transpose(back[:, t : t + P], turned[:, t : t + P], ident[:])
            nc.scalar.copy(out=result[:, lo:hi], in_=back[:, : hi - lo])

        def store(m, lo, hi):
            nc.scalar.dma_start(out[m * P : (m + 1) * P, lo:hi], result[:, m * T + lo : m * T + hi])

        y[2] = tile("y2", S, F32, "codes2")
        empty(2, 2, last_group[2])
        empty(2, 0, first_group[2])
        empty(2, 1, both_passes(bank(4)[:], 2, 1))
        nc.scalar.copy(out=shared[:, 1, :], in_=shared_expert(bank(1)[:], 1, 0, BANK))
        pieces = ((0, 256), (256, T), (T, T + 256), (T + 256, 2 * T), (2 * T, 2 * T + CUT))
        pick(0, 0, 0, T)
        pick(1, 0, 0, T)
        turned = [sum_turned(*pieces[0], 5), sum_turned(*pieces[1], 7)]
        rest = shared_expert(bank(1)[:], 2, P, T)

        pick(1, 1, 0, T)
        first[1] = tile("first1", T, F32, "y0")
        turn_back(*pieces[0], turned[0], 0)
        pick(0, 1, 0, 256)
        turned.append(sum_turned(*pieces[2], 5))
        turn_back(*pieces[1], turned[1], 3)
        store(0, 0, T)
        pick(0, 1, 256, T)
        turned.append(sum_turned(*pieces[3], 7))
        terms = tile("terms2", 2 * T, F32, "slots11")
        first[2], second[2] = terms[:, :T], terms[:, T:]
        pick(1, 2, 0, CUT)
        pick(0, 2, 0, CUT)
        turn_back(*pieces[2], turned[2], 6)
        store(1, 0, 256)
        turned.append(sum_turned(*pieces[4], 0))
        turn_back(*pieces[3], turned[3], 2)
        store(1, 256, T)
        turn_back(*pieces[4], turned[4], 3)
        store(2, 0, CUT)

        partial = tile("partial", T, F32)

        def finish(lo, hi):
            res = tile(f"res2_{lo}", hi - lo, F32)
            nc.vector.tensor_tensor(res[:], partial[:, lo:hi], second[2][:, lo:hi], ADD)
            nc.sync.dma_start(out[2 * P :, lo:hi], res[:])

        low, middle, high = (CUT, 384), (384, BANK), (BANK, T)
        pick(0, 2, CUT, T)
        pick(1, 2, *low)
        nc.vector.tensor_tensor(partial[:, CUT:], rest[:, CUT - P :], first[2][:, CUT:], ADD)
        pick(1, 2, *middle)
        finish(*low)
        pick(1, 2, *high)
        finish(*middle)
        finish(*high)
